import numpy as np, ml_dtypes
CORES = [5,29,101,125,133,157,229,253]
N = 8
import mx_ref
BF = ml_dtypes.bfloat16
def pick(q, e):
    c = np.concatenate([q[0].reshape(128, -1, 4), np.zeros((128, 1, 4), np.uint8)], axis=1); s = np.concatenate([q[1], np.ones((16, 1), np.uint8)], axis=1)
    return (np.ascontiguousarray(c[:, e].reshape(128, -1)), np.ascontiguousarray(s[:, e]))
def join(*qs):
    return (np.concatenate([q[0] for q in qs], axis=1), np.concatenate([q[1] for q in qs], axis=1))
def put(q, e, v):
    c, s = q[0].reshape(128, -1, 4).copy(), q[1].copy(); c[:, e] = v[0].reshape(128, -1, 4); s[:, e] = v[1]
    return (c.reshape(128, -1), s)
def pk(c, s):
    return (np.ascontiguousarray(c), mx_ref.live(s))
def emit(q):
    return q[0], q[1]
def decode(q):
    o = []
    for b in range(4):
        e = np.zeros((128, 128, 4), np.float32); e[np.arange(128), np.arange(128), b] = 1
        o.append(mx_ref.matmul(mx_ref.quantize(e.reshape(128, 512).astype(BF)), q))
    return np.stack(o, axis=2).reshape(128, -1)
def cut(t, i, w=512):
    return t[:, w * i:w * i + w]
def f(rng, *shape):
    return mx_ref.flush((rng.standard_normal(shape, dtype=np.float32) * np.exp2(rng.integers(-2, 3, shape[:-1] + (1,)))).astype(BF))
def wide(rng, *shape, cols=0):
    v = rng.standard_normal(shape, dtype=np.float32) * np.exp2(rng.integers(-12, 13, shape)).astype(np.float32)
    if cols: v *= np.repeat(np.exp2(rng.integers(-cols, cols + 1, shape[:-2] + (1, shape[-1] // 4))) * (rng.random(shape[:-2] + (1, shape[-1] // 4)) > 0.0625), 4, axis=-1).astype(np.float32)
    return mx_ref.flush(v.astype(BF))
P, K, O, L = 256, 64, 1, 3
def times(t, v):
    v = t.astype(np.float32) * np.asarray(v, np.float32)
    return np.where(np.abs(v) < 2.0 ** -16, 0, v).astype(np.float32).astype(BF)
def loud(u, e):
    v = u.astype(np.float32) * np.float32(2.0 ** e)
    return np.where(np.abs(v) < 2.0 ** -30, 0, v).astype(np.float32).astype(BF)
def strong(rng, u, n):
    return np.sign(u[0, :, None, :4].astype(np.float32)) * (1 + rng.random((128, n, 4))) * 128
def near(rng, u):
    ku, v = mx_ref.quantize(np.ascontiguousarray(u[0])), np.repeat(strong(rng, u, 1), 12, axis=1).astype(np.float32)
    v[127] = 0
    z = size(ku, mx_ref.quantize(np.ascontiguousarray(v.reshape(128, -1).astype(BF))))
    v[127, 1:, 0] = np.exp2(np.floor(np.log2(z[0])) - 23 + np.arange(11))
    z = size(ku, mx_ref.quantize(np.ascontiguousarray(v.reshape(128, -1).astype(BF))))
    return v[:, [0, int(np.argmax(z > z[0]))]]
def plain(rng):
    k = np.exp2(6 * rng.random(P) - 3) * np.exp2(rng.random((N, P)) - 0.5)
    u = np.zeros((N, 128, 512), BF)
    u[:, :, :4] = f(rng, 128, 4)
    return {"gr": times(f(rng, N, 128, 4 * P), np.repeat(k, 4, axis=1)[:, None]), "u": u, "w": f(rng, N, 128, 512 * O)}
def setup_inputs(rng):
    return plain(rng)
def setup_inputs_apart(rng):
    d, h = plain(rng), K // 2
    d["u"][:, :8] = 0
    d["u"][:, 120:] = 0
    d["u"][:, 127, 0] = 1
    g = d["gr"].astype(np.float32).reshape(N, 128, P, 4) * np.float32(2.0 ** -8)
    x = rng.permutation(P)[:N // 2 * K].reshape(N // 2, 2, h)
    c = near(rng, d["u"])
    for j in range(N // 2):
        rest = rng.permutation(np.setdiff1d(np.arange(P), x[j].reshape(-1)))[:K].reshape(2, h)
        for i in range(2):
            v = c[:, (x[j, i] >= P // 2).astype(int)]
            v[:8] = (1 + rng.random((8, h, 4))) * 128 * rng.choice([-1.0, 1.0], (8, h, 4))
            g[2 * j + i][:, x[j, i]] = v * np.exp2(rng.integers(0, 3, h))[:, None]
            g[2 * j + i][:, rest[i]] = strong(rng, d["u"], h) * 2.0 ** -4
    d["gr"] = times(g.reshape(N, 128, -1), 1)
    return d
def setup_inputs_cancel(rng):
    d, m = plain(rng), K // 8
    g = d["gr"].astype(np.float32).reshape(N, 128, P, 4)
    e = rng.permutation(P)[:3 * L * m].reshape(L, 3, m)
    g[:, :, e.reshape(-1)] = 0
    for b in range(L):
        for r in range(N):
            h = (r >> b) & 1
            g[r][:, e[b, 1 + h]] = strong(rng, d["u"], m)
            if r % (1 << b) == 0:
                g[r][:, e[b, 0]] = -g[r - (1 << b)][:, e[b, 0]] if h else strong(rng, d["u"], m)
    d["gr"] = times(g.reshape(N, 128, -1), 2.0 ** -10)
    d["u"] = loud(d["u"], -26)
    return d
def setup_inputs_few(rng):
    d, m, h = plain(rng), K // 8, N // 2
    d["u"][:, :64] = 0
    g = d["gr"].astype(np.float32).reshape(N, 128, P, 4)
    g[:, 64:] = 0
    g *= (np.arange(P) % 4 != rng.integers(0, 4, (N, 1)))[:, None, :, None]
    low, e = rng.permutation(K // 4)[:m], K + rng.permutation(P - K)[:(h + 3) * m].reshape(h + 3, m)
    c = np.concatenate([low, e[0]])
    for r in range(N):
        own = e[3 + r] if r < h else e[1:3].reshape(-1)
        g[r][:, own] += strong(rng, d["u"], own.size)
        if r % 2: g[r][:, c] = -g[r - 1][:, c]
        else: g[r][:, c] += strong(rng, d["u"], c.size)
    d["gr"] = times(g.reshape(N, 128, -1), 1)
    d["u"] = loud(d["u"], 24)
    return d
def setup_inputs_spread(rng):
    d = plain(rng)
    e = rng.permutation(P)[:K]
    k = np.exp2(rng.integers(-12, -5, (N, P))) * (rng.random((N, P)) > 0.0625)
    k[:, e] = np.exp2(rng.integers(0, 7, (N, K))) * rng.choice([-1.0, 1.0], (N, K))
    g = wide(rng, N, 128, 4 * P).astype(np.float32).reshape(N, 128, P, 4)
    g[:, :, e] = np.abs(g[:, :, e]) * np.sign(d["u"][0, :, None, :4].astype(np.float32))
    d["gr"] = times(g.reshape(N, 128, -1), np.repeat(k, 4, axis=1)[:, None])
    return d
def setup_inputs_ties(rng):
    d = plain(rng)
    x = f(rng, 128, 24).astype(np.float32).reshape(128, 6, 4)
    h = np.stack([rng.permutation(P) % 6 for r in range(N)])
    sign = rng.choice([-1.0, 1.0], (N, 1, P, 1))
    d["gr"] = times((np.moveaxis(x[:, h], 1, 0) * sign).reshape(N, 128, -1), 1)
    return d
def check_inputs(d):
    b = []
    for k, lo, hi in (("gr", -16, 24), ("u", -30, 30), ("w", -30, 30)):
        v = np.abs(d[k].astype(np.float32))
        if not (np.isfinite(v).all() and ((v == 0) | (v >= 2.0 ** lo) & (v <= 2.0 ** hi)).all()): b.append("a value of " + k)
    v = d["u"].astype(np.float32)
    if (v[:, :, 4:] != 0).any(): b.append("u has numbers behind its column 0")
    if (v != v[:1]).any(): b.append("u isn't the same on all ranks")
    return b
def size(ku, q):
    return np.abs(mx_ref.matmul(ku, q)[0])
def best(s):
    return np.sort(np.argsort(-s, kind="stable")[:K])
def merge(ku, a, b):
    i, j = np.intersect1d(a[0], b[0], return_indices=True)[1:]
    q = join(a[1], b[1])
    v = decode(q).reshape(128, 2 * K, 4)
    v[:, i] = v[:, i] + v[:, K + j]
    q = put(q, i, pick(mx_ref.quantize(np.ascontiguousarray(v.reshape(128, -1).astype(BF))), i))
    n = np.concatenate([a[0], b[0]])
    e = np.setdiff1d(np.arange(2 * K), K + j)
    e = e[np.argsort(n[e])]
    e = e[best(size(ku, q)[e])]
    return n[e], pick(q, e)
def reference(gr, u, w):
    ku, S = [mx_ref.quantize(np.ascontiguousarray(u[r])) for r in range(N)], []
    for r in range(N):
        q = mx_ref.quantize(np.ascontiguousarray(gr[r]))
        e = best(size(ku[r], q))
        S.append((e, pick(q, e)))
    for b in range(L):
        new = list(S)
        for r in range(N):
            p = r ^ (1 << b)
            if r < p: new[r] = new[p] = merge(ku[r], S[r], S[p])
        S = new
    oc, osc = np.zeros((N, 128, 4 * K), np.uint8), np.zeros((N, 16, K), np.uint8)
    nb, y = np.zeros((N, 1, K), np.float32), np.zeros((N, 128, O * K), np.float32)
    for r in range(N):
        oc[r], osc[r] = emit(S[r][1])
        nb[r, 0] = S[r][0]
        for o in range(O): y[r, :, o * K:o * K + K] = mx_ref.matmul(mx_ref.quantize(np.ascontiguousarray(cut(w[r], o))), S[r][1])
    return {"oc": oc, "osc": osc, "nb": nb, "y": y}

@@ -1,0 +1,356 @@
+from concourse.mybir import dt, AluOpType as OP, AxisListType, ActivationFunctionType as AF
+
+K = 64
+BIG = 1.0e29
+TINY = 2.0 ** -120
+MAGIC = 1.5 * 2.0 ** 27
+
+F32, B16, I32, U16, U8, MX = "float32", "bfloat16", "int32", "uint16", "uint8", "float8_e4m3fn_x4"
+SCRATCH = {}
+for _d, _names in (
+        (B16, "ut 16|grt 1024|wt 512|ones 520|zer 512|ur 512|zd 520|idt 128|iot 256|hp 512|ld0 128|ldz 128|kr 64|neg1 64|xx0 576|xx 544"
+              "|pt 512|c0 256|c1 256|ht0 1024|m_t1 256|m_t2 256|m_t3 256|m_t4 256|m_nr 128|m_da 272|m_db 256|m_mt 512|m_ld 128|m_ht 512"),
+        (F32, "cst 8|mask4 64|rst4 64|m4 4|phi 4|plo 4|sr0 256|sc0 8|nsc0 8|d0 128|d1 128|rk0 8|nbs 64|ys 64|m_dg 64|m_dga 64|m_na 8"
+              "|m_nb2 8|m_nc 8|m_ncx 8|m_pen 8|m_hm 8|m_cnt 8|m_notm 8|m_eq 128|m_eq2 128|m_g4 64|m_g5 64|m_mb 64|m_rw 128|m_sr 128"
+              "|m_rm 64|m_bc 8|m_sc 8|m_dd 128|m_cc 128|m_rk 8|m_sel 8|m_ps 8"),
+        (I32, "pi 8|bi 8|bj 8"),
+        (U16, "hl 2|lst0 8|lst1 8|lst2 8|lst3 8|bl0 2|bl1 4|bl2 4|bu 4|m_toff 16")):
+    for _n in _names.split("|"):
+        SCRATCH[_n.split()[0]] = ("sbuf", [128, int(_n.split()[1])], _d)
+for _n, _w in (("u", 128), ("e", 512), ("g", 256), ("w", 128), ("n", 128), ("x0", 144), ("x1", 136), ("x2", 136), ("x3", 136), ("p", 128),
+               ("h0", 256), ("h1", 128), ("h2", 128), ("h3", 128)):
+    SCRATCH["q" + _n] = ("sbuf", [128, _w], MX)
+    SCRATCH["s" + _n] = ("sbuf", [128, _w], U8)
+for _b in range(4):
+    SCRATCH["x%d" % _b] = ("sbuf", [128, 320 if _b < 3 else 128], MX)
+    SCRATCH["s%d" % _b] = ("sbuf", [128, 320 if _b < 3 else 128], U8)
+SCRATCH["hc"] = ("sbuf", [128, 64], MX)
+SCRATCH["hs"] = ("sbuf", [128, 64], U8)
+SCRATCH["PE"] = ("psum", [128, 2048], F32)
+for _n in ("PR", "PC", "PL", "PS"):
+    SCRATCH[_n] = ("psum", [128, 512], F32)
+
+SEMAPHORES = (["kv", "ka", "kt", "kg", "sent", "hc", "hs", "hl"] + ["al%d" % b for b in range(3)] + ["ac%d" % b for b in range(3)]
+              + ["ld%d" % i for i in range(4)] + ["st%d" % i for i in range(8)])
+
+
+def make_flow(g, T):
+    eng = {"v": g.vector, "a": g.scalar, "t": g.tensor, "g": g, "s": g.sync}
+    own = {"v": "kv", "a": "ka", "t": "kt", "g": "kg"}
+    total, clock, ev, wr, rd, order = {}, {k: {} for k in eng}, {}, {}, {}, {}
+
+    def need(q, events):
+        for e in sorted(events, key=lambda e: -order.get(e, 0)):
+            sem, val = e
+            if clock[q].get(sem, 0) >= val:
+                continue
+            eng[q].wait_ge(T.sem[sem], val)
+            for s, v in ev.get(e, {}).items():
+                clock[q][s] = max(clock[q].get(s, 0), v)
+            clock[q][sem] = max(clock[q].get(sem, 0), val)
+
+    def deps(mine, reads, writes):
+        out = set()
+        for t in reads:
+            if t not in wr:
+                raise ValueError("nothing wrote " + t)
+            out.add(wr[t])
+        for t in writes:
+            if t in wr and wr[t][0] != mine:
+                out.add(wr[t])
+            for e in rd.get(t, ()):
+                if e[0] != mine:
+                    out.add(e)
+        return out
+
+    def note(q, e, reads, writes):
+        ev[e] = dict(clock[q])
+        ev[e][e[0]] = e[1]
+        order[e] = len(order) + 1
+        for t in reads:
+            rd.setdefault(t, []).append(e)
+        for t in writes:
+            wr[t] = e
+            rd[t] = []
+
+    def op(q, reads, writes, fn):
+        sem = own[q]
+        need(q, deps(sem, reads, writes))
+        total[sem] = total.get(sem, 0) + 1
+        fn(eng[q]).then_inc(T.sem[sem], 1)
+        note(q, (sem, total[sem]), reads, writes)
+
+    def dma(q, reads, writes, sem, out, in_):
+        need(q, deps(None, reads, writes))
+        eng[q].dma_start(out, in_).then_inc(T.sem[sem], 16)
+        total[sem] = total.get(sem, 0) + 16
+        note(q, (sem, total[sem]), reads, writes)
+
+    def arrives(tok, sem, val):
+        ev[(sem, val)] = {sem: val}
+        order[(sem, val)] = len(order) + 1
+        total[sem] = val
+        wr[tok] = (sem, val)
+        rd[tok] = []
+
+    def ready(q, reads):
+        need(q, deps(None, reads, []))
+
+    def finish():
+        need("g", list(total.items()))
+
+    return op, dma, arrives, ready, finish
+
+
+def rank_program(g, core, T, topo):
+    rank = T.rank_of(core)
+    sent = [0]
+
+    def send(out, in_, dst, sem, away=None):
+        e = [x for x in topo.engines(core, dst) if away is None or x in topo.engines(core, away)]
+        rid, pid = topo.addr(dst, core)
+        g.remote_dma(out, in_, T.sem[sem], T.sem.sent, pid, rid, sum(1 << x for x in e))
+        sent[0] += len(e)
+
+    def helpers(r):
+        c0, far = T.cores[r], T.cores[r ^ 1]
+        hs = [c for c in topo.cores_of(c0) if c != c0 and topo.die(c) == topo.die(c0) and topo.may_write(c, far)]
+        return hs[0], hs[-1]
+
+    def bits(v):
+        return v.bitcast(dt.uint8)
+
+    if rank is None:
+        for r in range(len(T.cores)):
+            a, b = helpers(r)
+            if core not in (a, b):
+                continue
+            far = T.cores[r ^ 1]
+            n = len([x for x in topo.engines(T.cores[r], core) if x in topo.engines(T.cores[r], T.cores[r ^ 2])])
+            if core == b:
+                g.wait_ge(T.sem.hl, n)
+                send(T.bl0[:], T.hl[:], far, "al0")
+            if core == a:
+                g.wait_ge(T.sem.hc, n)
+                send(bits(T.x0[:, 128:192]), bits(T.hc[:]), far, "ac0")
+            if core == b:
+                g.wait_ge(T.sem.hs, n)
+                send(T.s0[:, 128:192], T.hs[:], far, "ac0")
+            g.wait_ge(T.sem.sent, sent[0])
+        return
+
+    op, dma, arrives, ready, finish = make_flow(g, T)
+    X = AxisListType.X
+    pf, pm4, q4, isa, isb = [T.cst[:, i:i + 1] for i in range(5)]
+
+    dma("s", [], ["ut"], "ld0", T.ut[:, 0:4], T.u[:, 0:4])
+    dma("a", [], ["gr1"], "ld2", T.grt[:, 512:1024], T.gr[:, 512:1024])
+    dma("s", [], ["gr0"], "ld1", T.grt[:, 0:512], T.gr[:, 0:512])
+    dma("s", [], ["wt"], "ld3", T.wt[:], T.w[:])
+
+    op("v", [], ["ones"], lambda e: e.memset(T.ones[:], 1.0))
+    op("g", [], ["pi"], lambda e: e.iota(T.pi[:, 0:1], [[0, 1]], 0, 1))
+    op("v", [], ["zer"], lambda e: e.memset(T.zer[:], 0.0))
+    op("v", [], ["xx0"], lambda e: e.memset(T.xx0[:], 0.0))
+    op("v", [], ["m4"], lambda e: e.memset(T.m4[:], MAGIC))
+    op("v", [], ["ldz"], lambda e: e.memset(T.ldz[:], -TINY))
+    op("g", ["ldz"], ["ld0"], lambda e: e.affine_select(T.ld0[:], T.ldz[:], [[-1, 128]], OP.is_gt, 0.0, 0, 1))
+    op("g", [], ["hp"], lambda e: e.iota(T.hp[:], [[0, 8], [1, 16], [16, 4]], 0, 0, allow_small_or_imprecise_dtypes=True))
+    op("v", ["pi"], ["pf"], lambda e: e.tensor_copy(pf, T.pi[:, 0:1]))
+    for t in range(4):
+        op("v", ["ones", "ut"], ["ur"], lambda e: e.tensor_scalar(T.ur[:, t:512:4], T.ones[:, 0:128], T.ut[:, t:t + 1], None, OP.mult))
+    op("v", ["ur"], ["qu"], lambda e: e.quantize_mx(T.qu[:], T.su[:], T.ur[:]))
+    op("v", ["m4", "pf"], ["phi"], lambda e: e.tensor_scalar(T.phi[:], T.m4[:], pf, MAGIC, OP.add, OP.subtract))
+    op("v", ["phi", "pf"], ["plo"], lambda e: e.tensor_scalar(T.plo[:], T.phi[:], pf, -1.0, OP.subtract, OP.mult))
+    for i, src, add in ((0, "phi", 0.0), (32, "phi", 128.0), (64, "plo", 0.0)):
+        op("v", [src, "xx0"], ["xx0"], lambda e: e.tensor_scalar(T.xx0[:, i:i + 16:5], T[src][:], add, None, OP.add))
+        op("v", [src, "xx0"], ["xx0"], lambda e: e.tensor_scalar(T.xx0[:, i + 16:i + 22:5], T[src][:, 0:2], add, None, OP.add))
+        op("v", [src, "xx0"], ["xx0"], lambda e: e.tensor_scalar(T.xx0[:, i + 18:i + 24:5], T[src][:, 0:2], add, 256.0, OP.add, OP.mult))
+    op("v", ["xx0"], ["qx0"], lambda e: e.quantize_mx(T.qx0[:], T.sx0[:], T.xx0[:]))
+    op("v", ["zer"], ["x0p", "x0o"], lambda e: e.quantize_mx(T.x0[:, 0:128], T.s0[:, 0:128], T.zer[:]))
+
+    H = [slice(0, 128), slice(128, 256)]
+    for h in range(2):
+        op("v", ["gr%d" % h], ["qg"], lambda e: e.quantize_mx(T.qg[:, H[h]], T.sg[:, H[h]], T.grt[:, 512 * h:512 * h + 512]))
+    op("t", ["qu", "qg"], ["PR"], lambda e: e.matmul_mx(T.PR[:, 0:256], T.qu[:], T.su[:], T.qg[:], T.sg[:], True, True))
+    for h, P in ((0, "PC"), (1, "PS")):
+        op("t", ["qu", "qg"], [P], lambda e: e.matmul_mx(T[P][:, 0:128], T.qg[:, H[h]], T.sg[:, H[h]], T.qu[:], T.su[:], True, True))
+    op("a", ["PR"], ["sr0"], lambda e: e.activation(T.sr0[:], T.PR[:, 0:256], AF.Abs))
+    for h, P in ((0, "PC"), (1, "PS")):
+        op("v", [P], ["nsc%d" % h], lambda e: e.tensor_reduce(T.nsc0[:, h:h + 1], T[P][:, 0:1], X, OP.max, negate=True, apply_absolute_value=True))
+        op("v", [P], ["sc0%d" % h], lambda e: e.tensor_reduce(T.sc0[:, h:h + 1], T[P][:, 0:1], X, OP.max, apply_absolute_value=True))
+        op("a", ["sr0", "nsc%d" % h], ["d%d" % h], lambda e: e.activation(T["d%d" % h][:], T.sr0[:, H[h]], AF.Identity, bias=T.nsc0[:, h:h + 1]))
+    for h in range(2):
+        op("v", ["sr0", "sc0%d" % h], ["c%da" % h], lambda e: e.tensor_scalar(
+            T["c%d" % h][:, H[1 - h]], T.sr0[:, H[1 - h]], T.sc0[:, h:h + 1], None, OP.is_ge if h else OP.is_gt))
+    for h in range(2):
+        op("v", ["d%d" % h, "ld0"], ["c%db" % h], lambda e: e.tensor_tensor(T["c%d" % h][:, H[h]], T["d%d" % h][:], T.ld0[:], OP.is_gt))
+    for h in range(2):
+        op("v", ["c%da" % h, "c%db" % h], ["rk0%d" % h], lambda e: e.tensor_reduce(T.rk0[:, h:h + 1], T["c%d" % h][:], X, OP.add))
+    for h in range(2):
+        op("v", ["hp", "rk0%d" % h], ["ht0%d" % h], lambda e: e.tensor_scalar(T.ht0[:, 512 * h:512 * h + 512], T.hp[:], T.rk0[:, h:h + 1], None, OP.is_equal))
+    for h in range(2):
+        op("v", ["ht0%d" % h], ["qh0%d" % h], lambda e: e.quantize_mx(T.qh0[:, H[h]], T.sh0[:, H[h]], T.ht0[:, 512 * h:512 * h + 512]))
+    for i, (h, c) in enumerate(((0, 0), (0, 16), (1, 8), (1, 16))):
+        op("t", ["qh0%d" % h, "qx0"], ["PL"], lambda e: e.matmul_mx(T.PL[:, 0:128], T.qh0[:, H[h]], T.sh0[:, H[h]], T.qx0[:, c:c + 128], T.sx0[:, c:c + 128], i == 0, i == 3))
+    op("v", ["PL"], ["lst0"], lambda e: e.tensor_copy(T.lst0[:, 0:6], T.PL[:, 0:6]))
+
+    def pick(src, ssrc, lo, hi, lst, b):
+        toks = ["qg"] if b == 0 else ["x%do" % (b - 1), "s%do" % (b - 1), "x%dl" % (b - 1), "x%dm" % (b - 1)]
+        op("v", toks + [lst], ["x%do" % b], lambda e: e.tensor_copy(
+            T["x%d" % b][:, 64:128].bitcast(dt.uint32), T[src][:, lo:hi].bitcast(dt.uint32).indirect(T[lst][:, 0:4])))
+        op("a", toks + [lst, "x%dp" % b], ["s%do" % b], lambda e: e.activation(
+            T["s%d" % b][:, 64:128], T[ssrc][:, lo:hi].indirect(T[lst][:, 0:4]), AF.Copy))
+
+    ha, hb = helpers(rank)
+    away = T.cores[rank ^ 2]
+    ready("g", ["lst0"])
+    send(T.hl[:], T.lst0[:, 4:6], hb, "hl", away)
+    pick("qg", "sg", 0, 256, "lst0", 0)
+    ready("g", ["x0o"])
+    send(bits(T.hc[:]), bits(T.x0[:, 64:128]), ha, "hc", away)
+    ready("g", ["s0o"])
+    send(T.hs[:], T.s0[:, 64:128], hb, "hs", away)
+
+    op("g", [], ["iot"], lambda e: e.iota(T.iot[:], [[1, 256]], 0, 0, allow_small_or_imprecise_dtypes=True))
+    op("g", ["ones"], ["zd"], lambda e: e.affine_select(T.zd[:, 0:516], T.ones[:, 0:516], [[-1, 516]], OP.is_equal, 0.0, 3, 4))
+    op("g", [], ["kr"], lambda e: e.iota(T.kr[:], [[0, 16], [1, 4]], 0, 0, allow_small_or_imprecise_dtypes=True))
+    op("g", ["ones"], ["idt"], lambda e: e.affine_select(T.idt[:], T.ones[:, 0:128], [[-1, 128]], OP.is_equal, 0.0, 0, 1))
+
+    def own_tables(b, aw, awt):
+        op("v", [], ["t1"], lambda e: e.memset(T.m_t1[:], 64.0))
+        op("v", [], ["t4"], lambda e: e.memset(T.m_t4[:], BIG))
+        op("v", ["t1", "iot", awt], ["t1"], lambda e: e.tensor_copy(T.m_t1[:].indirect(aw), T.iot[:, 0:64]))
+        op("a", ["iot", awt], ["nra"], lambda e: e.activation(T.m_nr[:, 0:64], T.iot[:].indirect(aw), AF.Copy))
+        op("v", ["t1"], ["t2"], lambda e: e.tensor_scalar(T.m_t2[:], T.m_t1[:], 63.5, None, OP.is_lt))
+        op("v", ["t1"], ["t3"], lambda e: e.tensor_scalar(T.m_t3[:], T.m_t1[:], 63.5, BIG, OP.is_gt, OP.mult))
+        op("v", ["nra", "idt"], ["dga"], lambda e: e.tensor_tensor(T.m_dga[:], T.m_nr[:, 0:64], T.idt[:, 0:64], OP.mult))
+        op("v", ["dga"], ["na"], lambda e: e.tensor_reduce(T.m_na[:, 0:1], T.m_dga[:], X, OP.add))
+        for t in range(4):
+            op("t", ["qe", "x%dp" % b, "x%do" % b, "s%do" % b], ["PE%d" % t], lambda e: e.matmul_mx(
+                T.PE[:, 512 * t:512 * t + 128], T.qe[:, 128 * t:128 * t + 128], T.se[:, 128 * t:128 * t + 128], T["x%d" % b][:, 0:128], T["s%d" % b][:, 0:128], True, True))
+            op("a", ["PE%d" % t], ["da"], lambda e: e.activation(T.m_da[:, t:256:4], T.PE[:, 512 * t + 64:512 * t + 128], AF.Copy))
+
+    for t in range(4):
+        op("v", ["zd"], ["qe"], lambda e: e.quantize_mx(T.qe[:, 128 * t:128 * t + 128], T.se[:, 128 * t:128 * t + 128], T.zd[:, 3 - t:515 - t]))
+    op("v", [], ["da"], lambda e: e.memset(T.m_da[:, 256:272], 0.0))
+    own_tables(0, T.lst0[:, 0:4], "lst0")
+    op("v", ["pi"], ["pr3"], lambda e: e.tensor_scalar(T.pi[:, 1:2], T.pi[:, 0:1], 3, None, OP.bitwise_and))
+    op("v", ["pi"], ["pq"], lambda e: e.tensor_scalar(T.pi[:, 2:3], T.pi[:, 0:1], 2, 3, OP.logical_shift_right, OP.bitwise_and))
+    op("v", ["pf"], ["isa"], lambda e: e.tensor_scalar(isa, pf, 63.5, 1000.0, OP.is_lt, OP.mult))
+    op("v", ["pf"], ["isb"], lambda e: e.tensor_scalar(isb, pf, 63.5, 128.0, OP.is_gt, OP.mult))
+    op("v", ["pr3"], ["pm4"], lambda e: e.tensor_copy(pm4, T.pi[:, 1:2]))
+    op("v", ["pq"], ["q4"], lambda e: e.tensor_copy(q4, T.pi[:, 2:3]))
+    op("v", ["kr"], ["rst4"], lambda e: e.tensor_scalar(T.rst4[:], T.kr[:], 0.5, None, OP.is_gt))
+    op("v", ["kr", "q4"], ["mask4"], lambda e: e.tensor_scalar(T.mask4[:], T.kr[:], q4, None, OP.is_equal))
+    op("v", [], ["neg1"], lambda e: e.memset(T.neg1[:], -1.0))
+    op("v", [], ["xx"], lambda e: e.memset(T.xx[:], 0.0))
+    op("v", [], ["mtz"], lambda e: e.memset(T.m_mt[:, 0:256], 0.0))
+    op("v", ["plo", "xx"], ["xx"], lambda e: e.tensor_copy(T.xx[:, 32:48:5], T.plo[:]))
+    for b in range(1, 4):
+        op("v", ["zer"], ["x%dp" % b, "x%do" % b, "s%do" % b], lambda e: e.quantize_mx(T["x%d" % b][:, 0:128], T["s%d" % b][:, 0:128], T.zer[:]))
+
+    def idle_work():
+        op("v", [], ["pt"], lambda e: e.memset(T.pt[:], 0.0))
+        op("v", ["ones"], ["qn"], lambda e: e.quantize_mx(T.qn[:], T.sn[:], T.ones[:, 0:512]))
+        op("v", ["wt"], ["qw"], lambda e: e.quantize_mx(T.qw[:], T.sw[:], T.wt[:]))
+
+    for b in range(3):
+        nx = b + 1
+        x, s = T["x%d" % b], T["s%d" % b]
+        aw, awt = (T.lst0[:, 0:4], "lst0") if b == 0 else (T["lst%d" % b][:, 4:8], "lst%d" % b)
+        src = helpers(rank ^ 1)[0] if b == 0 else T.cores[rank ^ (1 << b)]
+        n = len(topo.engines(src, core))
+        arrives("bl%d" % b, "al%d" % b, n)
+        arrives("x%dl" % b, "ac%d" % b, 2 * n)
+
+        if b == 0:
+            op("v", ["bl0"], ["bi"], lambda e: e.tensor_copy(T.bi[:, 0:2], T.bl0[:]))
+            op("v", ["bi"], ["bj"], lambda e: e.tensor_scalar(T.bj[:, 0:2], T.bi[:, 0:2], 255, None, OP.bitwise_and))
+            op("v", ["bi"], ["bj"], lambda e: e.tensor_scalar(T.bj[:, 2:4], T.bi[:, 0:2], 8, None, OP.logical_shift_right))
+            op("v", ["bj"], ["bu"], lambda e: e.tensor_copy(T.bu[:], T.bj[:, 0:4]))
+        bwt = "bl%d" % b if b else "bu"
+        bw = T[bwt][:]
+        op("v", ["t1", bwt, "mask4"], ["g4"], lambda e: e.tensor_tensor(T.m_g4[:], T.m_t1[:].indirect(bw), T.mask4[:], OP.mult))
+        op("a", ["t2", bwt], ["mb"], lambda e: e.activation(T.m_mb[:], T.m_t2[:].indirect(bw), AF.Copy))
+        op("v", ["g4", "rst4"], ["g5"], lambda e: e.tensor_tensor_scan(T.m_g5[:], T.rst4[:], T.m_g4[:], 0.0, OP.mult, OP.add))
+        op("v", ["iot", bwt, "idt"], ["dg"], lambda e: e.tensor_tensor(T.m_dg[:], T.iot[:].indirect(bw), T.idt[:, 64:128], OP.mult))
+        op("v", ["g5", "pm4"], ["toff"], lambda e: e.tensor_scalar(T.m_toff[:], T.m_g5[:, 3:64:4], 4.0, pm4, OP.mult, OP.add))
+        op("a", ["iot", bwt], ["nrb"], lambda e: e.activation(T.m_nr[:, 64:128], T.iot[:].indirect(bw), AF.Copy))
+        op("v", ["dg"], ["nb2"], lambda e: e.tensor_reduce(T.m_nb2[:, 0:1], T.m_dg[:], X, OP.add))
+        op("v", ["na", "nb2"], ["nc"], lambda e: e.tensor_tensor(T.m_nc[:, 0:1], T.m_na[:, 0:1], T.m_nb2[:, 0:1], OP.add))
+        op("a", ["nra", "nrb", "nc"], ["eq"], lambda e: e.activation(T.m_eq[:], T.m_nr[:], AF.Abs, bias=T.m_nc[:, 0:1], scale=-1.0))
+        op("a", ["eq"], ["cnt", "eq2"], lambda e: e.activation(T.m_eq2[:], T.m_eq[:], AF.Relu, bias=1.0, scale=-1.0, accum_out=T.m_cnt[:, 0:1]))
+        op("a", ["cnt"], ["notm"], lambda e: e.activation(T.m_notm[:, 0:1], T.m_cnt[:, 0:1], AF.Copy, bias=2.0, scale=-1.0))
+        op("v", ["t4", "neg1", bwt], ["t4"], lambda e: e.tensor_copy(T.m_t4[:].indirect(bw), T.neg1[:]))
+        op("v", ["m4", "nc", "xx"], ["xx"], lambda e: e.tensor_scalar(T.xx[:, 16:32:5], T.m4[:], T.m_nc[:, 0:1], MAGIC, OP.add, OP.subtract))
+        op("v", ["xx", "nc"], ["xx"], lambda e: e.tensor_scalar(T.xx[:, 48:64:5], T.xx[:, 16:32:5], T.m_nc[:, 0:1], -1.0, OP.subtract, OP.mult))
+        op("v", ["cnt", "isa"], ["pen"], lambda e: e.tensor_scalar(T.m_pen[:, 0:1], T.m_cnt[:, 0:1], -1.0, isa, OP.add, OP.mult))
+        op("v", ["cnt", "isb"], ["hm"], lambda e: e.tensor_scalar(T.m_hm[:, 0:1], T.m_cnt[:, 0:1], -1.0, isb, OP.add, OP.mult))
+        op("v", ["pen", "nc"], ["ncx"], lambda e: e.tensor_tensor(T.m_ncx[:, 0:1], T.m_pen[:, 0:1], T.m_nc[:, 0:1], OP.add))
+        op("v", ["phi", "hm"], ["xx"], lambda e: e.tensor_scalar(T.xx[:, 0:16:5], T.phi[:], T.m_hm[:, 0:1], None, OP.add))
+        op("v", ["nra", "nrb", "ncx"], ["ld"], lambda e: e.tensor_scalar(T.m_ld[:], T.m_nr[:], T.m_ncx[:, 0:1], -TINY, OP.is_lt, OP.mult))
+        op("v", ["xx"], ["qx"], lambda e: e.quantize_mx(T["qx%d" % nx][:], T["sx%d" % nx][:], T.xx[:]))
+
+        both = ["x%do" % b, "s%do" % b, "x%dl" % b]
+        for t in range(4):
+            op("t", ["qe"] + both, ["PE%d" % t], lambda e: e.matmul_mx(
+                T.PE[:, 512 * t:512 * t + 128], T.qe[:, 128 * t:128 * t + 128], T.se[:, 128 * t:128 * t + 128], x[:, 64:192], s[:, 64:192], True, True))
+        op("t", ["qu"] + both, ["PR"], lambda e: e.matmul_mx(T.PR[:, 0:128], T.qu[:], T.su[:], x[:, 64:192], s[:, 64:192], True, True))
+        op("t", ["qu"] + both, ["PC"], lambda e: e.matmul_mx(T.PC[:, 0:128], x[:, 64:192], s[:, 64:192], T.qu[:], T.su[:], True, True))
+        for t in range(4):
+            op("v", ["PE%d" % t, "mb"], ["db"], lambda e: e.tensor_tensor(T.m_db[:, t:256:4], T.PE[:, 512 * t + 64:512 * t + 128], T.m_mb[:], OP.mult))
+        op("a", ["PR"], ["rw"], lambda e: e.activation(T.m_rw[:], T.PR[:, 0:128], AF.Abs))
+        op("a", ["PC", "notm"], ["bc"], lambda e: e.activation(T.m_bc[:, 0:1], T.PC[:, 0:1], AF.Abs, scale=T.m_notm[:, 0:1]))
+        op("v", ["da", "toff", "db"], ["mt"], lambda e: e.tensor_tensor(T.m_mt[:, 256:512], T.m_da[:, 0:260].indirect(T.m_toff[:]), T.m_db[:], OP.add))
+        op("v", ["mt", "mtz"], ["x%dm" % b], lambda e: e.quantize_mx(x[:, 192:320], s[:, 192:320], T.m_mt[:]))
+        op("t", ["qu", "x%dm" % b], ["PR"], lambda e: e.matmul_mx(T.PR[:, 0:128], T.qu[:], T.su[:], x[:, 192:320], s[:, 192:320], True, True))
+        op("t", ["qu", "x%dm" % b], ["PC"], lambda e: e.matmul_mx(T.PC[:, 0:128], x[:, 192:320], s[:, 192:320], T.qu[:], T.su[:], True, True))
+        op("v", ["t4", "rw", awt], ["sra"], lambda e: e.tensor_tensor(T.m_sr[:, 0:64], T.m_t4[:].indirect(aw), T.m_rw[:, 0:64], OP.min))
+        op("v", ["t3", "rw", bwt], ["srb"], lambda e: e.tensor_tensor(T.m_sr[:, 64:128], T.m_t3[:].indirect(bw), T.m_rw[:, 64:128], OP.min))
+        op("a", ["PR"], ["rm"], lambda e: e.activation(T.m_rm[:], T.PR[:, 64:128], AF.Abs))
+        op("a", ["PC", "bc"], ["sc"], lambda e: e.activation(T.m_sc[:, 0:1], T.PC[:, 0:1], AF.Abs, bias=T.m_bc[:, 0:1]))
+        op("v", ["srb", "rm"], ["srb"], lambda e: e.tensor_tensor(T.m_sr[:, 64:128], T.m_sr[:, 64:128], T.m_rm[:], OP.add))
+        op("v", ["sra", "srb", "sc"], ["dd"], lambda e: e.tensor_scalar(T.m_dd[:], T.m_sr[:], T.m_sc[:, 0:1], None, OP.subtract))
+        op("v", ["dd", "ld"], ["cc"], lambda e: e.tensor_tensor(T.m_cc[:], T.m_dd[:], T.m_ld[:], OP.is_gt))
+        op("v", ["cc"], ["rk"], lambda e: e.tensor_reduce(T.m_rk[:, 0:1], T.m_cc[:], X, OP.add))
+        key = "rk"
+        if b == 2:
+            op("v", ["rk"], ["sel"], lambda e: e.tensor_scalar(T.m_sel[:, 0:1], T.m_rk[:, 0:1], 63.5, None, OP.is_lt))
+            op("v", ["rk"], ["pen"], lambda e: e.tensor_scalar(T.m_pen[:, 0:1], T.m_rk[:, 0:1], 63.5, 1000.0, OP.is_gt, OP.mult))
+            op("v", ["nra", "nrb", "nc", "sel", "pt"], ["pt"], lambda e: e.tensor_scalar(T.pt[:, 0:512:4], T.m_nr[:], T.m_nc[:, 0:1], T.m_sel[:, 0:1], OP.is_gt, OP.mult))
+            op("v", ["pt"], ["qp"], lambda e: e.quantize_mx(T.qp[:], T.sp[:], T.pt[:]))
+            op("t", ["qp", "qn"], ["PC"], lambda e: e.matmul_mx(T.PC[:, 0:128], T.qp[:], T.sp[:], T.qn[:], T.sn[:], True, True))
+            op("v", ["PC", "pen"], ["ps"], lambda e: e.tensor_tensor(T.m_ps[:, 0:1], T.PC[:, 0:1], T.m_pen[:, 0:1], OP.add))
+            key = "ps"
+        op("v", ["hp", key], ["ht"], lambda e: e.tensor_scalar(T.m_ht[:], T.hp[:], T["m_" + key][:, 0:1], None, OP.is_equal))
+        op("v", ["ht"], ["qh"], lambda e: e.quantize_mx(T["qh%d" % nx][:], T["sh%d" % nx][:], T.m_ht[:]))
+        for c in (0, 8):
+            op("t", ["qh", "qx"], ["PL"], lambda e: e.matmul_mx(
+                T.PL[:, 0:128], T["qh%d" % nx][:], T["sh%d" % nx][:], T["qx%d" % nx][:, c:c + 128], T["sx%d" % nx][:, c:c + 128], c == 0, c == 8))
+        lst = "lst%d" % nx
+        op("v", ["PL"], [lst], lambda e: e.tensor_copy(T[lst][:], T.PL[:, 0:8]))
+        if b < 2:
+            to = T.cores[rank ^ (1 << nx)]
+            ready("g", [lst])
+            send(T["bl%d" % nx][:], T[lst][:, 4:8], to, "al%d" % nx)
+            pick("x%d" % b, "s%d" % b, 64, 320, lst, nx)
+            ready("g", ["x%do" % nx])
+            send(bits(T["x%d" % nx][:, 128:192]), bits(T["x%d" % nx][:, 64:128]), to, "ac%d" % nx)
+            ready("g", ["s%do" % nx])
+            send(T["s%d" % nx][:, 128:192], T["s%d" % nx][:, 64:128], to, "ac%d" % nx)
+            own_tables(nx, T[lst][:, 4:8], lst)
+            if b == 0:
+                idle_work()
+
+    pick("x2", "s2", 64, 320, "lst3", 3)
+    dma("s", ["x3o"], [], "st0", T.oc[:], bits(T.x3[:, 64:128]))
+    op("t", ["qw", "x3p", "x3o", "s3o"], ["PS"], lambda e: e.matmul_mx(T.PS[:, 0:128], T.qw[:], T.sw[:], T.x3[:], T.s3[:], True, True))
+    op("v", ["iot", "lst3"], ["nbs"], lambda e: e.tensor_copy(T.nbs[:], T.iot[:].indirect(T.lst3[:, 4:8])))
+    for k in range(4):
+        dma("sa"[k % 2], ["s3o"], [], "st%d" % (1 + k), T.osc[4 * k:4 * k + 4, :], T.s3[32 * k:32 * k + 4, 64:128])
+    op("v", ["PS"], ["ys"], lambda e: e.tensor_copy(T.ys[:], T.PS[:, 64:128]))
+    dma("s", ["nbs"], [], "st5", T.nb[:], T.nbs[0:1, :])
+    dma("a", ["ys"], [], "st6", T.y[:], T.ys[:])
+    finish()
+    g.wait_ge(T.sem.sent, sent[0])

@@ -1,6 +1,5 @@
 from concourse.mybir import dt, AluOpType as OP, AxisListType, ActivationFunctionType as AF
 
-K = 64
 BIG = 1.0e29
 TINY = 2.0 ** -120
 MAGIC = 1.5 * 2.0 ** 27
@@ -8,16 +7,16 @@ MAGIC = 1.5 * 2.0 ** 27
 F32, B16, I32, U16, U8, MX = "float32", "bfloat16", "int32", "uint16", "uint8", "float8_e4m3fn_x4"
 SCRATCH = {}
 for _d, _names in (
-        (B16, "ut 16|grt 1024|wt 512|ones 520|zer 512|ur 512|zd 520|idt 128|iot 256|hp 512|ld0 128|ldz 128|kr 64|neg1 64|xx0 576|xx 544"
-              "|pt 512|c0 256|c1 256|ht0 1024|m_t1 256|m_t2 256|m_t3 256|m_t4 256|m_nr 128|m_da 272|m_db 256|m_mt 512|m_ld 128|m_ht 512"),
-        (F32, "cst 8|mask4 64|rst4 64|m4 4|phi 4|plo 4|sr0 256|sc0 8|nsc0 8|d0 128|d1 128|rk0 8|nbs 64|ys 64|m_dg 64|m_dga 64|m_na 8"
+        (B16, "ut 16|grt 1024|wt 512|ones 520|zer 512|ur 512|zd 520|idt 128|iot 256|hp 512|ld0 128|ldz 128|kr 64|neg1 64|xx0 576|xx 560"
+              "|pt 512|c0 256|c1 256|c2 256|ht0 1024|m_t1 256|m_t2 256|m_t3 256|m_t4 256|m_nr 128|m_da 272|m_db 256|m_mt 512|m_ld 128|m_ht 512"),
+        (F32, "cst 8|mask4 64|rst4 64|m4 4|phi 4|plo 4|sr0 256|sc0 8|nsc0 8|d0 128|d1 128|rk0 8|nbs 64|ys 64|ytab 256|m_dg 64|m_dga 64|m_na 8"
               "|m_nb2 8|m_nc 8|m_ncx 8|m_pen 8|m_hm 8|m_cnt 8|m_notm 8|m_eq 128|m_eq2 128|m_g4 64|m_g5 64|m_mb 64|m_rw 128|m_sr 128"
-              "|m_rm 64|m_bc 8|m_sc 8|m_dd 128|m_cc 128|m_rk 8|m_sel 8|m_ps 8"),
+              "|m_rm 64|m_bc 8|m_sc 8|m_dd 128|m_cc 128|m_rk 8|m_sel 8"),
         (I32, "pi 8|bi 8|bj 8"),
-        (U16, "hl 2|lst0 8|lst1 8|lst2 8|lst3 8|bl0 2|bl1 4|bl2 4|bu 4|m_toff 16")):
+        (U16, "hl 4|lst0 8|lst1 8|lst2 12|lst3 8|bl0 4|bl1 4|bl2 2|bu 4|m_toff 16")):
     for _n in _names.split("|"):
         SCRATCH[_n.split()[0]] = ("sbuf", [128, int(_n.split()[1])], _d)
-for _n, _w in (("u", 128), ("e", 512), ("g", 256), ("w", 128), ("n", 128), ("x0", 144), ("x1", 136), ("x2", 136), ("x3", 136), ("p", 128),
+for _n, _w in (("u", 128), ("e", 512), ("g", 256), ("w", 128), ("n", 128), ("x0", 144), ("x1", 140), ("x2", 140), ("x3", 140), ("p", 128),
                ("h0", 256), ("h1", 128), ("h2", 128), ("h3", 128)):
     SCRATCH["q" + _n] = ("sbuf", [128, _w], MX)
     SCRATCH["s" + _n] = ("sbuf", [128, _w], U8)
@@ -143,60 +142,57 @@ def rank_program(g, core, T, topo):
     X = AxisListType.X
     pf, pm4, q4, isa, isb = [T.cst[:, i:i + 1] for i in range(5)]
 
-    dma("s", [], ["ut"], "ld0", T.ut[:, 0:4], T.u[:, 0:4])
-    dma("a", [], ["gr1"], "ld2", T.grt[:, 512:1024], T.gr[:, 512:1024])
     dma("s", [], ["gr0"], "ld1", T.grt[:, 0:512], T.gr[:, 0:512])
+    dma("a", [], ["ut"], "ld0", T.ut[:, 0:4], T.u[:, 0:4])
+    dma("a", [], ["gr1"], "ld2", T.grt[:, 512:1024], T.gr[:, 512:1024])
     dma("s", [], ["wt"], "ld3", T.wt[:], T.w[:])
 
-    op("v", [], ["ones"], lambda e: e.memset(T.ones[:], 1.0))
     op("g", [], ["pi"], lambda e: e.iota(T.pi[:, 0:1], [[0, 1]], 0, 1))
-    op("v", [], ["zer"], lambda e: e.memset(T.zer[:], 0.0))
-    op("v", [], ["xx0"], lambda e: e.memset(T.xx0[:], 0.0))
     op("v", [], ["m4"], lambda e: e.memset(T.m4[:], MAGIC))
     op("v", [], ["ldz"], lambda e: e.memset(T.ldz[:], -TINY))
+    op("v", [], ["xx0z"], lambda e: e.memset(T.xx0[:], 0.0))
+    op("v", ["pi"], ["pf"], lambda e: e.tensor_copy(pf, T.pi[:, 0:1]))
     op("g", ["ldz"], ["ld0"], lambda e: e.affine_select(T.ld0[:], T.ldz[:], [[-1, 128]], OP.is_gt, 0.0, 0, 1))
     op("g", [], ["hp"], lambda e: e.iota(T.hp[:], [[0, 8], [1, 16], [16, 4]], 0, 0, allow_small_or_imprecise_dtypes=True))
-    op("v", ["pi"], ["pf"], lambda e: e.tensor_copy(pf, T.pi[:, 0:1]))
+    op("v", ["m4", "pf"], ["phi"], lambda e: e.tensor_scalar(T.phi[:], T.m4[:], pf, MAGIC, OP.add, OP.subtract))
+    op("v", [], ["ones"], lambda e: e.memset(T.ones[:], 1.0))
+    op("v", ["phi", "pf"], ["plo"], lambda e: e.tensor_scalar(T.plo[:], T.phi[:], pf, -1.0, OP.subtract, OP.mult))
+    op("v", [], ["zer"], lambda e: e.memset(T.zer[:], 0.0))
+    for i, src, add in ((0, "phi", 0.0), (32, "phi", 128.0), (64, "plo", 0.0)):
+        op("v", [src, "xx0z"], ["xx0"], lambda e: e.tensor_scalar(T.xx0[:, i:i + 16:5], T[src][:], add, None, OP.add))
+    op("v", ["zer"], ["x0p", "x0o"], lambda e: e.quantize_mx(T.x0[:, 0:128], T.s0[:, 0:128], T.zer[:]))
+    op("v", ["xx0"], ["qx0"], lambda e: e.quantize_mx(T.qx0[:], T.sx0[:], T.xx0[:]))
     for t in range(4):
         op("v", ["ones", "ut"], ["ur"], lambda e: e.tensor_scalar(T.ur[:, t:512:4], T.ones[:, 0:128], T.ut[:, t:t + 1], None, OP.mult))
     op("v", ["ur"], ["qu"], lambda e: e.quantize_mx(T.qu[:], T.su[:], T.ur[:]))
-    op("v", ["m4", "pf"], ["phi"], lambda e: e.tensor_scalar(T.phi[:], T.m4[:], pf, MAGIC, OP.add, OP.subtract))
-    op("v", ["phi", "pf"], ["plo"], lambda e: e.tensor_scalar(T.plo[:], T.phi[:], pf, -1.0, OP.subtract, OP.mult))
-    for i, src, add in ((0, "phi", 0.0), (32, "phi", 128.0), (64, "plo", 0.0)):
-        op("v", [src, "xx0"], ["xx0"], lambda e: e.tensor_scalar(T.xx0[:, i:i + 16:5], T[src][:], add, None, OP.add))
-        op("v", [src, "xx0"], ["xx0"], lambda e: e.tensor_scalar(T.xx0[:, i + 16:i + 22:5], T[src][:, 0:2], add, None, OP.add))
-        op("v", [src, "xx0"], ["xx0"], lambda e: e.tensor_scalar(T.xx0[:, i + 18:i + 24:5], T[src][:, 0:2], add, 256.0, OP.add, OP.mult))
-    op("v", ["xx0"], ["qx0"], lambda e: e.quantize_mx(T.qx0[:], T.sx0[:], T.xx0[:]))
-    op("v", ["zer"], ["x0p", "x0o"], lambda e: e.quantize_mx(T.x0[:, 0:128], T.s0[:, 0:128], T.zer[:]))
 
     H = [slice(0, 128), slice(128, 256)]
     for h in range(2):
-        op("v", ["gr%d" % h], ["qg"], lambda e: e.quantize_mx(T.qg[:, H[h]], T.sg[:, H[h]], T.grt[:, 512 * h:512 * h + 512]))
-    op("t", ["qu", "qg"], ["PR"], lambda e: e.matmul_mx(T.PR[:, 0:256], T.qu[:], T.su[:], T.qg[:], T.sg[:], True, True))
+        op("v", ["gr%d" % h], ["qg%d" % h], lambda e: e.quantize_mx(T.qg[:, H[h]], T.sg[:, H[h]], T.grt[:, 512 * h:512 * h + 512]))
     for h, P in ((0, "PC"), (1, "PS")):
-        op("t", ["qu", "qg"], [P], lambda e: e.matmul_mx(T[P][:, 0:128], T.qg[:, H[h]], T.sg[:, H[h]], T.qu[:], T.su[:], True, True))
-    op("a", ["PR"], ["sr0"], lambda e: e.activation(T.sr0[:], T.PR[:, 0:256], AF.Abs))
-    for h, P in ((0, "PC"), (1, "PS")):
+        op("t", ["qu", "qg%d" % h], ["PE%d" % h], lambda e: e.matmul_mx(T.PE[:, 512 * h:512 * h + 128], T.qu[:], T.su[:], T.qg[:, H[h]], T.sg[:, H[h]], True, True))
+        op("t", ["qu", "qg%d" % h], [P], lambda e: e.matmul_mx(T[P][:, 0:128], T.qg[:, H[h]], T.sg[:, H[h]], T.qu[:], T.su[:], True, True))
+        op("a", ["PE%d" % h], ["sr0%d" % h], lambda e: e.activation(T.sr0[:, H[h]], T.PE[:, 512 * h:512 * h + 128], AF.Abs))
         op("v", [P], ["nsc%d" % h], lambda e: e.tensor_reduce(T.nsc0[:, h:h + 1], T[P][:, 0:1], X, OP.max, negate=True, apply_absolute_value=True))
         op("v", [P], ["sc0%d" % h], lambda e: e.tensor_reduce(T.sc0[:, h:h + 1], T[P][:, 0:1], X, OP.max, apply_absolute_value=True))
-        op("a", ["sr0", "nsc%d" % h], ["d%d" % h], lambda e: e.activation(T["d%d" % h][:], T.sr0[:, H[h]], AF.Identity, bias=T.nsc0[:, h:h + 1]))
     for h in range(2):
-        op("v", ["sr0", "sc0%d" % h], ["c%da" % h], lambda e: e.tensor_scalar(
+        op("a", ["sr0%d" % h, "nsc%d" % h], ["d%d" % h], lambda e: e.activation(T["d%d" % h][:], T.sr0[:, H[h]], AF.Identity, bias=T.nsc0[:, h:h + 1]))
+    for h in range(2):
+        op("v", ["sr0%d" % (1 - h), "sc0%d" % h], ["c%da" % h], lambda e: e.tensor_scalar(
             T["c%d" % h][:, H[1 - h]], T.sr0[:, H[1 - h]], T.sc0[:, h:h + 1], None, OP.is_ge if h else OP.is_gt))
-    for h in range(2):
         op("v", ["d%d" % h, "ld0"], ["c%db" % h], lambda e: e.tensor_tensor(T["c%d" % h][:, H[h]], T["d%d" % h][:], T.ld0[:], OP.is_gt))
-    for h in range(2):
-        op("v", ["c%da" % h, "c%db" % h], ["rk0%d" % h], lambda e: e.tensor_reduce(T.rk0[:, h:h + 1], T["c%d" % h][:], X, OP.add))
+    op("a", ["c0a", "c0b"], ["rk00", "c2"], lambda e: e.activation(T.c2[:], T.c0[:], AF.Copy, accum_out=T.rk0[:, 0:1]))
+    op("v", ["c1a", "c1b"], ["rk01"], lambda e: e.tensor_reduce(T.rk0[:, 1:2], T.c1[:], X, OP.add))
     for h in range(2):
         op("v", ["hp", "rk0%d" % h], ["ht0%d" % h], lambda e: e.tensor_scalar(T.ht0[:, 512 * h:512 * h + 512], T.hp[:], T.rk0[:, h:h + 1], None, OP.is_equal))
     for h in range(2):
         op("v", ["ht0%d" % h], ["qh0%d" % h], lambda e: e.quantize_mx(T.qh0[:, H[h]], T.sh0[:, H[h]], T.ht0[:, 512 * h:512 * h + 512]))
     for i, (h, c) in enumerate(((0, 0), (0, 16), (1, 8), (1, 16))):
         op("t", ["qh0%d" % h, "qx0"], ["PL"], lambda e: e.matmul_mx(T.PL[:, 0:128], T.qh0[:, H[h]], T.sh0[:, H[h]], T.qx0[:, c:c + 128], T.sx0[:, c:c + 128], i == 0, i == 3))
-    op("v", ["PL"], ["lst0"], lambda e: e.tensor_copy(T.lst0[:, 0:6], T.PL[:, 0:6]))
+    op("v", ["PL"], ["lst0"], lambda e: e.tensor_copy(T.lst0[:, 0:4], T.PL[:, 0:4]))
 
     def pick(src, ssrc, lo, hi, lst, b):
-        toks = ["qg"] if b == 0 else ["x%do" % (b - 1), "s%do" % (b - 1), "x%dl" % (b - 1), "x%dm" % (b - 1)]
+        toks = ["qg0", "qg1"] if b == 0 else ["x%do" % (b - 1), "s%do" % (b - 1), "x%dl" % (b - 1), "x%dm" % (b - 1)]
         op("v", toks + [lst], ["x%do" % b], lambda e: e.tensor_copy(
             T["x%d" % b][:, 64:128].bitcast(dt.uint32), T[src][:, lo:hi].bitcast(dt.uint32).indirect(T[lst][:, 0:4])))
         op("a", toks + [lst, "x%dp" % b], ["s%do" % b], lambda e: e.activation(
@@ -205,7 +201,7 @@ def rank_program(g, core, T, topo):
     ha, hb = helpers(rank)
     away = T.cores[rank ^ 2]
     ready("g", ["lst0"])
-    send(T.hl[:], T.lst0[:, 4:6], hb, "hl", away)
+    send(T.hl[:], T.lst0[:, 0:4], hb, "hl", away)
     pick("qg", "sg", 0, 256, "lst0", 0)
     ready("g", ["x0o"])
     send(bits(T.hc[:]), bits(T.x0[:, 64:128]), ha, "hc", away)
@@ -244,14 +240,14 @@ def rank_program(g, core, T, topo):
     op("v", ["kr"], ["rst4"], lambda e: e.tensor_scalar(T.rst4[:], T.kr[:], 0.5, None, OP.is_gt))
     op("v", ["kr", "q4"], ["mask4"], lambda e: e.tensor_scalar(T.mask4[:], T.kr[:], q4, None, OP.is_equal))
     op("v", [], ["neg1"], lambda e: e.memset(T.neg1[:], -1.0))
-    op("v", [], ["xx"], lambda e: e.memset(T.xx[:], 0.0))
+    op("v", [], ["xxz"], lambda e: e.memset(T.xx[:], 0.0))
     op("v", [], ["mtz"], lambda e: e.memset(T.m_mt[:, 0:256], 0.0))
-    op("v", ["plo", "xx"], ["xx"], lambda e: e.tensor_copy(T.xx[:, 32:48:5], T.plo[:]))
+    op("v", ["plo", "xxz"], ["xxz"], lambda e: e.tensor_copy(T.xx[:, 48:64:5], T.plo[:]))
     for b in range(1, 4):
         op("v", ["zer"], ["x%dp" % b, "x%do" % b, "s%do" % b], lambda e: e.quantize_mx(T["x%d" % b][:, 0:128], T["s%d" % b][:, 0:128], T.zer[:]))
 
     def idle_work():
-        op("v", [], ["pt"], lambda e: e.memset(T.pt[:], 0.0))
+        op("v", [], ["ptz"], lambda e: e.memset(T.pt[:], 0.0))
         op("v", ["ones"], ["qn"], lambda e: e.quantize_mx(T.qn[:], T.sn[:], T.ones[:, 0:512]))
         op("v", ["wt"], ["qw"], lambda e: e.quantize_mx(T.qw[:], T.sw[:], T.wt[:]))
 
@@ -264,33 +260,37 @@ def rank_program(g, core, T, topo):
         arrives("bl%d" % b, "al%d" % b, n)
         arrives("x%dl" % b, "ac%d" % b, 2 * n)
 
-        if b == 0:
-            op("v", ["bl0"], ["bi"], lambda e: e.tensor_copy(T.bi[:, 0:2], T.bl0[:]))
+        if b == 2:
+            op("v", ["bl2"], ["bi"], lambda e: e.tensor_copy(T.bi[:, 0:2], T.bl2[:]))
             op("v", ["bi"], ["bj"], lambda e: e.tensor_scalar(T.bj[:, 0:2], T.bi[:, 0:2], 255, None, OP.bitwise_and))
             op("v", ["bi"], ["bj"], lambda e: e.tensor_scalar(T.bj[:, 2:4], T.bi[:, 0:2], 8, None, OP.logical_shift_right))
             op("v", ["bj"], ["bu"], lambda e: e.tensor_copy(T.bu[:], T.bj[:, 0:4]))
-        bwt = "bl%d" % b if b else "bu"
+        bwt = "bl%d" % b if b < 2 else "bu"
         bw = T[bwt][:]
+        op("v", ["iot", bwt, "idt"], ["dg"], lambda e: e.tensor_tensor(T.m_dg[:], T.iot[:].indirect(bw), T.idt[:, 64:128], OP.mult))
+        op("a", ["iot", bwt], ["nrb"], lambda e: e.activation(T.m_nr[:, 64:128], T.iot[:].indirect(bw), AF.Copy))
         op("v", ["t1", bwt, "mask4"], ["g4"], lambda e: e.tensor_tensor(T.m_g4[:], T.m_t1[:].indirect(bw), T.mask4[:], OP.mult))
         op("a", ["t2", bwt], ["mb"], lambda e: e.activation(T.m_mb[:], T.m_t2[:].indirect(bw), AF.Copy))
-        op("v", ["g4", "rst4"], ["g5"], lambda e: e.tensor_tensor_scan(T.m_g5[:], T.rst4[:], T.m_g4[:], 0.0, OP.mult, OP.add))
-        op("v", ["iot", bwt, "idt"], ["dg"], lambda e: e.tensor_tensor(T.m_dg[:], T.iot[:].indirect(bw), T.idt[:, 64:128], OP.mult))
-        op("v", ["g5", "pm4"], ["toff"], lambda e: e.tensor_scalar(T.m_toff[:], T.m_g5[:, 3:64:4], 4.0, pm4, OP.mult, OP.add))
-        op("a", ["iot", bwt], ["nrb"], lambda e: e.activation(T.m_nr[:, 64:128], T.iot[:].indirect(bw), AF.Copy))
         op("v", ["dg"], ["nb2"], lambda e: e.tensor_reduce(T.m_nb2[:, 0:1], T.m_dg[:], X, OP.add))
+        op("v", ["g4", "rst4"], ["g5"], lambda e: e.tensor_tensor_scan(T.m_g5[:], T.rst4[:], T.m_g4[:], 0.0, OP.mult, OP.add))
         op("v", ["na", "nb2"], ["nc"], lambda e: e.tensor_tensor(T.m_nc[:, 0:1], T.m_na[:, 0:1], T.m_nb2[:, 0:1], OP.add))
+        op("v", ["g5", "pm4"], ["toff"], lambda e: e.tensor_scalar(T.m_toff[:], T.m_g5[:, 3:64:4], 4.0, pm4, OP.mult, OP.add))
         op("a", ["nra", "nrb", "nc"], ["eq"], lambda e: e.activation(T.m_eq[:], T.m_nr[:], AF.Abs, bias=T.m_nc[:, 0:1], scale=-1.0))
         op("a", ["eq"], ["cnt", "eq2"], lambda e: e.activation(T.m_eq2[:], T.m_eq[:], AF.Relu, bias=1.0, scale=-1.0, accum_out=T.m_cnt[:, 0:1]))
         op("a", ["cnt"], ["notm"], lambda e: e.activation(T.m_notm[:, 0:1], T.m_cnt[:, 0:1], AF.Copy, bias=2.0, scale=-1.0))
         op("v", ["t4", "neg1", bwt], ["t4"], lambda e: e.tensor_copy(T.m_t4[:].indirect(bw), T.neg1[:]))
-        op("v", ["m4", "nc", "xx"], ["xx"], lambda e: e.tensor_scalar(T.xx[:, 16:32:5], T.m4[:], T.m_nc[:, 0:1], MAGIC, OP.add, OP.subtract))
-        op("v", ["xx", "nc"], ["xx"], lambda e: e.tensor_scalar(T.xx[:, 48:64:5], T.xx[:, 16:32:5], T.m_nc[:, 0:1], -1.0, OP.subtract, OP.mult))
+        op("v", ["m4", "nc", "xxz"], ["xxn"], lambda e: e.tensor_scalar(T.xx[:, 16:32:5], T.m4[:], T.m_nc[:, 0:1], MAGIC, OP.add, OP.subtract))
         op("v", ["cnt", "isa"], ["pen"], lambda e: e.tensor_scalar(T.m_pen[:, 0:1], T.m_cnt[:, 0:1], -1.0, isa, OP.add, OP.mult))
         op("v", ["cnt", "isb"], ["hm"], lambda e: e.tensor_scalar(T.m_hm[:, 0:1], T.m_cnt[:, 0:1], -1.0, isb, OP.add, OP.mult))
+        op("v", ["xxn", "nc"], ["xxm"], lambda e: e.tensor_scalar(T.xx[:, 64:80:5], T.xx[:, 16:32:5], T.m_nc[:, 0:1], -1.0, OP.subtract, OP.mult))
         op("v", ["pen", "nc"], ["ncx"], lambda e: e.tensor_tensor(T.m_ncx[:, 0:1], T.m_pen[:, 0:1], T.m_nc[:, 0:1], OP.add))
         op("v", ["phi", "hm"], ["xx"], lambda e: e.tensor_scalar(T.xx[:, 0:16:5], T.phi[:], T.m_hm[:, 0:1], None, OP.add))
+        if b == 1:
+            for i in (0, 48):
+                op("v", ["xxn", "xxm"], ["xx"], lambda e: e.tensor_scalar(T.xx[:, i + 32:i + 38:5], T.xx[:, i + 16:i + 22:5], 1.0, None, OP.mult))
+                op("v", ["xxn", "xxm"], ["xx"], lambda e: e.tensor_scalar(T.xx[:, i + 34:i + 40:5], T.xx[:, i + 16:i + 22:5], 256.0, None, OP.mult))
         op("v", ["nra", "nrb", "ncx"], ["ld"], lambda e: e.tensor_scalar(T.m_ld[:], T.m_nr[:], T.m_ncx[:, 0:1], -TINY, OP.is_lt, OP.mult))
-        op("v", ["xx"], ["qx"], lambda e: e.quantize_mx(T["qx%d" % nx][:], T["sx%d" % nx][:], T.xx[:]))
+        op("v", ["xx", "xxm"], ["qx"], lambda e: e.quantize_mx(T["qx%d" % nx][:], T["sx%d" % nx][:], T.xx[:]))
 
         both = ["x%do" % b, "s%do" % b, "x%dl" % b]
         for t in range(4):
@@ -314,26 +314,28 @@ def rank_program(g, core, T, topo):
         op("v", ["sra", "srb", "sc"], ["dd"], lambda e: e.tensor_scalar(T.m_dd[:], T.m_sr[:], T.m_sc[:, 0:1], None, OP.subtract))
         op("v", ["dd", "ld"], ["cc"], lambda e: e.tensor_tensor(T.m_cc[:], T.m_dd[:], T.m_ld[:], OP.is_gt))
         op("v", ["cc"], ["rk"], lambda e: e.tensor_reduce(T.m_rk[:, 0:1], T.m_cc[:], X, OP.add))
-        key = "rk"
-        if b == 2:
+        if b < 2:
+            op("v", ["hp", "rk"], ["ht"], lambda e: e.tensor_scalar(T.m_ht[:], T.hp[:], T.m_rk[:, 0:1], None, OP.is_equal))
+        else:
+            for i, (lo, tok) in enumerate(((64, "x2l"), (192, "x2m"))):
+                op("t", ["qw", "x2o", "s2o", tok], ["PE%d" % i], lambda e: e.matmul_mx(T.PE[:, 512 * i:512 * i + 128], T.qw[:], T.sw[:], x[:, lo:lo + 128], s[:, lo:lo + 128], True, True))
+                op("a", ["PE%d" % i], ["yt%d" % i], lambda e: e.activation(T.ytab[:, 128 * i:128 * i + 128], T.PE[:, 512 * i:512 * i + 128], AF.Copy))
             op("v", ["rk"], ["sel"], lambda e: e.tensor_scalar(T.m_sel[:, 0:1], T.m_rk[:, 0:1], 63.5, None, OP.is_lt))
-            op("v", ["rk"], ["pen"], lambda e: e.tensor_scalar(T.m_pen[:, 0:1], T.m_rk[:, 0:1], 63.5, 1000.0, OP.is_gt, OP.mult))
-            op("v", ["nra", "nrb", "nc", "sel", "pt"], ["pt"], lambda e: e.tensor_scalar(T.pt[:, 0:512:4], T.m_nr[:], T.m_nc[:, 0:1], T.m_sel[:, 0:1], OP.is_gt, OP.mult))
+            op("v", ["nra", "nrb", "nc", "sel", "ptz"], ["pt"], lambda e: e.tensor_scalar(T.pt[:, 0:512:4], T.m_nr[:], T.m_nc[:, 0:1], T.m_sel[:, 0:1], OP.is_gt, OP.mult))
             op("v", ["pt"], ["qp"], lambda e: e.quantize_mx(T.qp[:], T.sp[:], T.pt[:]))
             op("t", ["qp", "qn"], ["PC"], lambda e: e.matmul_mx(T.PC[:, 0:128], T.qp[:], T.sp[:], T.qn[:], T.sn[:], True, True))
-            op("v", ["PC", "pen"], ["ps"], lambda e: e.tensor_tensor(T.m_ps[:, 0:1], T.PC[:, 0:1], T.m_pen[:, 0:1], OP.add))
-            key = "ps"
-        op("v", ["hp", key], ["ht"], lambda e: e.tensor_scalar(T.m_ht[:], T.hp[:], T["m_" + key][:, 0:1], None, OP.is_equal))
+            op("v", ["hp", "PC", "sel"], ["ht"], lambda e: e.tensor_scalar(T.m_ht[:], T.hp[:], T.PC[:, 0:1], T.m_sel[:, 0:1], OP.is_equal, OP.mult))
         op("v", ["ht"], ["qh"], lambda e: e.quantize_mx(T["qh%d" % nx][:], T["sh%d" % nx][:], T.m_ht[:]))
-        for c in (0, 8):
+        for c in (0, 12):
             op("t", ["qh", "qx"], ["PL"], lambda e: e.matmul_mx(
-                T.PL[:, 0:128], T["qh%d" % nx][:], T["sh%d" % nx][:], T["qx%d" % nx][:, c:c + 128], T["sx%d" % nx][:, c:c + 128], c == 0, c == 8))
+                T.PL[:, 0:128], T["qh%d" % nx][:], T["sh%d" % nx][:], T["qx%d" % nx][:, c:c + 128], T["sx%d" % nx][:, c:c + 128], c == 0, c == 12))
         lst = "lst%d" % nx
-        op("v", ["PL"], [lst], lambda e: e.tensor_copy(T[lst][:], T.PL[:, 0:8]))
+        m = 10 if b == 1 else 8
+        op("v", ["PL"], [lst], lambda e: e.tensor_copy(T[lst][:, 0:m], T.PL[:, 0:m]))
         if b < 2:
             to = T.cores[rank ^ (1 << nx)]
             ready("g", [lst])
-            send(T["bl%d" % nx][:], T[lst][:, 4:8], to, "al%d" % nx)
+            send(T["bl%d" % nx][:], T[lst][:, 4:8] if b == 0 else T[lst][:, 8:10], to, "al%d" % nx)
             pick("x%d" % b, "s%d" % b, 64, 320, lst, nx)
             ready("g", ["x%do" % nx])
             send(bits(T["x%d" % nx][:, 128:192]), bits(T["x%d" % nx][:, 64:128]), to, "ac%d" % nx)
@@ -345,12 +347,13 @@ def rank_program(g, core, T, topo):
 
     pick("x2", "s2", 64, 320, "lst3", 3)
     dma("s", ["x3o"], [], "st0", T.oc[:], bits(T.x3[:, 64:128]))
-    op("t", ["qw", "x3p", "x3o", "s3o"], ["PS"], lambda e: e.matmul_mx(T.PS[:, 0:128], T.qw[:], T.sw[:], T.x3[:], T.s3[:], True, True))
+    op("v", ["yt0", "yt1", "lst3"], ["ys"], lambda e: e.tensor_copy(T.ys[:], T.ytab[:].indirect(T.lst3[:, 0:4])))
     op("v", ["iot", "lst3"], ["nbs"], lambda e: e.tensor_copy(T.nbs[:], T.iot[:].indirect(T.lst3[:, 4:8])))
-    for k in range(4):
-        dma("sa"[k % 2], ["s3o"], [], "st%d" % (1 + k), T.osc[4 * k:4 * k + 4, :], T.s3[32 * k:32 * k + 4, 64:128])
-    op("v", ["PS"], ["ys"], lambda e: e.tensor_copy(T.ys[:], T.PS[:, 64:128]))
+    dma("a", ["s3o"], [], "st1", T.osc[0:4, :], T.s3[0:4, 64:128])
+    dma("s", ["ys"], [], "st6", T.y[:], T.ys[:])
+    dma("a", ["s3o"], [], "st2", T.osc[4:8, :], T.s3[32:36, 64:128])
+    dma("a", ["s3o"], [], "st3", T.osc[8:12, :], T.s3[64:68, 64:128])
     dma("s", ["nbs"], [], "st5", T.nb[:], T.nbs[0:1, :])
-    dma("a", ["ys"], [], "st6", T.y[:], T.ys[:])
+    dma("a", ["s3o"], [], "st4", T.osc[12:16, :], T.s3[96:100, 64:128])
     finish()
     g.wait_ge(T.sem.sent, sent[0])

@@ -7,13 +7,14 @@ MAGIC = 1.5 * 2.0 ** 27
 F32, B16, I32, U16, U8, MX = "float32", "bfloat16", "int32", "uint16", "uint8", "float8_e4m3fn_x4"
 SCRATCH = {}
 for _d, _names in (
-        (B16, "ut 16|grt 1024|wt 512|ones 520|zer 512|ur 512|zd 520|idt 128|iot 256|hp 512|ld0 128|ldz 128|kr 64|neg1 64|xx0 576|xx 560"
-              "|pt 512|c0 256|c1 256|c2 256|ht0 1024|m_t1 256|m_t2 256|m_t3 256|m_t4 256|m_nr 128|m_da 272|m_db 256|m_mt 512|m_ld 128|m_ht 512"),
-        (F32, "cst 8|mask4 64|rst4 64|m4 4|phi 4|plo 4|sr0 256|sc0 8|nsc0 8|d0 128|d1 128|rk0 8|nbs 64|ys 64|ytab 256|m_dg 64|m_dga 64|m_na 8"
-              "|m_nb2 8|m_nc 8|m_ncx 8|m_pen 8|m_hm 8|m_cnt 8|m_notm 8|m_eq 128|m_eq2 128|m_g4 64|m_g5 64|m_mb 64|m_rw 128|m_sr 128"
+        (B16, "ut 16|grt 1024|wt 512|ones 520|zer 512|ur 512|zd 520|iot 256|hp 512|ld0 128|ldz 128|kr 64|neg1 64|xx0 576|xx 560"
+              "|pt 512|c0 256|c1 256|c2 256|ht0 1024|m_t1 256|m_t2 256|m_t3 256|m_t4 256|m_nr 256|m_dx 128|m_dy 128|m_gt 128|m_da 320|m_db 256"
+              "|m_mt 512|m_ld 128|m_ht 512"),
+        (F32, "cst 8|mask 64|rst 64|m4 4|phi 4|plo 4|isb 4|sr0 256|sc0 8|nsc0 8|d0 128|d1 128|rk0 8|nbs 64|ys 64|ytab 256"
+              "|m_nc 8|m_ncx 8|m_cnt 8|m_notm 8|m_ok 8|m_eq 128|m_eq2 128|m_g4 64|m_g5 64|m_mb 64|m_rw 128|m_sr 128"
               "|m_rm 64|m_bc 8|m_sc 8|m_dd 128|m_cc 128|m_rk 8|m_sel 8"),
         (I32, "pi 8|bi 8|bj 8"),
-        (U16, "hl 4|lst0 8|lst1 8|lst2 12|lst3 8|bl0 4|bl1 4|bl2 2|bu 4|m_toff 16")):
+        (U16, "hl 4|lst0 8|lst1 8|lst2 12|lst3 8|bl0 4|bl1 4|bl2 2|bu 4|m_toff 4")):
     for _n in _names.split("|"):
         SCRATCH[_n.split()[0]] = ("sbuf", [128, int(_n.split()[1])], _d)
 for _n, _w in (("u", 128), ("e", 512), ("g", 256), ("w", 128), ("n", 128), ("x0", 144), ("x1", 140), ("x2", 140), ("x3", 140), ("p", 128),
@@ -140,7 +141,7 @@ def rank_program(g, core, T, topo):
 
     op, dma, arrives, ready, finish = make_flow(g, T)
     X = AxisListType.X
-    pf, pm4, q4, isa, isb = [T.cst[:, i:i + 1] for i in range(5)]
+    pf, pm, isb1, phm, isa1, k1000 = [T.cst[:, i:i + 1] for i in range(6)]
 
     dma("s", [], ["gr0"], "ld1", T.grt[:, 0:512], T.gr[:, 0:512])
     dma("a", [], ["ut"], "ld0", T.ut[:, 0:4], T.u[:, 0:4])
@@ -148,27 +149,28 @@ def rank_program(g, core, T, topo):
     dma("s", [], ["wt"], "ld3", T.wt[:], T.w[:])
 
     op("g", [], ["pi"], lambda e: e.iota(T.pi[:, 0:1], [[0, 1]], 0, 1))
-    op("v", [], ["m4"], lambda e: e.memset(T.m4[:], MAGIC))
-    op("v", [], ["ldz"], lambda e: e.memset(T.ldz[:], -TINY))
-    op("v", [], ["xx0z"], lambda e: e.memset(T.xx0[:], 0.0))
-    op("v", ["pi"], ["pf"], lambda e: e.tensor_copy(pf, T.pi[:, 0:1]))
-    op("g", ["ldz"], ["ld0"], lambda e: e.affine_select(T.ld0[:], T.ldz[:], [[-1, 128]], OP.is_gt, 0.0, 0, 1))
     op("g", [], ["hp"], lambda e: e.iota(T.hp[:], [[0, 8], [1, 16], [16, 4]], 0, 0, allow_small_or_imprecise_dtypes=True))
-    op("v", ["m4", "pf"], ["phi"], lambda e: e.tensor_scalar(T.phi[:], T.m4[:], pf, MAGIC, OP.add, OP.subtract))
+    op("v", [], ["m4"], lambda e: e.memset(T.m4[:], MAGIC))
     op("v", [], ["ones"], lambda e: e.memset(T.ones[:], 1.0))
+    op("v", ["pi"], ["pf"], lambda e: e.tensor_copy(pf, T.pi[:, 0:1]))
+    op("v", [], ["xx0z"], lambda e: e.memset(T.xx0[:], 0.0))
+    op("v", ["m4", "pf"], ["phi"], lambda e: e.tensor_scalar(T.phi[:], T.m4[:], pf, MAGIC, OP.add, OP.subtract))
+    op("v", [], ["ldz"], lambda e: e.memset(T.ldz[:], -TINY))
+    op("g", ["ldz"], ["ld0"], lambda e: e.affine_select(T.ld0[:], T.ldz[:], [[-1, 128]], OP.is_gt, 0.0, 0, 1))
     op("v", ["phi", "pf"], ["plo"], lambda e: e.tensor_scalar(T.plo[:], T.phi[:], pf, -1.0, OP.subtract, OP.mult))
-    op("v", [], ["zer"], lambda e: e.memset(T.zer[:], 0.0))
     for i, src, add in ((0, "phi", 0.0), (32, "phi", 128.0), (64, "plo", 0.0)):
-        op("v", [src, "xx0z"], ["xx0"], lambda e: e.tensor_scalar(T.xx0[:, i:i + 16:5], T[src][:], add, None, OP.add))
-    op("v", ["zer"], ["x0p", "x0o"], lambda e: e.quantize_mx(T.x0[:, 0:128], T.s0[:, 0:128], T.zer[:]))
-    op("v", ["xx0"], ["qx0"], lambda e: e.quantize_mx(T.qx0[:], T.sx0[:], T.xx0[:]))
+        op("a", [src, "xx0z"], ["xx0"], lambda e: e.activation(T.xx0[:, i:i + 16:5], T[src][:], AF.Copy, bias=add))
     for t in range(4):
         op("v", ["ones", "ut"], ["ur"], lambda e: e.tensor_scalar(T.ur[:, t:512:4], T.ones[:, 0:128], T.ut[:, t:t + 1], None, OP.mult))
-    op("v", ["ur"], ["qu"], lambda e: e.quantize_mx(T.qu[:], T.su[:], T.ur[:]))
-
     H = [slice(0, 128), slice(128, 256)]
-    for h in range(2):
-        op("v", ["gr%d" % h], ["qg%d" % h], lambda e: e.quantize_mx(T.qg[:, H[h]], T.sg[:, H[h]], T.grt[:, 512 * h:512 * h + 512]))
+    op("v", ["gr0"], ["qg0"], lambda e: e.quantize_mx(T.qg[:, H[0]], T.sg[:, H[0]], T.grt[:, 0:512]))
+    op("v", ["ur"], ["qu"], lambda e: e.quantize_mx(T.qu[:], T.su[:], T.ur[:]))
+    op("v", ["gr1"], ["qg1"], lambda e: e.quantize_mx(T.qg[:, H[1]], T.sg[:, H[1]], T.grt[:, 512:1024]))
+    op("v", ["xx0"], ["qx0"], lambda e: e.quantize_mx(T.qx0[:], T.sx0[:], T.xx0[:]))
+    op("g", [], ["iot"], lambda e: e.iota(T.iot[:], [[1, 256]], 0, 0, allow_small_or_imprecise_dtypes=True))
+    op("g", ["ones"], ["zd"], lambda e: e.affine_select(T.zd[:, 0:516], T.ones[:, 0:516], [[-1, 516]], OP.is_equal, 0.0, 3, 4))
+    op("g", [], ["kr"], lambda e: e.iota(T.kr[:], [[0, 4], [1, 16]], 0, 0, allow_small_or_imprecise_dtypes=True))
+
     for h, P in ((0, "PC"), (1, "PS")):
         op("t", ["qu", "qg%d" % h], ["PE%d" % h], lambda e: e.matmul_mx(T.PE[:, 512 * h:512 * h + 128], T.qu[:], T.su[:], T.qg[:, H[h]], T.sg[:, H[h]], True, True))
         op("t", ["qu", "qg%d" % h], [P], lambda e: e.matmul_mx(T[P][:, 0:128], T.qg[:, H[h]], T.sg[:, H[h]], T.qu[:], T.su[:], True, True))
@@ -180,6 +182,7 @@ def rank_program(g, core, T, topo):
     for h in range(2):
         op("v", ["sr0%d" % (1 - h), "sc0%d" % h], ["c%da" % h], lambda e: e.tensor_scalar(
             T["c%d" % h][:, H[1 - h]], T.sr0[:, H[1 - h]], T.sc0[:, h:h + 1], None, OP.is_ge if h else OP.is_gt))
+    for h in range(2):
         op("v", ["d%d" % h, "ld0"], ["c%db" % h], lambda e: e.tensor_tensor(T["c%d" % h][:, H[h]], T["d%d" % h][:], T.ld0[:], OP.is_gt))
     op("a", ["c0a", "c0b"], ["rk00", "c2"], lambda e: e.activation(T.c2[:], T.c0[:], AF.Copy, accum_out=T.rk0[:, 0:1]))
     op("v", ["c1a", "c1b"], ["rk01"], lambda e: e.tensor_reduce(T.rk0[:, 1:2], T.c1[:], X, OP.add))
@@ -189,13 +192,15 @@ def rank_program(g, core, T, topo):
         op("v", ["ht0%d" % h], ["qh0%d" % h], lambda e: e.quantize_mx(T.qh0[:, H[h]], T.sh0[:, H[h]], T.ht0[:, 512 * h:512 * h + 512]))
     for i, (h, c) in enumerate(((0, 0), (0, 16), (1, 8), (1, 16))):
         op("t", ["qh0%d" % h, "qx0"], ["PL"], lambda e: e.matmul_mx(T.PL[:, 0:128], T.qh0[:, H[h]], T.sh0[:, H[h]], T.qx0[:, c:c + 128], T.sx0[:, c:c + 128], i == 0, i == 3))
+    op("v", [], ["zer"], lambda e: e.memset(T.zer[:], 0.0))
+    op("v", ["zer"], ["x0p", "x0o"], lambda e: e.quantize_mx(T.x0[:, 0:128], T.s0[:, 0:128], T.zer[:]))
     op("v", ["PL"], ["lst0"], lambda e: e.tensor_copy(T.lst0[:, 0:4], T.PL[:, 0:4]))
 
     def pick(src, ssrc, lo, hi, lst, b):
         toks = ["qg0", "qg1"] if b == 0 else ["x%do" % (b - 1), "s%do" % (b - 1), "x%dl" % (b - 1), "x%dm" % (b - 1)]
         op("v", toks + [lst], ["x%do" % b], lambda e: e.tensor_copy(
             T["x%d" % b][:, 64:128].bitcast(dt.uint32), T[src][:, lo:hi].bitcast(dt.uint32).indirect(T[lst][:, 0:4])))
-        op("a", toks + [lst, "x%dp" % b], ["s%do" % b], lambda e: e.activation(
+        op("a", toks + [lst] + (["x%dp" % b] if b < 3 else []), ["s%do" % b], lambda e: e.activation(
             T["s%d" % b][:, 64:128], T[ssrc][:, lo:hi].indirect(T[lst][:, 0:4]), AF.Copy))
 
     ha, hb = helpers(rank)
@@ -208,11 +213,6 @@ def rank_program(g, core, T, topo):
     ready("g", ["s0o"])
     send(T.hs[:], T.s0[:, 64:128], hb, "hs", away)
 
-    op("g", [], ["iot"], lambda e: e.iota(T.iot[:], [[1, 256]], 0, 0, allow_small_or_imprecise_dtypes=True))
-    op("g", ["ones"], ["zd"], lambda e: e.affine_select(T.zd[:, 0:516], T.ones[:, 0:516], [[-1, 516]], OP.is_equal, 0.0, 3, 4))
-    op("g", [], ["kr"], lambda e: e.iota(T.kr[:], [[0, 16], [1, 4]], 0, 0, allow_small_or_imprecise_dtypes=True))
-    op("g", ["ones"], ["idt"], lambda e: e.affine_select(T.idt[:], T.ones[:, 0:128], [[-1, 128]], OP.is_equal, 0.0, 0, 1))
-
     def own_tables(b, aw, awt):
         op("v", [], ["t1"], lambda e: e.memset(T.m_t1[:], 64.0))
         op("v", [], ["t4"], lambda e: e.memset(T.m_t4[:], BIG))
@@ -220,30 +220,30 @@ def rank_program(g, core, T, topo):
         op("a", ["iot", awt], ["nra"], lambda e: e.activation(T.m_nr[:, 0:64], T.iot[:].indirect(aw), AF.Copy))
         op("v", ["t1"], ["t2"], lambda e: e.tensor_scalar(T.m_t2[:], T.m_t1[:], 63.5, None, OP.is_lt))
         op("v", ["t1"], ["t3"], lambda e: e.tensor_scalar(T.m_t3[:], T.m_t1[:], 63.5, BIG, OP.is_gt, OP.mult))
-        op("v", ["nra", "idt"], ["dga"], lambda e: e.tensor_tensor(T.m_dga[:], T.m_nr[:, 0:64], T.idt[:, 0:64], OP.mult))
-        op("v", ["dga"], ["na"], lambda e: e.tensor_reduce(T.m_na[:, 0:1], T.m_dga[:], X, OP.add))
+        op("g", ["nra"], ["dxa"], lambda e: e.affine_select(T.m_dx[:, 0:64], T.m_nr[:, 0:64], [[-1, 64]], OP.is_equal, 0.0, 0, 1))
         for t in range(4):
             op("t", ["qe", "x%dp" % b, "x%do" % b, "s%do" % b], ["PE%d" % t], lambda e: e.matmul_mx(
                 T.PE[:, 512 * t:512 * t + 128], T.qe[:, 128 * t:128 * t + 128], T.se[:, 128 * t:128 * t + 128], T["x%d" % b][:, 0:128], T["s%d" % b][:, 0:128], True, True))
-            op("a", ["PE%d" % t], ["da"], lambda e: e.activation(T.m_da[:, t:256:4], T.PE[:, 512 * t + 64:512 * t + 128], AF.Copy))
+            op("a", ["PE%d" % t, "daz"], ["da%d" % t], lambda e: e.activation(T.m_da[:, 80 * t:80 * t + 64], T.PE[:, 512 * t + 64:512 * t + 128], AF.Copy))
 
     for t in range(4):
         op("v", ["zd"], ["qe"], lambda e: e.quantize_mx(T.qe[:, 128 * t:128 * t + 128], T.se[:, 128 * t:128 * t + 128], T.zd[:, 3 - t:515 - t]))
-    op("v", [], ["da"], lambda e: e.memset(T.m_da[:, 256:272], 0.0))
+    op("v", [], ["daz"], lambda e: e.memset(T.m_da[:], 0.0))
     own_tables(0, T.lst0[:, 0:4], "lst0")
-    op("v", ["pi"], ["pr3"], lambda e: e.tensor_scalar(T.pi[:, 1:2], T.pi[:, 0:1], 3, None, OP.bitwise_and))
-    op("v", ["pi"], ["pq"], lambda e: e.tensor_scalar(T.pi[:, 2:3], T.pi[:, 0:1], 2, 3, OP.logical_shift_right, OP.bitwise_and))
-    op("v", ["pf"], ["isa"], lambda e: e.tensor_scalar(isa, pf, 63.5, 1000.0, OP.is_lt, OP.mult))
-    op("v", ["pf"], ["isb"], lambda e: e.tensor_scalar(isb, pf, 63.5, 128.0, OP.is_gt, OP.mult))
-    op("v", ["pr3"], ["pm4"], lambda e: e.tensor_copy(pm4, T.pi[:, 1:2]))
-    op("v", ["pq"], ["q4"], lambda e: e.tensor_copy(q4, T.pi[:, 2:3]))
-    op("v", ["kr"], ["rst4"], lambda e: e.tensor_scalar(T.rst4[:], T.kr[:], 0.5, None, OP.is_gt))
-    op("v", ["kr", "q4"], ["mask4"], lambda e: e.tensor_scalar(T.mask4[:], T.kr[:], q4, None, OP.is_equal))
+    op("v", ["pi"], ["pi15"], lambda e: e.tensor_scalar(T.pi[:, 1:2], T.pi[:, 0:1], 15, None, OP.bitwise_and))
+    op("v", ["kr"], ["rst"], lambda e: e.tensor_scalar(T.rst[:], T.kr[:], 0.5, None, OP.is_gt))
+    op("v", ["pf"], ["isb1"], lambda e: e.tensor_scalar(isb1, pf, 63.5, None, OP.is_gt))
+    op("v", ["pf"], ["isa1"], lambda e: e.tensor_scalar(isa1, pf, 63.5, None, OP.is_lt))
+    op("v", [], ["k1000"], lambda e: e.memset(k1000, 1000.0))
+    op("v", ["pi15"], ["pm"], lambda e: e.tensor_copy(pm, T.pi[:, 1:2]))
     op("v", [], ["neg1"], lambda e: e.memset(T.neg1[:], -1.0))
-    op("v", [], ["xxz"], lambda e: e.memset(T.xx[:], 0.0))
     op("v", [], ["mtz"], lambda e: e.memset(T.m_mt[:, 0:256], 0.0))
+    op("v", [], ["xxz"], lambda e: e.memset(T.xx[:], 0.0))
+    op("v", ["kr", "pm"], ["mask"], lambda e: e.tensor_scalar(T.mask[:], T.kr[:], pm, None, OP.is_equal))
+    op("v", ["isb1", "ones"], ["isb"], lambda e: e.tensor_scalar(T.isb[:], T.ones[:, 0:4], isb1, 128.0, OP.mult, OP.mult))
     op("v", ["plo", "xxz"], ["xxz"], lambda e: e.tensor_copy(T.xx[:, 48:64:5], T.plo[:]))
-    for b in range(1, 4):
+    op("v", ["isb", "phi"], ["phm"], lambda e: e.tensor_tensor(phm, T.phi[:, 0:1], T.isb[:, 0:1], OP.subtract))
+    for b in range(1, 3):
         op("v", ["zer"], ["x%dp" % b, "x%do" % b, "s%do" % b], lambda e: e.quantize_mx(T["x%d" % b][:, 0:128], T["s%d" % b][:, 0:128], T.zer[:]))
 
     def idle_work():
@@ -267,30 +267,17 @@ def rank_program(g, core, T, topo):
             op("v", ["bj"], ["bu"], lambda e: e.tensor_copy(T.bu[:], T.bj[:, 0:4]))
         bwt = "bl%d" % b if b < 2 else "bu"
         bw = T[bwt][:]
-        op("v", ["iot", bwt, "idt"], ["dg"], lambda e: e.tensor_tensor(T.m_dg[:], T.iot[:].indirect(bw), T.idt[:, 64:128], OP.mult))
+        op("v", ["t1", bwt, "mask"], ["g4"], lambda e: e.tensor_tensor(T.m_g4[:], T.m_t1[:].indirect(bw), T.mask[:], OP.mult))
+        op("v", ["g4", "rst"], ["g5"], lambda e: e.tensor_tensor_scan(T.m_g5[:], T.rst[:], T.m_g4[:], 0.0, OP.mult, OP.add))
+        op("v", ["g5"], ["toff"], lambda e: e.tensor_copy(T.m_toff[:], T.m_g5[:, 15:64:16]))
+        op("v", ["t4", "neg1", bwt], ["t4"], lambda e: e.tensor_copy(T.m_t4[:].indirect(bw), T.neg1[:]))
         op("a", ["iot", bwt], ["nrb"], lambda e: e.activation(T.m_nr[:, 64:128], T.iot[:].indirect(bw), AF.Copy))
-        op("v", ["t1", bwt, "mask4"], ["g4"], lambda e: e.tensor_tensor(T.m_g4[:], T.m_t1[:].indirect(bw), T.mask4[:], OP.mult))
         op("a", ["t2", bwt], ["mb"], lambda e: e.activation(T.m_mb[:], T.m_t2[:].indirect(bw), AF.Copy))
-        op("v", ["dg"], ["nb2"], lambda e: e.tensor_reduce(T.m_nb2[:, 0:1], T.m_dg[:], X, OP.add))
-        op("v", ["g4", "rst4"], ["g5"], lambda e: e.tensor_tensor_scan(T.m_g5[:], T.rst4[:], T.m_g4[:], 0.0, OP.mult, OP.add))
-        op("v", ["na", "nb2"], ["nc"], lambda e: e.tensor_tensor(T.m_nc[:, 0:1], T.m_na[:, 0:1], T.m_nb2[:, 0:1], OP.add))
-        op("v", ["g5", "pm4"], ["toff"], lambda e: e.tensor_scalar(T.m_toff[:], T.m_g5[:, 3:64:4], 4.0, pm4, OP.mult, OP.add))
-        op("a", ["nra", "nrb", "nc"], ["eq"], lambda e: e.activation(T.m_eq[:], T.m_nr[:], AF.Abs, bias=T.m_nc[:, 0:1], scale=-1.0))
+        op("g", ["nrb"], ["dxb"], lambda e: e.affine_select(T.m_dx[:, 64:128], T.m_nr[:, 64:128], [[-1, 64]], OP.is_equal, 0.0, -64, 1))
+        op("a", ["dxa", "dxb"], ["nc", "dy"], lambda e: e.activation(T.m_dy[:], T.m_dx[:], AF.Copy, accum_out=T.m_nc[:, 0:1]))
+        op("a", ["nra", "nrb", "nc"], ["eq"], lambda e: e.activation(T.m_eq[:], T.m_nr[:, 0:128], AF.Abs, bias=T.m_nc[:, 0:1], scale=-1.0))
         op("a", ["eq"], ["cnt", "eq2"], lambda e: e.activation(T.m_eq2[:], T.m_eq[:], AF.Relu, bias=1.0, scale=-1.0, accum_out=T.m_cnt[:, 0:1]))
         op("a", ["cnt"], ["notm"], lambda e: e.activation(T.m_notm[:, 0:1], T.m_cnt[:, 0:1], AF.Copy, bias=2.0, scale=-1.0))
-        op("v", ["t4", "neg1", bwt], ["t4"], lambda e: e.tensor_copy(T.m_t4[:].indirect(bw), T.neg1[:]))
-        op("v", ["m4", "nc", "xxz"], ["xxn"], lambda e: e.tensor_scalar(T.xx[:, 16:32:5], T.m4[:], T.m_nc[:, 0:1], MAGIC, OP.add, OP.subtract))
-        op("v", ["cnt", "isa"], ["pen"], lambda e: e.tensor_scalar(T.m_pen[:, 0:1], T.m_cnt[:, 0:1], -1.0, isa, OP.add, OP.mult))
-        op("v", ["cnt", "isb"], ["hm"], lambda e: e.tensor_scalar(T.m_hm[:, 0:1], T.m_cnt[:, 0:1], -1.0, isb, OP.add, OP.mult))
-        op("v", ["xxn", "nc"], ["xxm"], lambda e: e.tensor_scalar(T.xx[:, 64:80:5], T.xx[:, 16:32:5], T.m_nc[:, 0:1], -1.0, OP.subtract, OP.mult))
-        op("v", ["pen", "nc"], ["ncx"], lambda e: e.tensor_tensor(T.m_ncx[:, 0:1], T.m_pen[:, 0:1], T.m_nc[:, 0:1], OP.add))
-        op("v", ["phi", "hm"], ["xx"], lambda e: e.tensor_scalar(T.xx[:, 0:16:5], T.phi[:], T.m_hm[:, 0:1], None, OP.add))
-        if b == 1:
-            for i in (0, 48):
-                op("v", ["xxn", "xxm"], ["xx"], lambda e: e.tensor_scalar(T.xx[:, i + 32:i + 38:5], T.xx[:, i + 16:i + 22:5], 1.0, None, OP.mult))
-                op("v", ["xxn", "xxm"], ["xx"], lambda e: e.tensor_scalar(T.xx[:, i + 34:i + 40:5], T.xx[:, i + 16:i + 22:5], 256.0, None, OP.mult))
-        op("v", ["nra", "nrb", "ncx"], ["ld"], lambda e: e.tensor_scalar(T.m_ld[:], T.m_nr[:], T.m_ncx[:, 0:1], -TINY, OP.is_lt, OP.mult))
-        op("v", ["xx", "xxm"], ["qx"], lambda e: e.quantize_mx(T["qx%d" % nx][:], T["sx%d" % nx][:], T.xx[:]))
 
         both = ["x%do" % b, "s%do" % b, "x%dl" % b]
         for t in range(4):
@@ -298,39 +285,73 @@ def rank_program(g, core, T, topo):
                 T.PE[:, 512 * t:512 * t + 128], T.qe[:, 128 * t:128 * t + 128], T.se[:, 128 * t:128 * t + 128], x[:, 64:192], s[:, 64:192], True, True))
         op("t", ["qu"] + both, ["PR"], lambda e: e.matmul_mx(T.PR[:, 0:128], T.qu[:], T.su[:], x[:, 64:192], s[:, 64:192], True, True))
         op("t", ["qu"] + both, ["PC"], lambda e: e.matmul_mx(T.PC[:, 0:128], x[:, 64:192], s[:, 64:192], T.qu[:], T.su[:], True, True))
-        for t in range(4):
-            op("v", ["PE%d" % t, "mb"], ["db"], lambda e: e.tensor_tensor(T.m_db[:, t:256:4], T.PE[:, 512 * t + 64:512 * t + 128], T.m_mb[:], OP.mult))
+
+        def side(which):
+            if which == "n":
+                op("v", ["m4", "nc", "xxz"], ["xxn"], lambda e: e.tensor_scalar(T.xx[:, 16:32:5], T.m4[:], T.m_nc[:, 0:1], MAGIC, OP.add, OP.subtract))
+            if which == "m":
+                op("v", ["xxn", "nc"], ["xxm"], lambda e: e.tensor_scalar(T.xx[:, 64:80:5], T.xx[:, 16:32:5], T.m_nc[:, 0:1], -1.0, OP.subtract, OP.mult))
+            if which == "l":
+                op("v", ["nra", "nrb", "nc"], ["ld"], lambda e: e.tensor_scalar(T.m_ld[:], T.m_nr[:, 0:128], T.m_nc[:, 0:1], -TINY, OP.is_lt, OP.mult))
+            if which == "q":
+                op("v", ["xxs", "xxm"] + (["xxp"] if b == 1 else []), ["qx"], lambda e: e.quantize_mx(T["qx%d" % nx][:], T["sx%d" % nx][:], T.xx[:]))
+
+        if b < 2:
+            side("n")
+            side("l")
+        for t in range(5):
+            if t < 4:
+                op("v", ["PE%d" % t, "mb"], ["db%d" % t], lambda e: e.tensor_tensor(T.m_db[:, 64 * t:64 * t + 64], T.PE[:, 512 * t + 64:512 * t + 128], T.m_mb[:], OP.mult))
+            if t > 0:
+                i = t - 1
+                op("v", ["da%d" % i, "toff", "db%d" % i], ["mt"], lambda e: e.tensor_tensor(
+                    T.m_mt[:, 256 + i:512:4], T.m_da[:, 80 * i:80 * i + 80].indirect(T.m_toff[:]), T.m_db[:, 64 * i:64 * i + 64], OP.add))
+        side("m" if b < 2 else "l")
         op("a", ["PR"], ["rw"], lambda e: e.activation(T.m_rw[:], T.PR[:, 0:128], AF.Abs))
         op("a", ["PC", "notm"], ["bc"], lambda e: e.activation(T.m_bc[:, 0:1], T.PC[:, 0:1], AF.Abs, scale=T.m_notm[:, 0:1]))
-        op("v", ["da", "toff", "db"], ["mt"], lambda e: e.tensor_tensor(T.m_mt[:, 256:512], T.m_da[:, 0:260].indirect(T.m_toff[:]), T.m_db[:], OP.add))
+        op("a", ["cnt", "isb", "phm", "xxz"], ["xxs"], lambda e: e.activation(T.xx[:, 0:16:5], T.isb[:], AF.Identity, bias=phm, scale=T.m_cnt[:, 0:1]))
+        op("a", ["notm", "isa1", "isb1"], ["ok"], lambda e: e.activation(T.m_ok[:, 0:1], T.m_notm[:, 0:1], AF.Identity, bias=isb1, scale=isa1))
+        if b == 1:
+            for i in (0, 48):
+                op("a", ["xxn", "xxm"], ["xxp"], lambda e: e.activation(T.xx[:, i + 32:i + 38:5], T.xx[:, i + 16:i + 22:5], AF.Copy))
+                op("a", ["xxn", "xxm"], ["xxp"], lambda e: e.activation(T.xx[:, i + 34:i + 40:5], T.xx[:, i + 16:i + 22:5], AF.Copy, scale=256.0))
+        if b == 2:
+            op("a", ["ok", "k1000"], ["nct"], lambda e: e.activation(T.m_ncx[:, 0:1], T.m_ok[:, 0:1], AF.Identity, bias=k1000, scale=-1000.0))
+            op("a", ["nct", "nc"], ["ncx"], lambda e: e.activation(T.m_ncx[:, 1:2], T.m_ncx[:, 0:1], AF.Identity, bias=T.m_nc[:, 0:1]))
+            op("a", ["nra", "nrb"], ["nrc"], lambda e: e.activation(T.m_nr[:, 128:256], T.m_nr[:, 0:128], AF.Copy))
         op("v", ["mt", "mtz"], ["x%dm" % b], lambda e: e.quantize_mx(x[:, 192:320], s[:, 192:320], T.m_mt[:]))
-        op("t", ["qu", "x%dm" % b], ["PR"], lambda e: e.matmul_mx(T.PR[:, 0:128], T.qu[:], T.su[:], x[:, 192:320], s[:, 192:320], True, True))
+        op("t", ["qu", "x%dm" % b], ["PS"], lambda e: e.matmul_mx(T.PS[:, 0:128], T.qu[:], T.su[:], x[:, 192:320], s[:, 192:320], True, True))
         op("t", ["qu", "x%dm" % b], ["PC"], lambda e: e.matmul_mx(T.PC[:, 0:128], x[:, 192:320], s[:, 192:320], T.qu[:], T.su[:], True, True))
-        op("v", ["t4", "rw", awt], ["sra"], lambda e: e.tensor_tensor(T.m_sr[:, 0:64], T.m_t4[:].indirect(aw), T.m_rw[:, 0:64], OP.min))
         op("v", ["t3", "rw", bwt], ["srb"], lambda e: e.tensor_tensor(T.m_sr[:, 64:128], T.m_t3[:].indirect(bw), T.m_rw[:, 64:128], OP.min))
-        op("a", ["PR"], ["rm"], lambda e: e.activation(T.m_rm[:], T.PR[:, 64:128], AF.Abs))
+        op("v", ["t4", "rw", awt], ["sra"], lambda e: e.tensor_tensor(T.m_sr[:, 0:64], T.m_t4[:].indirect(aw), T.m_rw[:, 0:64], OP.min))
+        op("a", ["PS"], ["rm"], lambda e: e.activation(T.m_rm[:], T.PS[:, 64:128], AF.Abs))
         op("a", ["PC", "bc"], ["sc"], lambda e: e.activation(T.m_sc[:, 0:1], T.PC[:, 0:1], AF.Abs, bias=T.m_bc[:, 0:1]))
+        if b < 2:
+            side("q")
+        else:
+            op("v", ["nra", "nrb", "ncx"], ["gt"], lambda e: e.tensor_scalar(T.m_gt[:], T.m_nr[:, 0:128], T.m_ncx[:, 1:2], 1000.0, OP.is_le, OP.mult))
         op("v", ["srb", "rm"], ["srb"], lambda e: e.tensor_tensor(T.m_sr[:, 64:128], T.m_sr[:, 64:128], T.m_rm[:], OP.add))
         op("v", ["sra", "srb", "sc"], ["dd"], lambda e: e.tensor_scalar(T.m_dd[:], T.m_sr[:], T.m_sc[:, 0:1], None, OP.subtract))
         op("v", ["dd", "ld"], ["cc"], lambda e: e.tensor_tensor(T.m_cc[:], T.m_dd[:], T.m_ld[:], OP.is_gt))
         op("v", ["cc"], ["rk"], lambda e: e.tensor_reduce(T.m_rk[:, 0:1], T.m_cc[:], X, OP.add))
         if b < 2:
-            op("v", ["hp", "rk"], ["ht"], lambda e: e.tensor_scalar(T.m_ht[:], T.hp[:], T.m_rk[:, 0:1], None, OP.is_equal))
+            op("v", ["hp", "rk", "ok"], ["ht"], lambda e: e.tensor_scalar(T.m_ht[:], T.hp[:], T.m_rk[:, 0:1], T.m_ok[:, 0:1], OP.is_equal, OP.mult))
         else:
             for i, (lo, tok) in enumerate(((64, "x2l"), (192, "x2m"))):
                 op("t", ["qw", "x2o", "s2o", tok], ["PE%d" % i], lambda e: e.matmul_mx(T.PE[:, 512 * i:512 * i + 128], T.qw[:], T.sw[:], x[:, lo:lo + 128], s[:, lo:lo + 128], True, True))
                 op("a", ["PE%d" % i], ["yt%d" % i], lambda e: e.activation(T.ytab[:, 128 * i:128 * i + 128], T.PE[:, 512 * i:512 * i + 128], AF.Copy))
-            op("v", ["rk"], ["sel"], lambda e: e.tensor_scalar(T.m_sel[:, 0:1], T.m_rk[:, 0:1], 63.5, None, OP.is_lt))
-            op("v", ["nra", "nrb", "nc", "sel", "ptz"], ["pt"], lambda e: e.tensor_scalar(T.pt[:, 0:512:4], T.m_nr[:], T.m_nc[:, 0:1], T.m_sel[:, 0:1], OP.is_gt, OP.mult))
+            op("v", ["gt", "rk", "ptz"], ["pt"], lambda e: e.tensor_scalar(T.pt[:, 0:512:4], T.m_gt[:], T.m_rk[:, 0:1], 63.5, OP.add, OP.is_lt))
+            op("v", ["rk", "ok"], ["sel"], lambda e: e.tensor_scalar(T.m_sel[:, 0:1], T.m_rk[:, 0:1], 63.5, T.m_ok[:, 0:1], OP.is_lt, OP.mult))
             op("v", ["pt"], ["qp"], lambda e: e.quantize_mx(T.qp[:], T.sp[:], T.pt[:]))
             op("t", ["qp", "qn"], ["PC"], lambda e: e.matmul_mx(T.PC[:, 0:128], T.qp[:], T.sp[:], T.qn[:], T.sn[:], True, True))
+            side("q")
             op("v", ["hp", "PC", "sel"], ["ht"], lambda e: e.tensor_scalar(T.m_ht[:], T.hp[:], T.PC[:, 0:1], T.m_sel[:, 0:1], OP.is_equal, OP.mult))
         op("v", ["ht"], ["qh"], lambda e: e.quantize_mx(T["qh%d" % nx][:], T["sh%d" % nx][:], T.m_ht[:]))
         for c in (0, 12):
             op("t", ["qh", "qx"], ["PL"], lambda e: e.matmul_mx(
                 T.PL[:, 0:128], T["qh%d" % nx][:], T["sh%d" % nx][:], T["qx%d" % nx][:, c:c + 128], T["sx%d" % nx][:, c:c + 128], c == 0, c == 12))
         lst = "lst%d" % nx
-        m = 10 if b == 1 else 8
+        m = (8, 10, 4)[b]
         op("v", ["PL"], [lst], lambda e: e.tensor_copy(T[lst][:, 0:m], T.PL[:, 0:m]))
         if b < 2:
             to = T.cores[rank ^ (1 << nx)]
@@ -348,7 +369,7 @@ def rank_program(g, core, T, topo):
     pick("x2", "s2", 64, 320, "lst3", 3)
     dma("s", ["x3o"], [], "st0", T.oc[:], bits(T.x3[:, 64:128]))
     op("v", ["yt0", "yt1", "lst3"], ["ys"], lambda e: e.tensor_copy(T.ys[:], T.ytab[:].indirect(T.lst3[:, 0:4])))
-    op("v", ["iot", "lst3"], ["nbs"], lambda e: e.tensor_copy(T.nbs[:], T.iot[:].indirect(T.lst3[:, 4:8])))
+    op("v", ["nra", "nrb", "nrc", "lst3"], ["nbs"], lambda e: e.tensor_copy(T.nbs[:], T.m_nr[:].indirect(T.lst3[:, 0:4])))
     dma("a", ["s3o"], [], "st1", T.osc[0:4, :], T.s3[0:4, 64:128])
     dma("s", ["ys"], [], "st6", T.y[:], T.ys[:])
     dma("a", ["s3o"], [], "st2", T.osc[4:8, :], T.s3[32:36, 64:128])

@@ -8,22 +8,20 @@ F32, B16, I32, U16, U8, MX = "float32", "bfloat16", "int32", "uint16", "uint8", 
 SCRATCH = {}
 for _d, _names in (
         (B16, "ut 16|grt 1024|wt 512|ones 520|zer 512|ur 512|zd 520|iot 256|hp 512|ld0 128|ldz 128|kr 64|neg1 64|xx0 576|xx 560"
-              "|pt 512|c0 256|c1 256|c2 256|ht0 1024|m_t1 256|m_t2 256|m_t3 256|m_t4 256|m_nr 256|m_dx 128|m_dy 128|m_gt 128|m_da 320|m_db 256"
-              "|m_mt 512|m_ld 128|m_ht 512"),
-        (F32, "cst 8|mask 64|rst 64|m4 4|phi 4|plo 4|isb 4|sr0 256|sc0 8|nsc0 8|d0 128|d1 128|rk0 8|nbs 64|ys 64|ytab 256"
-              "|m_nc 8|m_ncx 8|m_cnt 8|m_notm 8|m_ok 8|m_eq 128|m_eq2 128|m_g4 64|m_g5 64|m_mb 64|m_rw 128|m_sr 128"
-              "|m_rm 64|m_bc 8|m_sc 8|m_dd 128|m_cc 128|m_rk 8|m_sel 8"),
+              "|pt 512|c0 256|c1 256|c2 256|c3 128|ht0 1024|t10 256|t11 256|t12 256|t40 256|t41 256|t42 256|m_nr 128|m_dx 128|m_dy 128"
+              "|m_gt 128|m_da 320|m_pa 256|m_mt 512|m_ld 128|m_ht 512"),
+        (F32, "cst 8|mask 64|rst 64|m4 4|phi 4|plo 4|jc 4|sr0 256|sc0 8|d0 128|d1 128|rk0 8|nbs 64|ys 64|ytab 128"
+              "|m_nc 8|m_s 8|m_eq 128|m_eq2 128|m_g4 64|m_g5 64|m_fa 4|m_fb 4|m_rw 64|m_sr 128|m_dd 128|m_cc 128"),
         (I32, "pi 8|bi 8|bj 8"),
-        (U16, "hl 4|lst0 8|lst1 8|lst2 12|lst3 8|bl0 4|bl1 4|bl2 2|bu 4|m_toff 4")):
+        (U16, "hl 4|lst0 8|lst1 8|lst2 12|lst3 8|bl0 4|bl1 4|bl2 2|bu 4|m_toff 4|m_fl 4")):
     for _n in _names.split("|"):
         SCRATCH[_n.split()[0]] = ("sbuf", [128, int(_n.split()[1])], _d)
-for _n, _w in (("u", 128), ("e", 512), ("g", 256), ("w", 128), ("n", 128), ("x0", 144), ("x1", 140), ("x2", 140), ("x3", 140), ("p", 128),
-               ("h0", 256), ("h1", 128), ("h2", 128), ("h3", 128)):
+for _n, _w in (("u", 128), ("e", 512), ("g", 256), ("w", 128), ("n", 128), ("x0", 144), ("x", 140), ("p", 128), ("h0", 256), ("h", 128)):
     SCRATCH["q" + _n] = ("sbuf", [128, _w], MX)
     SCRATCH["s" + _n] = ("sbuf", [128, _w], U8)
-for _b in range(4):
-    SCRATCH["x%d" % _b] = ("sbuf", [128, 320 if _b < 3 else 128], MX)
-    SCRATCH["s%d" % _b] = ("sbuf", [128, 320 if _b < 3 else 128], U8)
+for _n, _w in [("o%d" % _b, 64) for _b in range(3)] + [("p%d" % _b, 192) for _b in range(3)] + [("z%d" % _b, 128) for _b in range(3)] + [("y3", 64)]:
+    SCRATCH[_n] = ("sbuf", [128, _w], MX)
+    SCRATCH["s" + _n] = ("sbuf", [128, _w], U8)
 SCRATCH["hc"] = ("sbuf", [128, 64], MX)
 SCRATCH["hs"] = ("sbuf", [128, 64], U8)
 SCRATCH["PE"] = ("psum", [128, 2048], F32)
@@ -132,16 +130,18 @@ def rank_program(g, core, T, topo):
                 send(T.bl0[:], T.hl[:], far, "al0")
             if core == a:
                 g.wait_ge(T.sem.hc, n)
-                send(bits(T.x0[:, 128:192]), bits(T.hc[:]), far, "ac0")
+                send(bits(T.p0[:, 0:64]), bits(T.hc[:]), far, "ac0")
             if core == b:
                 g.wait_ge(T.sem.hs, n)
-                send(T.s0[:, 128:192], T.hs[:], far, "ac0")
+                send(T.sp0[:, 0:64], T.hs[:], far, "ac0")
             g.wait_ge(T.sem.sent, sent[0])
         return
 
     op, dma, arrives, ready, finish = make_flow(g, T)
     X = AxisListType.X
-    pf, pm, isb1, phm, isa1, k1000 = [T.cst[:, i:i + 1] for i in range(6)]
+    pf, pm, nisa, okb, k1000 = [T.cst[:, i:i + 1] for i in range(5)]
+    nct, ncx, cnt, okc, sc, rk, sel = [T.m_s[:, i:i + 1] for i in range(7)]
+    nc = T.m_nc[:, 0:1]
 
     dma("s", [], ["gr0"], "ld1", T.grt[:, 0:512], T.gr[:, 0:512])
     dma("a", [], ["ut"], "ld0", T.ut[:, 0:4], T.u[:, 0:4])
@@ -151,205 +151,221 @@ def rank_program(g, core, T, topo):
     op("g", [], ["pi"], lambda e: e.iota(T.pi[:, 0:1], [[0, 1]], 0, 1))
     op("g", [], ["hp"], lambda e: e.iota(T.hp[:], [[0, 8], [1, 16], [16, 4]], 0, 0, allow_small_or_imprecise_dtypes=True))
     op("v", [], ["m4"], lambda e: e.memset(T.m4[:], MAGIC))
-    op("v", [], ["ones"], lambda e: e.memset(T.ones[:], 1.0))
+    op("v", [], ["onesa"], lambda e: e.memset(T.ones[:, 0:128], 1.0))
+    op("v", [], ["onesb"], lambda e: e.memset(T.ones[:, 128:520], 1.0))
     op("v", ["pi"], ["pf"], lambda e: e.tensor_copy(pf, T.pi[:, 0:1]))
-    op("v", [], ["xx0z"], lambda e: e.memset(T.xx0[:], 0.0))
     op("v", ["m4", "pf"], ["phi"], lambda e: e.tensor_scalar(T.phi[:], T.m4[:], pf, MAGIC, OP.add, OP.subtract))
     op("v", [], ["ldz"], lambda e: e.memset(T.ldz[:], -TINY))
     op("g", ["ldz"], ["ld0"], lambda e: e.affine_select(T.ld0[:], T.ldz[:], [[-1, 128]], OP.is_gt, 0.0, 0, 1))
     op("v", ["phi", "pf"], ["plo"], lambda e: e.tensor_scalar(T.plo[:], T.phi[:], pf, -1.0, OP.subtract, OP.mult))
-    for i, src, add in ((0, "phi", 0.0), (32, "phi", 128.0), (64, "plo", 0.0)):
-        op("a", [src, "xx0z"], ["xx0"], lambda e: e.activation(T.xx0[:, i:i + 16:5], T[src][:], AF.Copy, bias=add))
     for t in range(4):
-        op("v", ["ones", "ut"], ["ur"], lambda e: e.tensor_scalar(T.ur[:, t:512:4], T.ones[:, 0:128], T.ut[:, t:t + 1], None, OP.mult))
+        op("v", ["onesa", "ut"], ["ur"], lambda e: e.tensor_scalar(T.ur[:, t:512:4], T.ones[:, 0:128], T.ut[:, t:t + 1], None, OP.mult))
     H = [slice(0, 128), slice(128, 256)]
     op("v", ["gr0"], ["qg0"], lambda e: e.quantize_mx(T.qg[:, H[0]], T.sg[:, H[0]], T.grt[:, 0:512]))
     op("v", ["ur"], ["qu"], lambda e: e.quantize_mx(T.qu[:], T.su[:], T.ur[:]))
     op("v", ["gr1"], ["qg1"], lambda e: e.quantize_mx(T.qg[:, H[1]], T.sg[:, H[1]], T.grt[:, 512:1024]))
-    op("v", ["xx0"], ["qx0"], lambda e: e.quantize_mx(T.qx0[:], T.sx0[:], T.xx0[:]))
+    op("v", [], ["xx0z"], lambda e: e.memset(T.xx0[:], 0.0))
     op("g", [], ["iot"], lambda e: e.iota(T.iot[:], [[1, 256]], 0, 0, allow_small_or_imprecise_dtypes=True))
-    op("g", ["ones"], ["zd"], lambda e: e.affine_select(T.zd[:, 0:516], T.ones[:, 0:516], [[-1, 516]], OP.is_equal, 0.0, 3, 4))
+    op("g", ["onesa", "onesb"], ["zd"], lambda e: e.affine_select(T.zd[:, 0:516], T.ones[:, 0:516], [[-1, 516]], OP.is_equal, 0.0, 3, 4))
     op("g", [], ["kr"], lambda e: e.iota(T.kr[:], [[0, 4], [1, 16]], 0, 0, allow_small_or_imprecise_dtypes=True))
+    op("g", [], ["t10"], lambda e: e.iota(T.t10[:], [[0, 256]], 64, 0, allow_small_or_imprecise_dtypes=True))
 
     for h, P in ((0, "PC"), (1, "PS")):
         op("t", ["qu", "qg%d" % h], ["PE%d" % h], lambda e: e.matmul_mx(T.PE[:, 512 * h:512 * h + 128], T.qu[:], T.su[:], T.qg[:, H[h]], T.sg[:, H[h]], True, True))
         op("t", ["qu", "qg%d" % h], [P], lambda e: e.matmul_mx(T[P][:, 0:128], T.qg[:, H[h]], T.sg[:, H[h]], T.qu[:], T.su[:], True, True))
         op("a", ["PE%d" % h], ["sr0%d" % h], lambda e: e.activation(T.sr0[:, H[h]], T.PE[:, 512 * h:512 * h + 128], AF.Abs))
-        op("v", [P], ["nsc%d" % h], lambda e: e.tensor_reduce(T.nsc0[:, h:h + 1], T[P][:, 0:1], X, OP.max, negate=True, apply_absolute_value=True))
+        op("v", [P], ["nsc%d" % h], lambda e: e.tensor_reduce(T.sc0[:, h + 2:h + 3], T[P][:, 0:1], X, OP.max, negate=True, apply_absolute_value=True))
         op("v", [P], ["sc0%d" % h], lambda e: e.tensor_reduce(T.sc0[:, h:h + 1], T[P][:, 0:1], X, OP.max, apply_absolute_value=True))
     for h in range(2):
-        op("a", ["sr0%d" % h, "nsc%d" % h], ["d%d" % h], lambda e: e.activation(T["d%d" % h][:], T.sr0[:, H[h]], AF.Identity, bias=T.nsc0[:, h:h + 1]))
+        op("a", ["sr0%d" % h, "nsc%d" % h], ["d%d" % h], lambda e: e.activation(T["d%d" % h][:], T.sr0[:, H[h]], AF.Identity, bias=T.sc0[:, h + 2:h + 3]))
+    for i, src, add in ((0, "phi", 0.0), (32, "phi", 128.0), (64, "plo", 0.0)):
+        op("a", [src, "xx0z"], ["xx0"], lambda e: e.activation(T.xx0[:, i:i + 16:5], T[src][:], AF.Copy, bias=add))
     for h in range(2):
         op("v", ["sr0%d" % (1 - h), "sc0%d" % h], ["c%da" % h], lambda e: e.tensor_scalar(
             T["c%d" % h][:, H[1 - h]], T.sr0[:, H[1 - h]], T.sc0[:, h:h + 1], None, OP.is_ge if h else OP.is_gt))
     for h in range(2):
         op("v", ["d%d" % h, "ld0"], ["c%db" % h], lambda e: e.tensor_tensor(T["c%d" % h][:, H[h]], T["d%d" % h][:], T.ld0[:], OP.is_gt))
+    op("a", ["c1a"], ["rk1a", "c3"], lambda e: e.activation(T.c3[:], T.c1[:, H[0]], AF.Copy, accum_out=T.rk0[:, 2:3]))
     op("a", ["c0a", "c0b"], ["rk00", "c2"], lambda e: e.activation(T.c2[:], T.c0[:], AF.Copy, accum_out=T.rk0[:, 0:1]))
-    op("v", ["c1a", "c1b"], ["rk01"], lambda e: e.tensor_reduce(T.rk0[:, 1:2], T.c1[:], X, OP.add))
-    for h in range(2):
-        op("v", ["hp", "rk0%d" % h], ["ht0%d" % h], lambda e: e.tensor_scalar(T.ht0[:, 512 * h:512 * h + 512], T.hp[:], T.rk0[:, h:h + 1], None, OP.is_equal))
-    for h in range(2):
+    op("v", ["c1b"], ["rk1b"], lambda e: e.tensor_reduce(T.rk0[:, 1:2], T.c1[:, H[1]], X, OP.add))
+    op("v", ["xx0"], ["qx0"], lambda e: e.quantize_mx(T.qx0[:], T.sx0[:], T.xx0[:]))
+    op("v", ["hp", "rk1a", "rk1b"], ["ht01"], lambda e: e.tensor_scalar(T.ht0[:, 512:1024], T.hp[:], T.rk0[:, 2:3], T.rk0[:, 1:2], OP.subtract, OP.is_equal))
+    op("v", ["hp", "rk00"], ["ht00"], lambda e: e.tensor_scalar(T.ht0[:, 0:512], T.hp[:], T.rk0[:, 0:1], None, OP.is_equal))
+    for h in (1, 0):
         op("v", ["ht0%d" % h], ["qh0%d" % h], lambda e: e.quantize_mx(T.qh0[:, H[h]], T.sh0[:, H[h]], T.ht0[:, 512 * h:512 * h + 512]))
-    for i, (h, c) in enumerate(((0, 0), (0, 16), (1, 8), (1, 16))):
+    for i, (h, c) in enumerate(((1, 8), (1, 16), (0, 0), (0, 16))):
         op("t", ["qh0%d" % h, "qx0"], ["PL"], lambda e: e.matmul_mx(T.PL[:, 0:128], T.qh0[:, H[h]], T.sh0[:, H[h]], T.qx0[:, c:c + 128], T.sx0[:, c:c + 128], i == 0, i == 3))
+
+    def zeros(b, which):
+        if which == "z":
+            op("v", ["zer"], ["z%d%s" % (b, k) for k in "osFf"], lambda e: e.quantize_mx(T["z%d" % b][:], T["sz%d" % b][:], T.zer[:]))
+        else:
+            op("v", ["zer"], ["p%dm" % b], lambda e: e.quantize_mx(T["p%d" % b][:, 64:192], T["sp%d" % b][:, 64:192], T.zer[:]))
+
     op("v", [], ["zer"], lambda e: e.memset(T.zer[:], 0.0))
-    op("v", ["zer"], ["x0p", "x0o"], lambda e: e.quantize_mx(T.x0[:, 0:128], T.s0[:, 0:128], T.zer[:]))
+    zeros(0, "z")
     op("v", ["PL"], ["lst0"], lambda e: e.tensor_copy(T.lst0[:, 0:4], T.PL[:, 0:4]))
 
-    def pick(src, ssrc, lo, hi, lst, b):
-        toks = ["qg0", "qg1"] if b == 0 else ["x%do" % (b - 1), "s%do" % (b - 1), "x%dl" % (b - 1), "x%dm" % (b - 1)]
-        op("v", toks + [lst], ["x%do" % b], lambda e: e.tensor_copy(
-            T["x%d" % b][:, 64:128].bitcast(dt.uint32), T[src][:, lo:hi].bitcast(dt.uint32).indirect(T[lst][:, 0:4])))
-        op("a", toks + [lst] + (["x%dp" % b] if b < 3 else []), ["s%do" % b], lambda e: e.activation(
-            T["s%d" % b][:, 64:128], T[ssrc][:, lo:hi].indirect(T[lst][:, 0:4]), AF.Copy))
+    def pick(b, into, toks):
+        src, ssrc, n, frm = ("qg", "sg", 256, ["qg0", "qg1"]) if b == 0 else ("z%d" % (b - 1), "sz%d" % (b - 1), 128, ["z%d%s" % (b - 1, k) for k in "osFf"])
+        lst = "lst%d" % b
+        op("v", frm + [lst], [toks[0]], lambda e: e.tensor_copy(
+            T[into][:, 0:64].bitcast(dt.uint32), T[src][:, 0:n].bitcast(dt.uint32).indirect(T[lst][:, 0:4])))
+        op("a", frm + [lst], [toks[1]], lambda e: e.activation(T["s" + into][:, 0:64], T[ssrc][:, 0:n].indirect(T[lst][:, 0:4]), AF.Copy))
 
     ha, hb = helpers(rank)
     away = T.cores[rank ^ 2]
     ready("g", ["lst0"])
     send(T.hl[:], T.lst0[:, 0:4], hb, "hl", away)
-    pick("qg", "sg", 0, 256, "lst0", 0)
-    ready("g", ["x0o"])
-    send(bits(T.hc[:]), bits(T.x0[:, 64:128]), ha, "hc", away)
-    ready("g", ["s0o"])
-    send(T.hs[:], T.s0[:, 64:128], hb, "hs", away)
+    pick(0, "o0", ("o0c", "o0s"))
+    ready("g", ["o0c"])
+    send(bits(T.hc[:]), bits(T.o0[:]), ha, "hc", away)
+    ready("g", ["o0s"])
+    send(T.hs[:], T.so0[:], hb, "hs", away)
+
+    def big(b):
+        op("g", ["iot"], ["t4%d" % b], lambda e: e.affine_select(T["t4%d" % b][:], T.iot[:], [[0, 256]], OP.is_gt, BIG, -1, 0))
 
     def own_tables(b, aw, awt):
-        op("v", [], ["t1"], lambda e: e.memset(T.m_t1[:], 64.0))
-        op("v", [], ["t4"], lambda e: e.memset(T.m_t4[:], BIG))
-        op("v", ["t1", "iot", awt], ["t1"], lambda e: e.tensor_copy(T.m_t1[:].indirect(aw), T.iot[:, 0:64]))
+        z, s, zt = T["z%d" % b], T["sz%d" % b], ["z%d%s" % (b, k) for k in "osFf"]
+        pick(b, "z%d" % b, zt[0:2])
+        op("v", ["iot", awt, "t1%d" % b], ["t1%d" % b], lambda e: e.tensor_copy(T["t1%d" % b][:].indirect(aw), T.iot[:, 0:64]))
         op("a", ["iot", awt], ["nra"], lambda e: e.activation(T.m_nr[:, 0:64], T.iot[:].indirect(aw), AF.Copy))
-        op("v", ["t1"], ["t2"], lambda e: e.tensor_scalar(T.m_t2[:], T.m_t1[:], 63.5, None, OP.is_lt))
-        op("v", ["t1"], ["t3"], lambda e: e.tensor_scalar(T.m_t3[:], T.m_t1[:], 63.5, BIG, OP.is_gt, OP.mult))
         op("g", ["nra"], ["dxa"], lambda e: e.affine_select(T.m_dx[:, 0:64], T.m_nr[:, 0:64], [[-1, 64]], OP.is_equal, 0.0, 0, 1))
+        if b == 0:
+            big(0)
         for t in range(4):
-            op("t", ["qe", "x%dp" % b, "x%do" % b, "s%do" % b], ["PE%d" % t], lambda e: e.matmul_mx(
-                T.PE[:, 512 * t:512 * t + 128], T.qe[:, 128 * t:128 * t + 128], T.se[:, 128 * t:128 * t + 128], T["x%d" % b][:, 0:128], T["s%d" % b][:, 0:128], True, True))
-            op("a", ["PE%d" % t, "daz"], ["da%d" % t], lambda e: e.activation(T.m_da[:, 80 * t:80 * t + 64], T.PE[:, 512 * t + 64:512 * t + 128], AF.Copy))
+            op("t", ["qe"] + zt, ["PE%d" % t], lambda e: e.matmul_mx(
+                T.PE[:, 512 * t:512 * t + 128], T.qe[:, 128 * t:128 * t + 128], T.se[:, 128 * t:128 * t + 128], z[:], s[:], True, True))
+            da, pe = T.m_da[:, 80 * t:80 * t + 64], T.PE[:, 512 * t:512 * t + 64]
+            if b > 0 and t < 2:
+                op("v", ["PE%d" % t, "daz"], ["da%d" % t], lambda e: e.tensor_copy(da, pe))
+            else:
+                op("a", ["PE%d" % t, "daz"], ["da%d" % t], lambda e: e.activation(da, pe, AF.Copy))
+        op("t", ["qu"] + zt, ["PR"], lambda e: e.matmul_mx(T.PR[:, 0:128], T.qu[:], T.su[:], z[:], s[:], True, True))
 
     for t in range(4):
         op("v", ["zd"], ["qe"], lambda e: e.quantize_mx(T.qe[:, 128 * t:128 * t + 128], T.se[:, 128 * t:128 * t + 128], T.zd[:, 3 - t:515 - t]))
-    op("v", [], ["daz"], lambda e: e.memset(T.m_da[:], 0.0))
+    op("v", [], ["daz"], lambda e: e.memset(T.m_da[:, 64:320:80], 0.0))
     own_tables(0, T.lst0[:, 0:4], "lst0")
+    zeros(0, "p")
     op("v", ["pi"], ["pi15"], lambda e: e.tensor_scalar(T.pi[:, 1:2], T.pi[:, 0:1], 15, None, OP.bitwise_and))
     op("v", ["kr"], ["rst"], lambda e: e.tensor_scalar(T.rst[:], T.kr[:], 0.5, None, OP.is_gt))
-    op("v", ["pf"], ["isb1"], lambda e: e.tensor_scalar(isb1, pf, 63.5, None, OP.is_gt))
-    op("v", ["pf"], ["isa1"], lambda e: e.tensor_scalar(isa1, pf, 63.5, None, OP.is_lt))
-    op("v", [], ["k1000"], lambda e: e.memset(k1000, 1000.0))
+    op("v", ["pf"], ["nisa"], lambda e: e.tensor_scalar(nisa, pf, 63.5, -1.0, OP.is_lt, OP.mult))
     op("v", ["pi15"], ["pm"], lambda e: e.tensor_copy(pm, T.pi[:, 1:2]))
+    op("v", ["pf"], ["okb"], lambda e: e.tensor_scalar(okb, pf, 63.5, 1.0, OP.is_lt, OP.add))
     op("v", [], ["neg1"], lambda e: e.memset(T.neg1[:], -1.0))
-    op("v", [], ["mtz"], lambda e: e.memset(T.m_mt[:, 0:256], 0.0))
-    op("v", [], ["xxz"], lambda e: e.memset(T.xx[:], 0.0))
     op("v", ["kr", "pm"], ["mask"], lambda e: e.tensor_scalar(T.mask[:], T.kr[:], pm, None, OP.is_equal))
-    op("v", ["isb1", "ones"], ["isb"], lambda e: e.tensor_scalar(T.isb[:], T.ones[:, 0:4], isb1, 128.0, OP.mult, OP.mult))
-    op("v", ["plo", "xxz"], ["xxz"], lambda e: e.tensor_copy(T.xx[:, 48:64:5], T.plo[:]))
-    op("v", ["isb", "phi"], ["phm"], lambda e: e.tensor_tensor(phm, T.phi[:, 0:1], T.isb[:, 0:1], OP.subtract))
-    for b in range(1, 3):
-        op("v", ["zer"], ["x%dp" % b, "x%do" % b, "s%do" % b], lambda e: e.quantize_mx(T["x%d" % b][:, 0:128], T["s%d" % b][:, 0:128], T.zer[:]))
-
-    def idle_work():
-        op("v", [], ["ptz"], lambda e: e.memset(T.pt[:], 0.0))
-        op("v", ["ones"], ["qn"], lambda e: e.quantize_mx(T.qn[:], T.sn[:], T.ones[:, 0:512]))
-        op("v", ["wt"], ["qw"], lambda e: e.quantize_mx(T.qw[:], T.sw[:], T.wt[:]))
+    op("v", ["hp", "pm"], ["jc"], lambda e: e.tensor_scalar(T.jc[:], T.hp[:, 0:4], pm, None, OP.add))
+    op("v", [], ["mtz"], lambda e: e.memset(T.m_mt[:, 256:512], 0.0))
+    op("v", [], ["xxz"], lambda e: e.memset(T.xx[:], 0.0))
+    op("v", [], ["k1000"], lambda e: e.memset(k1000, 1000.0))
+    zeros(1, "z")
+    op("v", ["plo", "xxz"], ["xxl"], lambda e: e.tensor_copy(T.xx[:, 48:64:5], T.plo[:]))
+    op("v", ["phi", "xxz"], ["xxh"], lambda e: e.tensor_copy(T.xx[:, 0:16:5], T.phi[:]))
+    zeros(1, "p")
 
     for b in range(3):
         nx = b + 1
-        x, s = T["x%d" % b], T["s%d" % b]
+        z, sz, p, sp = T["z%d" % b], T["sz%d" % b], T["p%d" % b], T["sp%d" % b]
+        zt = ["z%d%s" % (b, k) for k in "osFf"]
+        t1, t4 = "t1%d" % b, "t4%d" % b
         aw, awt = (T.lst0[:, 0:4], "lst0") if b == 0 else (T["lst%d" % b][:, 4:8], "lst%d" % b)
         src = helpers(rank ^ 1)[0] if b == 0 else T.cores[rank ^ (1 << b)]
         n = len(topo.engines(src, core))
         arrives("bl%d" % b, "al%d" % b, n)
-        arrives("x%dl" % b, "ac%d" % b, 2 * n)
+        arrives("p%dl" % b, "ac%d" % b, 2 * n)
 
         if b == 2:
             op("v", ["bl2"], ["bi"], lambda e: e.tensor_copy(T.bi[:, 0:2], T.bl2[:]))
-            op("v", ["bi"], ["bj"], lambda e: e.tensor_scalar(T.bj[:, 0:2], T.bi[:, 0:2], 255, None, OP.bitwise_and))
-            op("v", ["bi"], ["bj"], lambda e: e.tensor_scalar(T.bj[:, 2:4], T.bi[:, 0:2], 8, None, OP.logical_shift_right))
-            op("v", ["bj"], ["bu"], lambda e: e.tensor_copy(T.bu[:], T.bj[:, 0:4]))
+            op("v", ["bi"], ["bj0"], lambda e: e.tensor_scalar(T.bj[:, 0:2], T.bi[:, 0:2], 255, None, OP.bitwise_and))
+            op("v", ["bi"], ["bj1"], lambda e: e.tensor_scalar(T.bj[:, 2:4], T.bi[:, 0:2], 8, None, OP.logical_shift_right))
+            op("v", ["bj0", "bj1"], ["bu"], lambda e: e.tensor_copy(T.bu[:], T.bj[:, 0:4]))
         bwt = "bl%d" % b if b < 2 else "bu"
         bw = T[bwt][:]
-        op("v", ["t1", bwt, "mask"], ["g4"], lambda e: e.tensor_tensor(T.m_g4[:], T.m_t1[:].indirect(bw), T.mask[:], OP.mult))
+        op("v", [t1, bwt, "mask"], ["g4"], lambda e: e.tensor_tensor(T.m_g4[:], T[t1][:].indirect(bw), T.mask[:], OP.mult))
         op("v", ["g4", "rst"], ["g5"], lambda e: e.tensor_tensor_scan(T.m_g5[:], T.rst[:], T.m_g4[:], 0.0, OP.mult, OP.add))
         op("v", ["g5"], ["toff"], lambda e: e.tensor_copy(T.m_toff[:], T.m_g5[:, 15:64:16]))
-        op("v", ["t4", "neg1", bwt], ["t4"], lambda e: e.tensor_copy(T.m_t4[:].indirect(bw), T.neg1[:]))
+        op("v", ["g5"], ["fa"], lambda e: e.tensor_scalar(T.m_fa[:], T.m_g5[:, 15:64:16], 63.5, 64.0, OP.is_lt, OP.mult))
         op("a", ["iot", bwt], ["nrb"], lambda e: e.activation(T.m_nr[:, 64:128], T.iot[:].indirect(bw), AF.Copy))
-        op("a", ["t2", bwt], ["mb"], lambda e: e.activation(T.m_mb[:], T.m_t2[:].indirect(bw), AF.Copy))
         op("g", ["nrb"], ["dxb"], lambda e: e.affine_select(T.m_dx[:, 64:128], T.m_nr[:, 64:128], [[-1, 64]], OP.is_equal, 0.0, -64, 1))
-        op("a", ["dxa", "dxb"], ["nc", "dy"], lambda e: e.activation(T.m_dy[:], T.m_dx[:], AF.Copy, accum_out=T.m_nc[:, 0:1]))
-        op("a", ["nra", "nrb", "nc"], ["eq"], lambda e: e.activation(T.m_eq[:], T.m_nr[:, 0:128], AF.Abs, bias=T.m_nc[:, 0:1], scale=-1.0))
-        op("a", ["eq"], ["cnt", "eq2"], lambda e: e.activation(T.m_eq2[:], T.m_eq[:], AF.Relu, bias=1.0, scale=-1.0, accum_out=T.m_cnt[:, 0:1]))
-        op("a", ["cnt"], ["notm"], lambda e: e.activation(T.m_notm[:, 0:1], T.m_cnt[:, 0:1], AF.Copy, bias=2.0, scale=-1.0))
-
-        both = ["x%do" % b, "s%do" % b, "x%dl" % b]
-        for t in range(4):
-            op("t", ["qe"] + both, ["PE%d" % t], lambda e: e.matmul_mx(
-                T.PE[:, 512 * t:512 * t + 128], T.qe[:, 128 * t:128 * t + 128], T.se[:, 128 * t:128 * t + 128], x[:, 64:192], s[:, 64:192], True, True))
-        op("t", ["qu"] + both, ["PR"], lambda e: e.matmul_mx(T.PR[:, 0:128], T.qu[:], T.su[:], x[:, 64:192], s[:, 64:192], True, True))
-        op("t", ["qu"] + both, ["PC"], lambda e: e.matmul_mx(T.PC[:, 0:128], x[:, 64:192], s[:, 64:192], T.qu[:], T.su[:], True, True))
-
-        def side(which):
-            if which == "n":
-                op("v", ["m4", "nc", "xxz"], ["xxn"], lambda e: e.tensor_scalar(T.xx[:, 16:32:5], T.m4[:], T.m_nc[:, 0:1], MAGIC, OP.add, OP.subtract))
-            if which == "m":
-                op("v", ["xxn", "nc"], ["xxm"], lambda e: e.tensor_scalar(T.xx[:, 64:80:5], T.xx[:, 16:32:5], T.m_nc[:, 0:1], -1.0, OP.subtract, OP.mult))
-            if which == "l":
-                op("v", ["nra", "nrb", "nc"], ["ld"], lambda e: e.tensor_scalar(T.m_ld[:], T.m_nr[:, 0:128], T.m_nc[:, 0:1], -TINY, OP.is_lt, OP.mult))
-            if which == "q":
-                op("v", ["xxs", "xxm"] + (["xxp"] if b == 1 else []), ["qx"], lambda e: e.quantize_mx(T["qx%d" % nx][:], T["sx%d" % nx][:], T.xx[:]))
-
         if b < 2:
-            side("n")
-            side("l")
-        for t in range(5):
-            if t < 4:
-                op("v", ["PE%d" % t, "mb"], ["db%d" % t], lambda e: e.tensor_tensor(T.m_db[:, 64 * t:64 * t + 64], T.PE[:, 512 * t + 64:512 * t + 128], T.m_mb[:], OP.mult))
-            if t > 0:
-                i = t - 1
-                op("v", ["da%d" % i, "toff", "db%d" % i], ["mt"], lambda e: e.tensor_tensor(
-                    T.m_mt[:, 256 + i:512:4], T.m_da[:, 80 * i:80 * i + 80].indirect(T.m_toff[:]), T.m_db[:, 64 * i:64 * i + 64], OP.add))
-        side("m" if b < 2 else "l")
-        op("a", ["PR"], ["rw"], lambda e: e.activation(T.m_rw[:], T.PR[:, 0:128], AF.Abs))
-        op("a", ["PC", "notm"], ["bc"], lambda e: e.activation(T.m_bc[:, 0:1], T.PC[:, 0:1], AF.Abs, scale=T.m_notm[:, 0:1]))
-        op("a", ["cnt", "isb", "phm", "xxz"], ["xxs"], lambda e: e.activation(T.xx[:, 0:16:5], T.isb[:], AF.Identity, bias=phm, scale=T.m_cnt[:, 0:1]))
-        op("a", ["notm", "isa1", "isb1"], ["ok"], lambda e: e.activation(T.m_ok[:, 0:1], T.m_notm[:, 0:1], AF.Identity, bias=isb1, scale=isa1))
+            op("g", [], ["t1%d" % nx], lambda e: e.iota(T["t1%d" % nx][:], [[0, 256]], 64, 0, allow_small_or_imprecise_dtypes=True))
+            big(nx)
+        if b == 0:
+            op("g", [], ["ptz"], lambda e: e.iota(T.pt[:], [[0, 512]], 0, 0, allow_small_or_imprecise_dtypes=True))
+        for t in range(2):
+            op("v", ["da%d" % t, "toff"], ["pa%d" % t], lambda e: e.tensor_copy(T.m_pa[:, 64 * t:64 * t + 64], T.m_da[:, 80 * t:80 * t + 65].indirect(T.m_toff[:])))
+        for t in range(2, 4):
+            op("a", ["da%d" % t, "toff"], ["pa%d" % t], lambda e: e.activation(T.m_pa[:, 64 * t:64 * t + 64], T.m_da[:, 80 * t:80 * t + 65].indirect(T.m_toff[:]), AF.Copy))
+        op("v", ["fa", "jc"], ["fb"], lambda e: e.tensor_tensor(T.m_fb[:], T.m_fa[:], T.jc[:], OP.add))
+        op("a", ["dxa", "dxb"], ["nc", "dy"], lambda e: e.activation(T.m_dy[:], T.m_dx[:], AF.Copy, accum_out=nc))
+        op("a", ["PR"], ["rw"], lambda e: e.activation(T.m_rw[:], T.PR[:, 0:64], AF.Abs))
+
+        for t in range(4):
+            op("t", ["qe", "p%dm" % b, "p%dl" % b], ["PE%d" % t], lambda e: e.matmul_mx(
+                T.PE[:, 512 * t:512 * t + 128], T.qe[:, 128 * t:128 * t + 128], T.se[:, 128 * t:128 * t + 128], p[:, 0:128], sp[:, 0:128], True, True))
+        for t in range(4):
+            op("v", ["PE%d" % t, "pa%d" % t], ["mt%d" % t], lambda e: e.tensor_tensor(
+                T.m_mt[:, t:256:4], T.PE[:, 512 * t:512 * t + 64], T.m_pa[:, 64 * t:64 * t + 64], OP.add))
+            if t == 1:
+                op("v", ["fb"], ["fl"], lambda e: e.tensor_copy(T.m_fl[:], T.m_fb[:]))
+        op("v", ["mt0", "mt1", "mt2", "mt3", "mtz"], ["p%dm" % b], lambda e: e.quantize_mx(p[:, 64:192], sp[:, 64:192], T.m_mt[:]))
+        op("v", ["m4", "nc", "xxz"], ["xxn"], lambda e: e.tensor_scalar(T.xx[:, 16:32:5], T.m4[:], nc, MAGIC, OP.add, OP.subtract))
+        op("v", ["p%dl" % b, "p%dm" % b, "fl"], [zt[2]], lambda e: e.tensor_copy(
+            z[:, 64:128].bitcast(dt.uint32), p[:, 0:128].bitcast(dt.uint32).indirect(T.m_fl[:])))
+        op("a", ["p%dl" % b, "p%dm" % b, "fl"], [zt[3]], lambda e: e.activation(sz[:, 64:128], sp[:, 0:128].indirect(T.m_fl[:]), AF.Copy))
+        op("t", ["qu"] + zt, ["PC"], lambda e: e.matmul_mx(T.PC[:, 0:128], z[:], sz[:], T.qu[:], T.su[:], True, True))
+        op("t", ["qu"] + zt, ["PS"], lambda e: e.matmul_mx(T.PS[:, 0:128], T.qu[:], T.su[:], z[:], sz[:], True, True))
+        op("a", ["nra", "nrb", "nc"], ["eq"], lambda e: e.activation(T.m_eq[:], T.m_nr[:], AF.Abs, bias=nc, scale=-1.0))
+        op("v", ["xxn", "nc"], ["xxm"], lambda e: e.tensor_scalar(T.xx[:, 64:80:5], T.xx[:, 16:32:5], nc, -1.0, OP.subtract, OP.mult))
+        op("v", [t4, "neg1", bwt], [t4], lambda e: e.tensor_copy(T[t4][:].indirect(bw), T.neg1[:]))
+        op("v", ["nra", "nrb", "nc"], ["ld"], lambda e: e.tensor_scalar(T.m_ld[:], T.m_nr[:], nc, -TINY, OP.is_lt, OP.mult))
+        op("v", [t4, "rw", awt], ["sra"], lambda e: e.tensor_tensor(T.m_sr[:, 0:64], T[t4][:].indirect(aw), T.m_rw[:], OP.min))
         if b == 1:
             for i in (0, 48):
                 op("a", ["xxn", "xxm"], ["xxp"], lambda e: e.activation(T.xx[:, i + 32:i + 38:5], T.xx[:, i + 16:i + 22:5], AF.Copy))
                 op("a", ["xxn", "xxm"], ["xxp"], lambda e: e.activation(T.xx[:, i + 34:i + 40:5], T.xx[:, i + 16:i + 22:5], AF.Copy, scale=256.0))
+
+        def lists():
+            op("v", ["xxl", "xxh", "xxn", "xxm"] + (["xxp"] if b == 1 else []), ["qx"], lambda e: e.quantize_mx(T.qx[:], T.sx[:], T.xx[:]))
+
+        op("a", ["PS"], ["srb"], lambda e: e.activation(T.m_sr[:, 64:128], T.PS[:, 64:128], AF.Abs))
+        op("a", ["eq"], ["cnt", "eq2"], lambda e: e.activation(T.m_eq2[:], T.m_eq[:], AF.Relu, bias=1.0, scale=-1.0, accum_out=cnt))
+        op("a", ["cnt", "nisa", "okb"], ["ok"], lambda e: e.activation(okc, cnt, AF.Identity, bias=okb, scale=nisa))
         if b == 2:
-            op("a", ["ok", "k1000"], ["nct"], lambda e: e.activation(T.m_ncx[:, 0:1], T.m_ok[:, 0:1], AF.Identity, bias=k1000, scale=-1000.0))
-            op("a", ["nct", "nc"], ["ncx"], lambda e: e.activation(T.m_ncx[:, 1:2], T.m_ncx[:, 0:1], AF.Identity, bias=T.m_nc[:, 0:1]))
-            op("a", ["nra", "nrb"], ["nrc"], lambda e: e.activation(T.m_nr[:, 128:256], T.m_nr[:, 0:128], AF.Copy))
-        op("v", ["mt", "mtz"], ["x%dm" % b], lambda e: e.quantize_mx(x[:, 192:320], s[:, 192:320], T.m_mt[:]))
-        op("t", ["qu", "x%dm" % b], ["PS"], lambda e: e.matmul_mx(T.PS[:, 0:128], T.qu[:], T.su[:], x[:, 192:320], s[:, 192:320], True, True))
-        op("t", ["qu", "x%dm" % b], ["PC"], lambda e: e.matmul_mx(T.PC[:, 0:128], x[:, 192:320], s[:, 192:320], T.qu[:], T.su[:], True, True))
-        op("v", ["t3", "rw", bwt], ["srb"], lambda e: e.tensor_tensor(T.m_sr[:, 64:128], T.m_t3[:].indirect(bw), T.m_rw[:, 64:128], OP.min))
-        op("v", ["t4", "rw", awt], ["sra"], lambda e: e.tensor_tensor(T.m_sr[:, 0:64], T.m_t4[:].indirect(aw), T.m_rw[:, 0:64], OP.min))
-        op("a", ["PS"], ["rm"], lambda e: e.activation(T.m_rm[:], T.PS[:, 64:128], AF.Abs))
-        op("a", ["PC", "bc"], ["sc"], lambda e: e.activation(T.m_sc[:, 0:1], T.PC[:, 0:1], AF.Abs, bias=T.m_bc[:, 0:1]))
+            op("a", ["ok", "k1000"], ["nct"], lambda e: e.activation(nct, okc, AF.Identity, bias=k1000, scale=-1000.0))
+            op("a", ["nct", "nc"], ["ncx"], lambda e: e.activation(ncx, nct, AF.Identity, bias=nc))
+        op("v", ["PC"], ["sc"], lambda e: e.tensor_reduce(sc, T.PC[:, 0:1], X, OP.max, apply_absolute_value=True))
+        if b != 1:
+            lists()
+        op("v", ["sra", "sc"], ["dda"], lambda e: e.tensor_scalar(T.m_dd[:, 0:64], T.m_sr[:, 0:64], sc, None, OP.subtract))
+        op("v", ["srb", "sc"], ["ddb"], lambda e: e.tensor_scalar(T.m_dd[:, 64:128], T.m_sr[:, 64:128], sc, None, OP.subtract))
+        op("v", ["dda", "ld"], ["cca"], lambda e: e.tensor_tensor(T.m_cc[:, 0:64], T.m_dd[:, 0:64], T.m_ld[:, 0:64], OP.is_gt))
+        op("v", ["ddb", "ld"], ["ccb"], lambda e: e.tensor_tensor(T.m_cc[:, 64:128], T.m_dd[:, 64:128], T.m_ld[:, 64:128], OP.is_gt))
+        if b == 1:
+            lists()
+        op("v", ["cca", "ccb"], ["rk"], lambda e: e.tensor_reduce(rk, T.m_cc[:], X, OP.add))
         if b < 2:
-            side("q")
+            op("v", ["hp", "rk", "ok"], ["ht"], lambda e: e.tensor_scalar(T.m_ht[:], T.hp[:], rk, okc, OP.is_equal, OP.mult))
         else:
-            op("v", ["nra", "nrb", "ncx"], ["gt"], lambda e: e.tensor_scalar(T.m_gt[:], T.m_nr[:, 0:128], T.m_ncx[:, 1:2], 1000.0, OP.is_le, OP.mult))
-        op("v", ["srb", "rm"], ["srb"], lambda e: e.tensor_tensor(T.m_sr[:, 64:128], T.m_sr[:, 64:128], T.m_rm[:], OP.add))
-        op("v", ["sra", "srb", "sc"], ["dd"], lambda e: e.tensor_scalar(T.m_dd[:], T.m_sr[:], T.m_sc[:, 0:1], None, OP.subtract))
-        op("v", ["dd", "ld"], ["cc"], lambda e: e.tensor_tensor(T.m_cc[:], T.m_dd[:], T.m_ld[:], OP.is_gt))
-        op("v", ["cc"], ["rk"], lambda e: e.tensor_reduce(T.m_rk[:, 0:1], T.m_cc[:], X, OP.add))
-        if b < 2:
-            op("v", ["hp", "rk", "ok"], ["ht"], lambda e: e.tensor_scalar(T.m_ht[:], T.hp[:], T.m_rk[:, 0:1], T.m_ok[:, 0:1], OP.is_equal, OP.mult))
-        else:
-            for i, (lo, tok) in enumerate(((64, "x2l"), (192, "x2m"))):
-                op("t", ["qw", "x2o", "s2o", tok], ["PE%d" % i], lambda e: e.matmul_mx(T.PE[:, 512 * i:512 * i + 128], T.qw[:], T.sw[:], x[:, lo:lo + 128], s[:, lo:lo + 128], True, True))
-                op("a", ["PE%d" % i], ["yt%d" % i], lambda e: e.activation(T.ytab[:, 128 * i:128 * i + 128], T.PE[:, 512 * i:512 * i + 128], AF.Copy))
-            op("v", ["gt", "rk", "ptz"], ["pt"], lambda e: e.tensor_scalar(T.pt[:, 0:512:4], T.m_gt[:], T.m_rk[:, 0:1], 63.5, OP.add, OP.is_lt))
-            op("v", ["rk", "ok"], ["sel"], lambda e: e.tensor_scalar(T.m_sel[:, 0:1], T.m_rk[:, 0:1], 63.5, T.m_ok[:, 0:1], OP.is_lt, OP.mult))
+            op("t", ["qw"] + zt, ["PE0"], lambda e: e.matmul_mx(T.PE[:, 0:128], T.qw[:], T.sw[:], z[:], sz[:], True, True))
+            op("a", ["PE0"], ["yt"], lambda e: e.activation(T.ytab[:], T.PE[:, 0:128], AF.Copy))
+            op("v", ["nra", "nrb", "ncx"], ["gt"], lambda e: e.tensor_scalar(T.m_gt[:], T.m_nr[:], ncx, 1000.0, OP.is_le, OP.mult))
+            op("v", ["gt", "rk", "ptz"], ["pt"], lambda e: e.tensor_scalar(T.pt[:, 0:512:4], T.m_gt[:], rk, 63.5, OP.add, OP.is_lt))
+            op("v", ["rk", "ok"], ["sel"], lambda e: e.tensor_scalar(sel, rk, 63.5, okc, OP.is_lt, OP.mult))
             op("v", ["pt"], ["qp"], lambda e: e.quantize_mx(T.qp[:], T.sp[:], T.pt[:]))
             op("t", ["qp", "qn"], ["PC"], lambda e: e.matmul_mx(T.PC[:, 0:128], T.qp[:], T.sp[:], T.qn[:], T.sn[:], True, True))
-            side("q")
-            op("v", ["hp", "PC", "sel"], ["ht"], lambda e: e.tensor_scalar(T.m_ht[:], T.hp[:], T.PC[:, 0:1], T.m_sel[:, 0:1], OP.is_equal, OP.mult))
-        op("v", ["ht"], ["qh"], lambda e: e.quantize_mx(T["qh%d" % nx][:], T["sh%d" % nx][:], T.m_ht[:]))
+            op("v", ["hp", "PC", "sel"], ["ht"], lambda e: e.tensor_scalar(T.m_ht[:], T.hp[:], T.PC[:, 0:1], sel, OP.is_equal, OP.mult))
+        op("v", ["ht"], ["qh"], lambda e: e.quantize_mx(T.qh[:], T.sh[:], T.m_ht[:]))
         for c in (0, 12):
-            op("t", ["qh", "qx"], ["PL"], lambda e: e.matmul_mx(
-                T.PL[:, 0:128], T["qh%d" % nx][:], T["sh%d" % nx][:], T["qx%d" % nx][:, c:c + 128], T["sx%d" % nx][:, c:c + 128], c == 0, c == 12))
+            op("t", ["qh", "qx"], ["PL"], lambda e: e.matmul_mx(T.PL[:, 0:128], T.qh[:], T.sh[:], T.qx[:, c:c + 128], T.sx[:, c:c + 128], c == 0, c == 12))
+        if b == 0:
+            zeros(2, "z")
+            zeros(2, "p")
+        if b == 1:
+            op("v", ["onesa", "onesb"], ["qn"], lambda e: e.quantize_mx(T.qn[:], T.sn[:], T.ones[:, 0:512]))
+            op("v", ["wt"], ["qw"], lambda e: e.quantize_mx(T.qw[:], T.sw[:], T.wt[:]))
         lst = "lst%d" % nx
         m = (8, 10, 4)[b]
         op("v", ["PL"], [lst], lambda e: e.tensor_copy(T[lst][:, 0:m], T.PL[:, 0:m]))
@@ -357,24 +373,23 @@ def rank_program(g, core, T, topo):
             to = T.cores[rank ^ (1 << nx)]
             ready("g", [lst])
             send(T["bl%d" % nx][:], T[lst][:, 4:8] if b == 0 else T[lst][:, 8:10], to, "al%d" % nx)
-            pick("x%d" % b, "s%d" % b, 64, 320, lst, nx)
-            ready("g", ["x%do" % nx])
-            send(bits(T["x%d" % nx][:, 128:192]), bits(T["x%d" % nx][:, 64:128]), to, "ac%d" % nx)
-            ready("g", ["s%do" % nx])
-            send(T["s%d" % nx][:, 128:192], T["s%d" % nx][:, 64:128], to, "ac%d" % nx)
+            o = "o%d" % nx
+            pick(nx, o, (o + "c", o + "s"))
+            ready("g", [o + "c"])
+            send(bits(T["p%d" % nx][:, 0:64]), bits(T[o][:]), to, "ac%d" % nx)
+            ready("g", [o + "s"])
+            send(T["sp%d" % nx][:, 0:64], T["s" + o][:], to, "ac%d" % nx)
             own_tables(nx, T[lst][:, 4:8], lst)
-            if b == 0:
-                idle_work()
 
-    pick("x2", "s2", 64, 320, "lst3", 3)
-    dma("s", ["x3o"], [], "st0", T.oc[:], bits(T.x3[:, 64:128]))
-    op("v", ["yt0", "yt1", "lst3"], ["ys"], lambda e: e.tensor_copy(T.ys[:], T.ytab[:].indirect(T.lst3[:, 0:4])))
-    op("v", ["nra", "nrb", "nrc", "lst3"], ["nbs"], lambda e: e.tensor_copy(T.nbs[:], T.m_nr[:].indirect(T.lst3[:, 0:4])))
-    dma("a", ["s3o"], [], "st1", T.osc[0:4, :], T.s3[0:4, 64:128])
+    pick(3, "y3", ("y3c", "y3s"))
+    dma("s", ["y3c"], [], "st0", T.oc[:], bits(T.y3[:]))
+    op("v", ["yt", "lst3"], ["ys"], lambda e: e.tensor_copy(T.ys[:], T.ytab[:].indirect(T.lst3[:, 0:4])))
+    op("a", ["nra", "nrb", "lst3"], ["nbs"], lambda e: e.activation(T.nbs[:], T.m_nr[:].indirect(T.lst3[:, 0:4]), AF.Copy))
+    dma("a", ["y3s"], [], "st1", T.osc[0:4, :], T.sy3[0:4, :])
     dma("s", ["ys"], [], "st6", T.y[:], T.ys[:])
-    dma("a", ["s3o"], [], "st2", T.osc[4:8, :], T.s3[32:36, 64:128])
-    dma("a", ["s3o"], [], "st3", T.osc[8:12, :], T.s3[64:68, 64:128])
+    dma("a", ["y3s"], [], "st2", T.osc[4:8, :], T.sy3[32:36, :])
+    dma("a", ["y3s"], [], "st3", T.osc[8:12, :], T.sy3[64:68, :])
     dma("s", ["nbs"], [], "st5", T.nb[:], T.nbs[0:1, :])
-    dma("a", ["s3o"], [], "st4", T.osc[12:16, :], T.s3[96:100, 64:128])
+    dma("a", ["y3s"], [], "st4", T.osc[12:16, :], T.sy3[96:100, :])
     finish()
     g.wait_ge(T.sem.sent, sent[0])

@@ -1,17 +1,18 @@
 from concourse.mybir import dt, AluOpType as OP, AxisListType, ActivationFunctionType as AF
 
 BIG = 1.0e29
-TINY = 2.0 ** -120
+FLOOR = 2.0 ** -124
+BELOW = 1.0 - 2.0 ** -24
 MAGIC = 1.5 * 2.0 ** 27
 
 F32, B16, I32, U16, U8, MX = "float32", "bfloat16", "int32", "uint16", "uint8", "float8_e4m3fn_x4"
 SCRATCH = {}
 for _d, _names in (
-        (B16, "ut 16|grt 1024|wt 512|ones 520|zer 512|ur 512|zd 520|iot 256|hp 512|ld0 128|ldz 128|kr 64|neg1 64|xx0 576|xx 560"
-              "|pt 512|c0 256|c1 256|c2 256|c3 128|ht0 1024|t10 256|t11 256|t12 256|t40 256|t41 256|t42 256|m_nr 128|m_dx 128|m_dy 128"
-              "|m_gt 128|m_da 320|m_pa 256|m_mt 512|m_ld 128|m_ht 512"),
-        (F32, "cst 8|mask 64|rst 64|m4 4|phi 4|plo 4|jc 4|sr0 256|sc0 8|d0 128|d1 128|rk0 8|nbs 64|ys 64|ytab 128"
-              "|m_nc 8|m_s 8|m_eq 128|m_eq2 128|m_g4 64|m_g5 64|m_fa 4|m_fb 4|m_rw 64|m_sr 128|m_dd 128|m_cc 128"),
+        (B16, "ut 16|grt 1024|wt 512|ones 520|zer 512|ur 512|zd 520|iot 256|hp 512|dgb 64|kr 64|neg1 64|xx0 576|xx 560"
+              "|pt 512|c0 256|c1 256|c2 256|c3 256|ht0 1024|t10 256|t11 256|t12 256|t40 256|t41 256|t42 256|m_nr 128|m_dx 128|m_dy 128"
+              "|m_gt 128|m_da 320|m_pa 256|m_mt 512|m_ht 512|nbz 192"),
+        (F32, "cst 16|mask 64|rst 64|m4 4|phi 4|plo 4|ph64 4|jc 4|sr0 256|sc0 8|ld0 128|ldz 128|d0 128|d1 128|rk0 8|nbs 64|ys 64|ytab 192"
+              "|m_c 16|m_r 8|m_sc 8|m_v 16|m_eq 128|m_eq2 128|m_g4 64|m_g5 64|m_vv 64|m_fa 4|m_fb 4|m_rw 64|m_sra 64|m_w 128|m_f 128|m_m 128|m_cc 128"),
         (I32, "pi 8|bi 8|bj 8"),
         (U16, "hl 4|lst0 8|lst1 8|lst2 12|lst3 8|bl0 4|bl1 4|bl2 2|bu 4|m_toff 4|m_fl 4")):
     for _n in _names.split("|"):
@@ -19,7 +20,7 @@ for _d, _names in (
 for _n, _w in (("u", 128), ("e", 512), ("g", 256), ("w", 128), ("n", 128), ("x0", 144), ("x", 140), ("p", 128), ("h0", 256), ("h", 128)):
     SCRATCH["q" + _n] = ("sbuf", [128, _w], MX)
     SCRATCH["s" + _n] = ("sbuf", [128, _w], U8)
-for _n, _w in [("o%d" % _b, 64) for _b in range(3)] + [("p%d" % _b, 192) for _b in range(3)] + [("z%d" % _b, 128) for _b in range(3)] + [("y3", 64)]:
+for _n, _w in [("z%d" % _b, 384) for _b in range(3)] + [("y3", 64)]:
     SCRATCH[_n] = ("sbuf", [128, _w], MX)
     SCRATCH["s" + _n] = ("sbuf", [128, _w], U8)
 SCRATCH["hc"] = ("sbuf", [128, 64], MX)
@@ -103,6 +104,7 @@ def make_flow(g, T):
 def rank_program(g, core, T, topo):
     rank = T.rank_of(core)
     sent = [0]
+    PARTNER, OWN = slice(128, 192), slice(192, 256)
 
     def send(out, in_, dst, sem, away=None):
         e = [x for x in topo.engines(core, dst) if away is None or x in topo.engines(core, away)]
@@ -130,18 +132,20 @@ def rank_program(g, core, T, topo):
                 send(T.bl0[:], T.hl[:], far, "al0")
             if core == a:
                 g.wait_ge(T.sem.hc, n)
-                send(bits(T.p0[:, 0:64]), bits(T.hc[:]), far, "ac0")
+                send(bits(T.z0[:, PARTNER]), bits(T.hc[:]), far, "ac0")
             if core == b:
                 g.wait_ge(T.sem.hs, n)
-                send(T.sp0[:, 0:64], T.hs[:], far, "ac0")
+                send(T.sz0[:, PARTNER], T.hs[:], far, "ac0")
             g.wait_ge(T.sem.sent, sent[0])
         return
 
     op, dma, arrives, ready, finish = make_flow(g, T)
     X = AxisListType.X
-    pf, pm, nisa, okb, k1000 = [T.cst[:, i:i + 1] for i in range(5)]
-    nct, ncx, cnt, okc, sc, rk, sel = [T.m_s[:, i:i + 1] for i in range(7)]
-    nc = T.m_nc[:, 0:1]
+    pf, pm, nisa, okb, floor = [T.cst[:, i:i + 1] for i in range(5)]
+    nc, cnt, okc = [T.m_c[:, i:i + 1] for i in range(3)]
+    v, hc, mc, ph, cc = [T.m_v[:, i:i + 1] for i in range(5)]
+    rk, rkb, sel = [T.m_r[:, i:i + 1] for i in range(3)]
+    sc = T.m_sc[:, 0:1]
 
     dma("s", [], ["gr0"], "ld1", T.grt[:, 0:512], T.gr[:, 0:512])
     dma("a", [], ["ut"], "ld0", T.ut[:, 0:4], T.u[:, 0:4])
@@ -149,86 +153,120 @@ def rank_program(g, core, T, topo):
     dma("s", [], ["wt"], "ld3", T.wt[:], T.w[:])
 
     op("g", [], ["pi"], lambda e: e.iota(T.pi[:, 0:1], [[0, 1]], 0, 1))
-    op("g", [], ["hp"], lambda e: e.iota(T.hp[:], [[0, 8], [1, 16], [16, 4]], 0, 0, allow_small_or_imprecise_dtypes=True))
+    op("v", [], ["ldz"], lambda e: e.memset(T.ldz[:], BELOW))
     op("v", [], ["m4"], lambda e: e.memset(T.m4[:], MAGIC))
     op("v", [], ["onesa"], lambda e: e.memset(T.ones[:, 0:128], 1.0))
     op("v", [], ["onesb"], lambda e: e.memset(T.ones[:, 128:520], 1.0))
     op("v", ["pi"], ["pf"], lambda e: e.tensor_copy(pf, T.pi[:, 0:1]))
+    op("v", [], ["floor"], lambda e: e.memset(floor, FLOOR))
+    op("v", [], ["xx0z"], lambda e: e.memset(T.xx0[:], 0.0))
     op("v", ["m4", "pf"], ["phi"], lambda e: e.tensor_scalar(T.phi[:], T.m4[:], pf, MAGIC, OP.add, OP.subtract))
-    op("v", [], ["ldz"], lambda e: e.memset(T.ldz[:], -TINY))
-    op("g", ["ldz"], ["ld0"], lambda e: e.affine_select(T.ld0[:], T.ldz[:], [[-1, 128]], OP.is_gt, 0.0, 0, 1))
+    op("v", [], ["zer"], lambda e: e.memset(T.zer[:], 0.0))
     op("v", ["phi", "pf"], ["plo"], lambda e: e.tensor_scalar(T.plo[:], T.phi[:], pf, -1.0, OP.subtract, OP.mult))
+    op("g", ["ldz"], ["ld0"], lambda e: e.affine_select(T.ld0[:], T.ldz[:], [[-1, 128]], OP.is_gt, 1.0, 0, 1))
+    op("g", ["onesa", "onesb"], ["zd"], lambda e: e.affine_select(T.zd[:, 0:516], T.ones[:, 0:516], [[-1, 516]], OP.is_equal, 0.0, 3, 4))
+    op("g", [], ["kr"], lambda e: e.iota(T.kr[:], [[0, 4], [1, 16]], 0, 0, allow_small_or_imprecise_dtypes=True))
+    op("g", [], ["hp"], lambda e: e.iota(T.hp[:], [[0, 8], [1, 16], [16, 4]], 0, 0, allow_small_or_imprecise_dtypes=True))
+    op("g", [], ["iot"], lambda e: e.iota(T.iot[:], [[1, 256]], 0, 0, allow_small_or_imprecise_dtypes=True))
+    op("g", [], ["t10"], lambda e: e.iota(T.t10[:], [[0, 256]], 64, 0, allow_small_or_imprecise_dtypes=True))
+    op("g", ["onesa"], ["dgb"], lambda e: e.affine_select(T.dgb[:], T.ones[:, 0:64], [[-1, 64]], OP.is_equal, 0.0, -64, 1))
+    for i, src, add in ((0, "phi", 0.0), (32, "phi", 128.0), (64, "plo", 0.0)):
+        op("a", [src, "xx0z"], ["xx0"], lambda e: e.activation(T.xx0[:, i:i + 16:5], T[src][:], AF.Copy, bias=add))
     for t in range(4):
         op("v", ["onesa", "ut"], ["ur"], lambda e: e.tensor_scalar(T.ur[:, t:512:4], T.ones[:, 0:128], T.ut[:, t:t + 1], None, OP.mult))
     H = [slice(0, 128), slice(128, 256)]
     op("v", ["gr0"], ["qg0"], lambda e: e.quantize_mx(T.qg[:, H[0]], T.sg[:, H[0]], T.grt[:, 0:512]))
     op("v", ["ur"], ["qu"], lambda e: e.quantize_mx(T.qu[:], T.su[:], T.ur[:]))
     op("v", ["gr1"], ["qg1"], lambda e: e.quantize_mx(T.qg[:, H[1]], T.sg[:, H[1]], T.grt[:, 512:1024]))
-    op("v", [], ["xx0z"], lambda e: e.memset(T.xx0[:], 0.0))
-    op("g", [], ["iot"], lambda e: e.iota(T.iot[:], [[1, 256]], 0, 0, allow_small_or_imprecise_dtypes=True))
-    op("g", ["onesa", "onesb"], ["zd"], lambda e: e.affine_select(T.zd[:, 0:516], T.ones[:, 0:516], [[-1, 516]], OP.is_equal, 0.0, 3, 4))
-    op("g", [], ["kr"], lambda e: e.iota(T.kr[:], [[0, 4], [1, 16]], 0, 0, allow_small_or_imprecise_dtypes=True))
-    op("g", [], ["t10"], lambda e: e.iota(T.t10[:], [[0, 256]], 64, 0, allow_small_or_imprecise_dtypes=True))
+    op("v", ["xx0"], ["qx0"], lambda e: e.quantize_mx(T.qx0[:], T.sx0[:], T.xx0[:]))
+
+    def unpacker(t):
+        op("v", ["zd"], ["qe"], lambda e: e.quantize_mx(T.qe[:, 128 * t:128 * t + 128], T.se[:, 128 * t:128 * t + 128], T.zd[:, 3 - t:515 - t]))
+
+    def zeros(b):
+        z, s = T["z%d" % b], T["sz%d" % b]
+        op("v", ["zer"], ["z%dm" % b], lambda e: e.quantize_mx(z[:, 256:384], s[:, 256:384], T.zer[:]))
+        op("v", ["zer"], ["z%dz" % b], lambda e: e.quantize_mx(z[:, 0:128], s[:, 0:128], T.zer[:]))
 
     for h, P in ((0, "PC"), (1, "PS")):
-        op("t", ["qu", "qg%d" % h], ["PE%d" % h], lambda e: e.matmul_mx(T.PE[:, 512 * h:512 * h + 128], T.qu[:], T.su[:], T.qg[:, H[h]], T.sg[:, H[h]], True, True))
         op("t", ["qu", "qg%d" % h], [P], lambda e: e.matmul_mx(T[P][:, 0:128], T.qg[:, H[h]], T.sg[:, H[h]], T.qu[:], T.su[:], True, True))
-        op("a", ["PE%d" % h], ["sr0%d" % h], lambda e: e.activation(T.sr0[:, H[h]], T.PE[:, 512 * h:512 * h + 128], AF.Abs))
-        op("v", [P], ["nsc%d" % h], lambda e: e.tensor_reduce(T.sc0[:, h + 2:h + 3], T[P][:, 0:1], X, OP.max, negate=True, apply_absolute_value=True))
-        op("v", [P], ["sc0%d" % h], lambda e: e.tensor_reduce(T.sc0[:, h:h + 1], T[P][:, 0:1], X, OP.max, apply_absolute_value=True))
-    for h in range(2):
-        op("a", ["sr0%d" % h, "nsc%d" % h], ["d%d" % h], lambda e: e.activation(T["d%d" % h][:], T.sr0[:, H[h]], AF.Identity, bias=T.sc0[:, h + 2:h + 3]))
-    for i, src, add in ((0, "phi", 0.0), (32, "phi", 128.0), (64, "plo", 0.0)):
-        op("a", [src, "xx0z"], ["xx0"], lambda e: e.activation(T.xx0[:, i:i + 16:5], T[src][:], AF.Copy, bias=add))
-    for h in range(2):
+        op("t", ["qu", "qg%d" % h], ["PE%d" % h], lambda e: e.matmul_mx(T.PE[:, 512 * h:512 * h + 128], T.qu[:], T.su[:], T.qg[:, H[h]], T.sg[:, H[h]], True, True))
+        op("a", [P, "floor"], ["sc0%d" % h], lambda e: e.activation(T.sc0[:, h:h + 1], T[P][:, 0:1], AF.Abs, bias=floor))
+        op("a", ["PE%d" % h, "floor"], ["sr0%d" % h], lambda e: e.activation(T.sr0[:, H[h]], T.PE[:, 512 * h:512 * h + 128], AF.Abs, bias=floor))
+
+    def across(h):
         op("v", ["sr0%d" % (1 - h), "sc0%d" % h], ["c%da" % h], lambda e: e.tensor_scalar(
             T["c%d" % h][:, H[1 - h]], T.sr0[:, H[1 - h]], T.sc0[:, h:h + 1], None, OP.is_ge if h else OP.is_gt))
+
+    def passed(h):
+        op("v", ["ld0", "sc0%d" % h], ["d%d" % h], lambda e: e.tensor_scalar(T["d%d" % h][:], T.ld0[:], T.sc0[:, h:h + 1], None, OP.mult))
+
+    def within(h):
+        op("v", ["sr0%d" % h, "d%d" % h], ["c%db" % h], lambda e: e.tensor_tensor(T["c%d" % h][:, H[h]], T.sr0[:, H[h]], T["d%d" % h][:], OP.is_gt))
+
+    def total(h, k, i):
+        part = H[1 - h] if k == "a" else H[h]
+        op("a", ["c%d%s" % (h, k)], ["rk%d%s" % (h, k), "cx%d%s" % (h, k)], lambda e: e.activation(
+            T["c%d" % (h + 2)][:, part], T["c%d" % h][:, part], AF.Copy, accum_out=T.rk0[:, i:i + 1]))
+
+    def onehot(h):
+        op("v", ["hp", "rk%da" % h, "rk%db" % h], ["ht0%d" % h], lambda e: e.tensor_scalar(
+            T.ht0[:, 512 * h:512 * h + 512], T.hp[:], T.rk0[:, 2 * h:2 * h + 1], T.rk0[:, 2 * h + 1:2 * h + 2], OP.subtract, OP.is_equal))
+
+    op("v", ["pi"], ["pi15"], lambda e: e.tensor_scalar(T.pi[:, 1:2], T.pi[:, 0:1], 15, None, OP.bitwise_and))
+    unpacker(0)
+    passed(0)
+    op("v", ["pi15"], ["pm"], lambda e: e.tensor_copy(pm, T.pi[:, 1:2]))
+    op("v", ["kr"], ["rst"], lambda e: e.tensor_scalar(T.rst[:], T.kr[:], 0.5, None, OP.is_gt))
+    within(0)
+    passed(1)
+    across(0)
+    across(1)
+    within(1)
+    total(0, "b", 0)
+    total(0, "a", 1)
+    total(1, "a", 2)
+    total(1, "b", 3)
+    unpacker(1)
+    onehot(0)
+    op("v", ["kr", "pm"], ["mask"], lambda e: e.tensor_scalar(T.mask[:], T.kr[:], pm, None, OP.is_equal))
+    onehot(1)
     for h in range(2):
-        op("v", ["d%d" % h, "ld0"], ["c%db" % h], lambda e: e.tensor_tensor(T["c%d" % h][:, H[h]], T["d%d" % h][:], T.ld0[:], OP.is_gt))
-    op("a", ["c1a"], ["rk1a", "c3"], lambda e: e.activation(T.c3[:], T.c1[:, H[0]], AF.Copy, accum_out=T.rk0[:, 2:3]))
-    op("a", ["c0a", "c0b"], ["rk00", "c2"], lambda e: e.activation(T.c2[:], T.c0[:], AF.Copy, accum_out=T.rk0[:, 0:1]))
-    op("v", ["c1b"], ["rk1b"], lambda e: e.tensor_reduce(T.rk0[:, 1:2], T.c1[:, H[1]], X, OP.add))
-    op("v", ["xx0"], ["qx0"], lambda e: e.quantize_mx(T.qx0[:], T.sx0[:], T.xx0[:]))
-    op("v", ["hp", "rk1a", "rk1b"], ["ht01"], lambda e: e.tensor_scalar(T.ht0[:, 512:1024], T.hp[:], T.rk0[:, 2:3], T.rk0[:, 1:2], OP.subtract, OP.is_equal))
-    op("v", ["hp", "rk00"], ["ht00"], lambda e: e.tensor_scalar(T.ht0[:, 0:512], T.hp[:], T.rk0[:, 0:1], None, OP.is_equal))
-    for h in (1, 0):
         op("v", ["ht0%d" % h], ["qh0%d" % h], lambda e: e.quantize_mx(T.qh0[:, H[h]], T.sh0[:, H[h]], T.ht0[:, 512 * h:512 * h + 512]))
-    for i, (h, c) in enumerate(((1, 8), (1, 16), (0, 0), (0, 16))):
-        op("t", ["qh0%d" % h, "qx0"], ["PL"], lambda e: e.matmul_mx(T.PL[:, 0:128], T.qh0[:, H[h]], T.sh0[:, H[h]], T.qx0[:, c:c + 128], T.sx0[:, c:c + 128], i == 0, i == 3))
-
-    def zeros(b, which):
-        if which == "z":
-            op("v", ["zer"], ["z%d%s" % (b, k) for k in "osFf"], lambda e: e.quantize_mx(T["z%d" % b][:], T["sz%d" % b][:], T.zer[:]))
-        else:
-            op("v", ["zer"], ["p%dm" % b], lambda e: e.quantize_mx(T["p%d" % b][:, 64:192], T["sp%d" % b][:, 64:192], T.zer[:]))
-
-    op("v", [], ["zer"], lambda e: e.memset(T.zer[:], 0.0))
-    zeros(0, "z")
+        for c in (8 * h, 16):
+            op("t", ["qh0%d" % h, "qx0"], ["PL"], lambda e: e.matmul_mx(
+                T.PL[:, 0:128], T.qh0[:, H[h]], T.sh0[:, H[h]], T.qx0[:, c:c + 128], T.sx0[:, c:c + 128], h == 0 and c == 0, h == 1 and c == 16))
+    zeros(0)
+    unpacker(2)
+    unpacker(3)
+    op("v", [], ["daz"], lambda e: e.memset(T.m_da[:, 64:320:80], 0.0))
     op("v", ["PL"], ["lst0"], lambda e: e.tensor_copy(T.lst0[:, 0:4], T.PL[:, 0:4]))
+    op("v", [], ["neg1"], lambda e: e.memset(T.neg1[:], -1.0))
+    op("v", ["hp", "pm"], ["jc"], lambda e: e.tensor_scalar(T.jc[:], T.hp[:, 0:4], pm, None, OP.add))
 
-    def pick(b, into, toks):
-        src, ssrc, n, frm = ("qg", "sg", 256, ["qg0", "qg1"]) if b == 0 else ("z%d" % (b - 1), "sz%d" % (b - 1), 128, ["z%d%s" % (b - 1, k) for k in "osFf"])
+    def pick(b, into, at):
+        src, ssrc, w, frm = (("qg", "sg", slice(0, 256), ["qg0", "qg1"]) if b == 0 else
+                             ("z%d" % (b - 1), "sz%d" % (b - 1), slice(128, 320), ["z%d%s" % (b - 1, k) for k in "psom"]))
         lst = "lst%d" % b
-        op("v", frm + [lst], [toks[0]], lambda e: e.tensor_copy(
-            T[into][:, 0:64].bitcast(dt.uint32), T[src][:, 0:n].bitcast(dt.uint32).indirect(T[lst][:, 0:4])))
-        op("a", frm + [lst], [toks[1]], lambda e: e.activation(T["s" + into][:, 0:64], T[ssrc][:, 0:n].indirect(T[lst][:, 0:4]), AF.Copy))
+        op("v", frm + [lst], [into + "o"], lambda e: e.tensor_copy(
+            T[into][:, at].bitcast(dt.uint32), T[src][:, w].bitcast(dt.uint32).indirect(T[lst][:, 0:4])))
+        op("a", frm + [lst], [into + "s"], lambda e: e.activation(T["s" + into][:, at], T[ssrc][:, w].indirect(T[lst][:, 0:4]), AF.Copy))
 
     ha, hb = helpers(rank)
     away = T.cores[rank ^ 2]
     ready("g", ["lst0"])
     send(T.hl[:], T.lst0[:, 0:4], hb, "hl", away)
-    pick(0, "o0", ("o0c", "o0s"))
-    ready("g", ["o0c"])
-    send(bits(T.hc[:]), bits(T.o0[:]), ha, "hc", away)
-    ready("g", ["o0s"])
-    send(T.hs[:], T.so0[:], hb, "hs", away)
+    pick(0, "z0", OWN)
+    ready("g", ["z0o"])
+    send(bits(T.hc[:]), bits(T.z0[:, OWN]), ha, "hc", away)
+    ready("g", ["z0s"])
+    send(T.hs[:], T.sz0[:, OWN], hb, "hs", away)
 
     def big(b):
         op("g", ["iot"], ["t4%d" % b], lambda e: e.affine_select(T["t4%d" % b][:], T.iot[:], [[0, 256]], OP.is_gt, BIG, -1, 0))
 
     def own_tables(b, aw, awt):
-        z, s, zt = T["z%d" % b], T["sz%d" % b], ["z%d%s" % (b, k) for k in "osFf"]
-        pick(b, "z%d" % b, zt[0:2])
+        z, s, zt = T["z%d" % b], T["sz%d" % b], ["z%d%s" % (b, k) for k in "osm"]
         op("v", ["iot", awt, "t1%d" % b], ["t1%d" % b], lambda e: e.tensor_copy(T["t1%d" % b][:].indirect(aw), T.iot[:, 0:64]))
         op("a", ["iot", awt], ["nra"], lambda e: e.activation(T.m_nr[:, 0:64], T.iot[:].indirect(aw), AF.Copy))
         op("g", ["nra"], ["dxa"], lambda e: e.affine_select(T.m_dx[:, 0:64], T.m_nr[:, 0:64], [[-1, 64]], OP.is_equal, 0.0, 0, 1))
@@ -236,45 +274,29 @@ def rank_program(g, core, T, topo):
             big(0)
         for t in range(4):
             op("t", ["qe"] + zt, ["PE%d" % t], lambda e: e.matmul_mx(
-                T.PE[:, 512 * t:512 * t + 128], T.qe[:, 128 * t:128 * t + 128], T.se[:, 128 * t:128 * t + 128], z[:], s[:], True, True))
-            da, pe = T.m_da[:, 80 * t:80 * t + 64], T.PE[:, 512 * t:512 * t + 64]
-            if b > 0 and t < 2:
-                op("v", ["PE%d" % t, "daz"], ["da%d" % t], lambda e: e.tensor_copy(da, pe))
-            else:
-                op("a", ["PE%d" % t, "daz"], ["da%d" % t], lambda e: e.activation(da, pe, AF.Copy))
-        op("t", ["qu"] + zt, ["PR"], lambda e: e.matmul_mx(T.PR[:, 0:128], T.qu[:], T.su[:], z[:], s[:], True, True))
+                T.PE[:, 512 * t:512 * t + 128], T.qe[:, 128 * t:128 * t + 128], T.se[:, 128 * t:128 * t + 128], z[:, 192:320], s[:, 192:320], True, True))
+            op("a", ["PE%d" % t, "daz"], ["da%d" % t], lambda e: e.activation(T.m_da[:, 80 * t:80 * t + 64], T.PE[:, 512 * t:512 * t + 64], AF.Copy))
+        op("t", ["qu"] + zt, ["PR"], lambda e: e.matmul_mx(T.PR[:, 0:128], T.qu[:], T.su[:], z[:, 192:320], s[:, 192:320], True, True))
 
-    for t in range(4):
-        op("v", ["zd"], ["qe"], lambda e: e.quantize_mx(T.qe[:, 128 * t:128 * t + 128], T.se[:, 128 * t:128 * t + 128], T.zd[:, 3 - t:515 - t]))
-    op("v", [], ["daz"], lambda e: e.memset(T.m_da[:, 64:320:80], 0.0))
     own_tables(0, T.lst0[:, 0:4], "lst0")
-    zeros(0, "p")
-    op("v", ["pi"], ["pi15"], lambda e: e.tensor_scalar(T.pi[:, 1:2], T.pi[:, 0:1], 15, None, OP.bitwise_and))
-    op("v", ["kr"], ["rst"], lambda e: e.tensor_scalar(T.rst[:], T.kr[:], 0.5, None, OP.is_gt))
     op("v", ["pf"], ["nisa"], lambda e: e.tensor_scalar(nisa, pf, 63.5, -1.0, OP.is_lt, OP.mult))
-    op("v", ["pi15"], ["pm"], lambda e: e.tensor_copy(pm, T.pi[:, 1:2]))
     op("v", ["pf"], ["okb"], lambda e: e.tensor_scalar(okb, pf, 63.5, 1.0, OP.is_lt, OP.add))
-    op("v", [], ["neg1"], lambda e: e.memset(T.neg1[:], -1.0))
-    op("v", ["kr", "pm"], ["mask"], lambda e: e.tensor_scalar(T.mask[:], T.kr[:], pm, None, OP.is_equal))
-    op("v", ["hp", "pm"], ["jc"], lambda e: e.tensor_scalar(T.jc[:], T.hp[:, 0:4], pm, None, OP.add))
+    op("v", ["phi"], ["ph64"], lambda e: e.tensor_scalar(T.ph64[:], T.phi[:], 64.0, None, OP.add))
     op("v", [], ["mtz"], lambda e: e.memset(T.m_mt[:, 256:512], 0.0))
     op("v", [], ["xxz"], lambda e: e.memset(T.xx[:], 0.0))
-    op("v", [], ["k1000"], lambda e: e.memset(k1000, 1000.0))
-    zeros(1, "z")
+    zeros(1)
     op("v", ["plo", "xxz"], ["xxl"], lambda e: e.tensor_copy(T.xx[:, 48:64:5], T.plo[:]))
-    op("v", ["phi", "xxz"], ["xxh"], lambda e: e.tensor_copy(T.xx[:, 0:16:5], T.phi[:]))
-    zeros(1, "p")
 
     for b in range(3):
         nx = b + 1
-        z, sz, p, sp = T["z%d" % b], T["sz%d" % b], T["p%d" % b], T["sp%d" % b]
-        zt = ["z%d%s" % (b, k) for k in "osFf"]
+        z, sz = T["z%d" % b], T["sz%d" % b]
+        own, mrg, prt = ["z%do" % b, "z%ds" % b], "z%dm" % b, "z%dp" % b
         t1, t4 = "t1%d" % b, "t4%d" % b
         aw, awt = (T.lst0[:, 0:4], "lst0") if b == 0 else (T["lst%d" % b][:, 4:8], "lst%d" % b)
         src = helpers(rank ^ 1)[0] if b == 0 else T.cores[rank ^ (1 << b)]
         n = len(topo.engines(src, core))
         arrives("bl%d" % b, "al%d" % b, n)
-        arrives("p%dl" % b, "ac%d" % b, 2 * n)
+        arrives(prt, "ac%d" % b, 2 * n)
 
         if b == 2:
             op("v", ["bl2"], ["bi"], lambda e: e.tensor_copy(T.bi[:, 0:2], T.bl2[:]))
@@ -284,107 +306,117 @@ def rank_program(g, core, T, topo):
         bwt = "bl%d" % b if b < 2 else "bu"
         bw = T[bwt][:]
         op("v", [t1, bwt, "mask"], ["g4"], lambda e: e.tensor_tensor(T.m_g4[:], T[t1][:].indirect(bw), T.mask[:], OP.mult))
+        op("v", ["iot", bwt, "dgb"], ["dxb"], lambda e: e.tensor_tensor(T.m_dx[:, 64:128], T.iot[:].indirect(bw), T.dgb[:], OP.mult))
         op("v", ["g4", "rst"], ["g5"], lambda e: e.tensor_tensor_scan(T.m_g5[:], T.rst[:], T.m_g4[:], 0.0, OP.mult, OP.add))
+        op("v", [t1, bwt, "dgb"], ["vv"], lambda e: e.tensor_tensor(T.m_vv[:], T[t1][:].indirect(bw), T.dgb[:], OP.mult))
         op("v", ["g5"], ["toff"], lambda e: e.tensor_copy(T.m_toff[:], T.m_g5[:, 15:64:16]))
         op("v", ["g5"], ["fa"], lambda e: e.tensor_scalar(T.m_fa[:], T.m_g5[:, 15:64:16], 63.5, 64.0, OP.is_lt, OP.mult))
+        op("v", ["vv"], ["v"], lambda e: e.tensor_reduce(v, T.m_vv[:], X, OP.add))
         op("a", ["iot", bwt], ["nrb"], lambda e: e.activation(T.m_nr[:, 64:128], T.iot[:].indirect(bw), AF.Copy))
-        op("g", ["nrb"], ["dxb"], lambda e: e.affine_select(T.m_dx[:, 64:128], T.m_nr[:, 64:128], [[-1, 64]], OP.is_equal, 0.0, -64, 1))
+        op("a", ["dxa", "dxb"], ["nc", "dy"], lambda e: e.activation(T.m_dy[:], T.m_dx[:], AF.Copy, accum_out=nc))
         if b < 2:
             op("g", [], ["t1%d" % nx], lambda e: e.iota(T["t1%d" % nx][:], [[0, 256]], 64, 0, allow_small_or_imprecise_dtypes=True))
             big(nx)
         if b == 0:
             op("g", [], ["ptz"], lambda e: e.iota(T.pt[:], [[0, 512]], 0, 0, allow_small_or_imprecise_dtypes=True))
-        for t in range(2):
-            op("v", ["da%d" % t, "toff"], ["pa%d" % t], lambda e: e.tensor_copy(T.m_pa[:, 64 * t:64 * t + 64], T.m_da[:, 80 * t:80 * t + 65].indirect(T.m_toff[:])))
-        for t in range(2, 4):
-            op("a", ["da%d" % t, "toff"], ["pa%d" % t], lambda e: e.activation(T.m_pa[:, 64 * t:64 * t + 64], T.m_da[:, 80 * t:80 * t + 65].indirect(T.m_toff[:]), AF.Copy))
-        op("v", ["fa", "jc"], ["fb"], lambda e: e.tensor_tensor(T.m_fb[:], T.m_fa[:], T.jc[:], OP.add))
-        op("a", ["dxa", "dxb"], ["nc", "dy"], lambda e: e.activation(T.m_dy[:], T.m_dx[:], AF.Copy, accum_out=nc))
-        op("a", ["PR"], ["rw"], lambda e: e.activation(T.m_rw[:], T.PR[:, 0:64], AF.Abs))
+        for t in range(4):
+            pa, da = T.m_pa[:, 64 * t:64 * t + 64], T.m_da[:, 80 * t:80 * t + 65].indirect(T.m_toff[:])
+            if t < 2:
+                op("v", ["da%d" % t, "toff"], ["pa%d" % t], lambda e: e.tensor_copy(pa, da))
+            else:
+                op("a", ["da%d" % t, "toff"], ["pa%d" % t], lambda e: e.activation(pa, da, AF.Copy))
+        op("v", ["v"], ["hc"], lambda e: e.tensor_scalar(hc, v, 63.5, None, OP.is_gt))
+        op("v", ["v"], ["mc"], lambda e: e.tensor_scalar(mc, v, 63.5, None, OP.is_lt))
+        op("a", ["PR", "floor"], ["rw"], lambda e: e.activation(T.m_rw[:], T.PR[:, 0:64], AF.Abs, bias=floor))
+        op("a", ["nra", "nrb", "nc"], ["eq"], lambda e: e.activation(T.m_eq[:], T.m_nr[:], AF.Abs, bias=nc, scale=-1.0))
+        op("a", ["eq"], ["cnt", "eq2"], lambda e: e.activation(T.m_eq2[:], T.m_eq[:], AF.Relu, bias=1.0, scale=-1.0, accum_out=cnt))
 
         for t in range(4):
-            op("t", ["qe", "p%dm" % b, "p%dl" % b], ["PE%d" % t], lambda e: e.matmul_mx(
-                T.PE[:, 512 * t:512 * t + 128], T.qe[:, 128 * t:128 * t + 128], T.se[:, 128 * t:128 * t + 128], p[:, 0:128], sp[:, 0:128], True, True))
-        for t in range(4):
+            op("t", ["qe", prt] + own, ["PE%d" % t], lambda e: e.matmul_mx(
+                T.PE[:, 512 * t:512 * t + 128], T.qe[:, 128 * t:128 * t + 128], T.se[:, 128 * t:128 * t + 128], z[:, 128:256], sz[:, 128:256], True, True))
+        op("t", ["qu", "z%dz" % b, prt], ["PL"], lambda e: e.matmul_mx(T.PL[:, 0:128], z[:, 64:192], sz[:, 64:192], T.qu[:], T.su[:], True, True))
+        op("t", ["qu", prt] + own, ["PR"], lambda e: e.matmul_mx(T.PR[:, 0:128], T.qu[:], T.su[:], z[:, 128:256], sz[:, 128:256], True, True))
+        for t in (0, 2, 1, 3):
             op("v", ["PE%d" % t, "pa%d" % t], ["mt%d" % t], lambda e: e.tensor_tensor(
                 T.m_mt[:, t:256:4], T.PE[:, 512 * t:512 * t + 64], T.m_pa[:, 64 * t:64 * t + 64], OP.add))
-            if t == 1:
-                op("v", ["fb"], ["fl"], lambda e: e.tensor_copy(T.m_fl[:], T.m_fb[:]))
-        op("v", ["mt0", "mt1", "mt2", "mt3", "mtz"], ["p%dm" % b], lambda e: e.quantize_mx(p[:, 64:192], sp[:, 64:192], T.m_mt[:]))
-        op("v", ["m4", "nc", "xxz"], ["xxn"], lambda e: e.tensor_scalar(T.xx[:, 16:32:5], T.m4[:], nc, MAGIC, OP.add, OP.subtract))
-        op("v", ["p%dl" % b, "p%dm" % b, "fl"], [zt[2]], lambda e: e.tensor_copy(
-            z[:, 64:128].bitcast(dt.uint32), p[:, 0:128].bitcast(dt.uint32).indirect(T.m_fl[:])))
-        op("a", ["p%dl" % b, "p%dm" % b, "fl"], [zt[3]], lambda e: e.activation(sz[:, 64:128], sp[:, 0:128].indirect(T.m_fl[:]), AF.Copy))
-        op("t", ["qu"] + zt, ["PC"], lambda e: e.matmul_mx(T.PC[:, 0:128], z[:], sz[:], T.qu[:], T.su[:], True, True))
-        op("t", ["qu"] + zt, ["PS"], lambda e: e.matmul_mx(T.PS[:, 0:128], T.qu[:], T.su[:], z[:], sz[:], True, True))
-        op("a", ["nra", "nrb", "nc"], ["eq"], lambda e: e.activation(T.m_eq[:], T.m_nr[:], AF.Abs, bias=nc, scale=-1.0))
-        op("v", ["xxn", "nc"], ["xxm"], lambda e: e.tensor_scalar(T.xx[:, 64:80:5], T.xx[:, 16:32:5], nc, -1.0, OP.subtract, OP.mult))
+        op("v", ["nra", "nrb", "nc"], ["f"], lambda e: e.tensor_scalar(T.m_f[:], T.m_nr[:], nc, BELOW, OP.is_ge, OP.max))
+        op("v", ["fa", "jc"], ["fb"], lambda e: e.tensor_tensor(T.m_fb[:], T.m_fa[:], T.jc[:], OP.add))
+        op("v", ["mt0", "mt1", "mt2", "mt3", "mtz"], [mrg], lambda e: e.quantize_mx(z[:, 256:384], sz[:, 256:384], T.m_mt[:]))
+        op("t", ["qu", mrg] + own, ["PC"], lambda e: e.matmul_mx(T.PC[:, 0:128], z[:, 192:320], sz[:, 192:320], T.qu[:], T.su[:], True, True))
+        op("t", ["qu", mrg] + own, ["PS"], lambda e: e.matmul_mx(T.PS[:, 0:128], T.qu[:], T.su[:], z[:, 192:320], sz[:, 192:320], True, True))
+        op("v", ["PL", "hc"], ["cc"], lambda e: e.tensor_scalar(cc, T.PL[:, 0:1], hc, FLOOR, OP.mult, OP.add))
+        if b < 2:
+            op("v", ["m4", "nc", "xxz"], ["xxn"], lambda e: e.tensor_scalar(T.xx[:, 16:32:5], T.m4[:], nc, MAGIC, OP.add, OP.subtract))
+        else:
+            op("v", ["nra", "nrb", "nc"], ["gt"], lambda e: e.tensor_scalar(T.m_gt[:], T.m_nr[:], nc, 1000.0, OP.is_le, OP.mult))
+        op("v", ["v"], ["ph"], lambda e: e.tensor_scalar(ph, v, 63.5, -128.0, OP.is_gt, OP.mult))
         op("v", [t4, "neg1", bwt], [t4], lambda e: e.tensor_copy(T[t4][:].indirect(bw), T.neg1[:]))
-        op("v", ["nra", "nrb", "nc"], ["ld"], lambda e: e.tensor_scalar(T.m_ld[:], T.m_nr[:], nc, -TINY, OP.is_lt, OP.mult))
-        op("v", [t4, "rw", awt], ["sra"], lambda e: e.tensor_tensor(T.m_sr[:, 0:64], T[t4][:].indirect(aw), T.m_rw[:], OP.min))
+        op("v", ["ph64", "ph", "xxz"], ["xxh"], lambda e: e.tensor_scalar(T.xx[:, 0:16:5], T.ph64[:], ph, None, OP.add))
+        if b < 2:
+            op("v", ["xxn", "nc"], ["xxm"], lambda e: e.tensor_scalar(T.xx[:, 64:80:5], T.xx[:, 16:32:5], nc, -1.0, OP.subtract, OP.mult))
+        op("v", ["fb"], ["fl"], lambda e: e.tensor_copy(T.m_fl[:], T.m_fb[:]))
+        op("v", [t4, "rw", awt], ["sra"], lambda e: e.tensor_tensor(T.m_sra[:], T[t4][:].indirect(aw), T.m_rw[:], OP.min))
+        op("a", ["cnt", "nisa", "okb"], ["ok"], lambda e: e.activation(okc, cnt, AF.Identity, bias=okb, scale=nisa))
+        op("a", ["PR", "floor"], ["wp"], lambda e: e.activation(T.m_w[:, 0:64], T.PR[:, 0:64], AF.Abs, bias=floor))
+
+        op("a", ["PC", "mc", "cc"], ["sc"], lambda e: e.activation(sc, T.PC[:, 0:1], AF.Abs, bias=cc, scale=mc))
+        op("a", ["PS", "floor"], ["wm"], lambda e: e.activation(T.m_w[:, 64:128], T.PS[:, 64:128], AF.Abs, bias=floor))
         if b == 1:
             for i in (0, 48):
                 op("a", ["xxn", "xxm"], ["xxp"], lambda e: e.activation(T.xx[:, i + 32:i + 38:5], T.xx[:, i + 16:i + 22:5], AF.Copy))
                 op("a", ["xxn", "xxm"], ["xxp"], lambda e: e.activation(T.xx[:, i + 34:i + 40:5], T.xx[:, i + 16:i + 22:5], AF.Copy, scale=256.0))
+        for k, i in (("m0", 0), ("m1", 64)):
+            op("v", ["f", "sc", "ok"], [k], lambda e: e.tensor_scalar(T.m_m[:, i:i + 64], T.m_f[:, i:i + 64], sc, okc, OP.mult, OP.mult))
+        op("v", ["sra", "m0"], ["cca"], lambda e: e.tensor_tensor(T.m_cc[:, 0:64], T.m_sra[:], T.m_m[:, 0:64], OP.is_gt))
+        op("v", ["wp", "wm", "fl", "m1"], ["ccb"], lambda e: e.tensor_tensor(T.m_cc[:, 64:128], T.m_w[:].indirect(T.m_fl[:]), T.m_m[:, 64:128], OP.is_gt))
 
-        def lists():
+        def places():
             op("v", ["xxl", "xxh", "xxn", "xxm"] + (["xxp"] if b == 1 else []), ["qx"], lambda e: e.quantize_mx(T.qx[:], T.sx[:], T.xx[:]))
 
-        op("a", ["PS"], ["srb"], lambda e: e.activation(T.m_sr[:, 64:128], T.PS[:, 64:128], AF.Abs))
-        op("a", ["eq"], ["cnt", "eq2"], lambda e: e.activation(T.m_eq2[:], T.m_eq[:], AF.Relu, bias=1.0, scale=-1.0, accum_out=cnt))
-        op("a", ["cnt", "nisa", "okb"], ["ok"], lambda e: e.activation(okc, cnt, AF.Identity, bias=okb, scale=nisa))
-        if b == 2:
-            op("a", ["ok", "k1000"], ["nct"], lambda e: e.activation(nct, okc, AF.Identity, bias=k1000, scale=-1000.0))
-            op("a", ["nct", "nc"], ["ncx"], lambda e: e.activation(ncx, nct, AF.Identity, bias=nc))
-        op("v", ["PC"], ["sc"], lambda e: e.tensor_reduce(sc, T.PC[:, 0:1], X, OP.max, apply_absolute_value=True))
-        if b != 1:
-            lists()
-        op("v", ["sra", "sc"], ["dda"], lambda e: e.tensor_scalar(T.m_dd[:, 0:64], T.m_sr[:, 0:64], sc, None, OP.subtract))
-        op("v", ["srb", "sc"], ["ddb"], lambda e: e.tensor_scalar(T.m_dd[:, 64:128], T.m_sr[:, 64:128], sc, None, OP.subtract))
-        op("v", ["dda", "ld"], ["cca"], lambda e: e.tensor_tensor(T.m_cc[:, 0:64], T.m_dd[:, 0:64], T.m_ld[:, 0:64], OP.is_gt))
-        op("v", ["ddb", "ld"], ["ccb"], lambda e: e.tensor_tensor(T.m_cc[:, 64:128], T.m_dd[:, 64:128], T.m_ld[:, 64:128], OP.is_gt))
-        if b == 1:
-            lists()
-        op("v", ["cca", "ccb"], ["rk"], lambda e: e.tensor_reduce(rk, T.m_cc[:], X, OP.add))
         if b < 2:
-            op("v", ["hp", "rk", "ok"], ["ht"], lambda e: e.tensor_scalar(T.m_ht[:], T.hp[:], rk, okc, OP.is_equal, OP.mult))
+            op("v", ["cca"], ["rka"], lambda e: e.tensor_reduce(rk, T.m_cc[:, 0:64], X, OP.add))
+            op("v", ["ccb"], ["rkb"], lambda e: e.tensor_reduce(rkb, T.m_cc[:, 64:128], X, OP.add))
+            places()
+            op("v", ["hp", "rka", "rkb"], ["ht"], lambda e: e.tensor_scalar(T.m_ht[:], T.hp[:], rk, rkb, OP.subtract, OP.is_equal))
         else:
-            op("t", ["qw"] + zt, ["PE0"], lambda e: e.matmul_mx(T.PE[:, 0:128], T.qw[:], T.sw[:], z[:], sz[:], True, True))
-            op("a", ["PE0"], ["yt"], lambda e: e.activation(T.ytab[:], T.PE[:, 0:128], AF.Copy))
-            op("v", ["nra", "nrb", "ncx"], ["gt"], lambda e: e.tensor_scalar(T.m_gt[:], T.m_nr[:], ncx, 1000.0, OP.is_le, OP.mult))
-            op("v", ["gt", "rk", "ptz"], ["pt"], lambda e: e.tensor_scalar(T.pt[:, 0:512:4], T.m_gt[:], rk, 63.5, OP.add, OP.is_lt))
-            op("v", ["rk", "ok"], ["sel"], lambda e: e.tensor_scalar(sel, rk, 63.5, okc, OP.is_lt, OP.mult))
+            op("v", ["cca", "ccb"], ["rka"], lambda e: e.tensor_reduce(rk, T.m_cc[:], X, OP.add))
+            op("t", ["qw", mrg, prt] + own, ["PE0"], lambda e: e.matmul_mx(T.PE[:, 0:192], T.qw[:], T.sw[:], z[:, 128:320], sz[:, 128:320], True, True))
+            op("a", ["PE0"], ["yt"], lambda e: e.activation(T.ytab[:], T.PE[:, 0:192], AF.Copy))
+            op("a", ["nra", "nrb"], ["nbz0"], lambda e: e.activation(T.nbz[:, 0:64], T.m_nr[:, 64:128], AF.Copy))
+            op("a", ["nra", "nrb"], ["nbz1"], lambda e: e.activation(T.nbz[:, 64:192], T.m_nr[:], AF.Copy))
+            op("v", ["gt", "rka", "ptz"], ["pt"], lambda e: e.tensor_scalar(T.pt[:, 0:512:4], T.m_gt[:], rk, 63.5, OP.add, OP.is_lt))
+            op("v", ["rka"], ["sel"], lambda e: e.tensor_scalar(sel, rk, 63.5, None, OP.is_lt))
             op("v", ["pt"], ["qp"], lambda e: e.quantize_mx(T.qp[:], T.sp[:], T.pt[:]))
+            places()
             op("t", ["qp", "qn"], ["PC"], lambda e: e.matmul_mx(T.PC[:, 0:128], T.qp[:], T.sp[:], T.qn[:], T.sn[:], True, True))
             op("v", ["hp", "PC", "sel"], ["ht"], lambda e: e.tensor_scalar(T.m_ht[:], T.hp[:], T.PC[:, 0:1], sel, OP.is_equal, OP.mult))
         op("v", ["ht"], ["qh"], lambda e: e.quantize_mx(T.qh[:], T.sh[:], T.m_ht[:]))
         for c in (0, 12):
             op("t", ["qh", "qx"], ["PL"], lambda e: e.matmul_mx(T.PL[:, 0:128], T.qh[:], T.sh[:], T.qx[:, c:c + 128], T.sx[:, c:c + 128], c == 0, c == 12))
         if b == 0:
-            zeros(2, "z")
-            zeros(2, "p")
+            zeros(2)
         if b == 1:
             op("v", ["onesa", "onesb"], ["qn"], lambda e: e.quantize_mx(T.qn[:], T.sn[:], T.ones[:, 0:512]))
             op("v", ["wt"], ["qw"], lambda e: e.quantize_mx(T.qw[:], T.sw[:], T.wt[:]))
         lst = "lst%d" % nx
-        m = (8, 10, 4)[b]
-        op("v", ["PL"], [lst], lambda e: e.tensor_copy(T[lst][:, 0:m], T.PL[:, 0:m]))
+        k = (8, 10, 4)[b]
+        op("v", ["PL"], [lst], lambda e: e.tensor_copy(T[lst][:, 0:k], T.PL[:, 0:k]))
         if b < 2:
             to = T.cores[rank ^ (1 << nx)]
             ready("g", [lst])
             send(T["bl%d" % nx][:], T[lst][:, 4:8] if b == 0 else T[lst][:, 8:10], to, "al%d" % nx)
-            o = "o%d" % nx
-            pick(nx, o, (o + "c", o + "s"))
-            ready("g", [o + "c"])
-            send(bits(T["p%d" % nx][:, 0:64]), bits(T[o][:]), to, "ac%d" % nx)
+            o = "z%d" % nx
+            pick(nx, o, OWN)
+            ready("g", [o + "o"])
+            send(bits(T[o][:, PARTNER]), bits(T[o][:, OWN]), to, "ac%d" % nx)
             ready("g", [o + "s"])
-            send(T["sp%d" % nx][:, 0:64], T["s" + o][:], to, "ac%d" % nx)
+            send(T["s" + o][:, PARTNER], T["s" + o][:, OWN], to, "ac%d" % nx)
             own_tables(nx, T[lst][:, 4:8], lst)
 
-    pick(3, "y3", ("y3c", "y3s"))
-    dma("s", ["y3c"], [], "st0", T.oc[:], bits(T.y3[:]))
+    pick(3, "y3", slice(0, 64))
+    dma("s", ["y3o"], [], "st0", T.oc[:], bits(T.y3[:]))
     op("v", ["yt", "lst3"], ["ys"], lambda e: e.tensor_copy(T.ys[:], T.ytab[:].indirect(T.lst3[:, 0:4])))
-    op("a", ["nra", "nrb", "lst3"], ["nbs"], lambda e: e.activation(T.nbs[:], T.m_nr[:].indirect(T.lst3[:, 0:4]), AF.Copy))
+    op("a", ["nbz0", "nbz1", "lst3"], ["nbs"], lambda e: e.activation(T.nbs[:], T.nbz[:].indirect(T.lst3[:, 0:4]), AF.Copy))
     dma("a", ["y3s"], [], "st1", T.osc[0:4, :], T.sy3[0:4, :])
     dma("s", ["ys"], [], "st6", T.y[:], T.ys[:])
     dma("a", ["y3s"], [], "st2", T.osc[4:8, :], T.sy3[32:36, :])

from concourse.mybir import dt, AluOpType as OP, AxisListType, ActivationFunctionType as AF

BIG = 1.0e29
FLOOR = 2.0 ** -124
BELOW = 1.0 - 2.0 ** -24
MAGIC = 1.5 * 2.0 ** 27

F32, B16, I32, U16, U8, MX = "float32", "bfloat16", "int32", "uint16", "uint8", "float8_e4m3fn_x4"
SCRATCH = {}
for _d, _names in (
        (B16, "ut 16|grt 1024|wt 512|ones 520|zer 512|ur 512|zd 520|iot 256|hp 512|dgb 64|kr 64|neg1 64|xx0 576|xx 560"
              "|pt 512|c0 256|c1 256|c2 256|c3 256|ht0 1024|t10 256|t11 256|t12 256|t40 256|t41 256|t42 256|m_nr 128|m_dx 128|m_dy 128"
              "|m_gt 128|m_da 320|m_pa 256|m_mt 512|m_ht 512|nbz 192"),
        (F32, "cst 16|mask 64|rst 64|m4 4|phi 4|plo 4|ph64 4|jc 4|sr0 256|sc0 8|ld0 128|ldz 128|d0 128|d1 128|rk0 8|nbs 64|ys 64|ytab 192"
              "|m_c 16|m_r 8|m_sc 8|m_v 16|m_eq 128|m_eq2 128|m_g4 64|m_g5 64|m_vv 64|m_fa 4|m_fb 4|m_rw 64|m_sra 64|m_w 128|m_f 128|m_m 128|m_cc 128"),
        (I32, "pi 8|bi 8|bj 8"),
        (U16, "hl 4|lst0 8|lst1 8|lst2 12|lst3 8|bl0 4|bl1 4|bl2 2|bu 4|m_toff 4|m_fl 4")):
    for _n in _names.split("|"):
        SCRATCH[_n.split()[0]] = ("sbuf", [128, int(_n.split()[1])], _d)
for _n, _w in (("u", 128), ("e", 512), ("g", 256), ("w", 128), ("n", 128), ("x0", 144), ("x", 140), ("p", 128), ("h0", 256), ("h", 128)):
    SCRATCH["q" + _n] = ("sbuf", [128, _w], MX)
    SCRATCH["s" + _n] = ("sbuf", [128, _w], U8)
for _n, _w in [("z%d" % _b, 384) for _b in range(3)] + [("y3", 64)]:
    SCRATCH[_n] = ("sbuf", [128, _w], MX)
    SCRATCH["s" + _n] = ("sbuf", [128, _w], U8)
SCRATCH["hc"] = ("sbuf", [128, 64], MX)
SCRATCH["hs"] = ("sbuf", [128, 64], U8)
SCRATCH["PE"] = ("psum", [128, 2048], F32)
for _n in ("PR", "PC", "PL", "PS"):
    SCRATCH[_n] = ("psum", [128, 512], F32)

SEMAPHORES = (["kv", "ka", "kt", "kg", "sent", "hc", "hs", "hl"] + ["al%d" % b for b in range(3)] + ["ac%d" % b for b in range(3)]
              + ["ld%d" % i for i in range(4)] + ["st%d" % i for i in range(8)])


def make_flow(g, T):
    eng = {"v": g.vector, "a": g.scalar, "t": g.tensor, "g": g, "s": g.sync}
    own = {"v": "kv", "a": "ka", "t": "kt", "g": "kg"}
    total, clock, ev, wr, rd, order = {}, {k: {} for k in eng}, {}, {}, {}, {}

    def need(q, events):
        for e in sorted(events, key=lambda e: -order.get(e, 0)):
            sem, val = e
            if clock[q].get(sem, 0) >= val:
                continue
            eng[q].wait_ge(T.sem[sem], val)
            for s, v in ev.get(e, {}).items():
                clock[q][s] = max(clock[q].get(s, 0), v)
            clock[q][sem] = max(clock[q].get(sem, 0), val)

    def deps(mine, reads, writes):
        out = set()
        for t in reads:
            if t not in wr:
                raise ValueError("nothing wrote " + t)
            out.add(wr[t])
        for t in writes:
            if t in wr and wr[t][0] != mine:
                out.add(wr[t])
            for e in rd.get(t, ()):
                if e[0] != mine:
                    out.add(e)
        return out

    def note(q, e, reads, writes):
        ev[e] = dict(clock[q])
        ev[e][e[0]] = e[1]
        order[e] = len(order) + 1
        for t in reads:
            rd.setdefault(t, []).append(e)
        for t in writes:
            wr[t] = e
            rd[t] = []

    def op(q, reads, writes, fn):
        sem = own[q]
        need(q, deps(sem, reads, writes))
        total[sem] = total.get(sem, 0) + 1
        fn(eng[q]).then_inc(T.sem[sem], 1)
        note(q, (sem, total[sem]), reads, writes)

    def dma(q, reads, writes, sem, out, in_):
        need(q, deps(None, reads, writes))
        eng[q].dma_start(out, in_).then_inc(T.sem[sem], 16)
        total[sem] = total.get(sem, 0) + 16
        note(q, (sem, total[sem]), reads, writes)

    def arrives(tok, sem, val):
        ev[(sem, val)] = {sem: val}
        order[(sem, val)] = len(order) + 1
        total[sem] = val
        wr[tok] = (sem, val)
        rd[tok] = []

    def ready(q, reads):
        need(q, deps(None, reads, []))

    def finish():
        need("g", list(total.items()))

    return op, dma, arrives, ready, finish


def rank_program(g, core, T, topo):
    rank = T.rank_of(core)
    sent = [0]
    PARTNER, OWN = slice(128, 192), slice(192, 256)

    def send(out, in_, dst, sem, away=None):
        e = [x for x in topo.engines(core, dst) if away is None or x in topo.engines(core, away)]
        rid, pid = topo.addr(dst, core)
        g.remote_dma(out, in_, T.sem[sem], T.sem.sent, pid, rid, sum(1 << x for x in e))
        sent[0] += len(e)

    def helpers(r):
        c0, far = T.cores[r], T.cores[r ^ 1]
        hs = [c for c in topo.cores_of(c0) if c != c0 and topo.die(c) == topo.die(c0) and topo.may_write(c, far)]
        return hs[0], hs[-1]

    def bits(v):
        return v.bitcast(dt.uint8)

    if rank is None:
        for r in range(len(T.cores)):
            a, b = helpers(r)
            if core not in (a, b):
                continue
            far = T.cores[r ^ 1]
            n = len([x for x in topo.engines(T.cores[r], core) if x in topo.engines(T.cores[r], T.cores[r ^ 2])])
            if core == b:
                g.wait_ge(T.sem.hl, n)
                send(T.bl0[:], T.hl[:], far, "al0")
            if core == a:
                g.wait_ge(T.sem.hc, n)
                send(bits(T.z0[:, PARTNER]), bits(T.hc[:]), far, "ac0")
            if core == b:
                g.wait_ge(T.sem.hs, n)
                send(T.sz0[:, PARTNER], T.hs[:], far, "ac0")
            g.wait_ge(T.sem.sent, sent[0])
        return

    op, dma, arrives, ready, finish = make_flow(g, T)
    X = AxisListType.X
    pf, pm, nisa, okb, floor = [T.cst[:, i:i + 1] for i in range(5)]
    nc, cnt, okc = [T.m_c[:, i:i + 1] for i in range(3)]
    v, hc, mc, ph, cc = [T.m_v[:, i:i + 1] for i in range(5)]
    rk, rkb, sel = [T.m_r[:, i:i + 1] for i in range(3)]
    sc = T.m_sc[:, 0:1]

    dma("s", [], ["gr0"], "ld1", T.grt[:, 0:512], T.gr[:, 0:512])
    dma("a", [], ["ut"], "ld0", T.ut[:, 0:4], T.u[:, 0:4])
    dma("a", [], ["gr1"], "ld2", T.grt[:, 512:1024], T.gr[:, 512:1024])
    dma("s", [], ["wt"], "ld3", T.wt[:], T.w[:])

    op("g", [], ["pi"], lambda e: e.iota(T.pi[:, 0:1], [[0, 1]], 0, 1))
    op("v", [], ["ldz"], lambda e: e.memset(T.ldz[:], BELOW))
    op("v", [], ["m4"], lambda e: e.memset(T.m4[:], MAGIC))
    op("v", [], ["onesa"], lambda e: e.memset(T.ones[:, 0:128], 1.0))
    op("v", [], ["onesb"], lambda e: e.memset(T.ones[:, 128:520], 1.0))
    op("v", ["pi"], ["pf"], lambda e: e.tensor_copy(pf, T.pi[:, 0:1]))
    op("v", [], ["floor"], lambda e: e.memset(floor, FLOOR))
    op("v", [], ["xx0z"], lambda e: e.memset(T.xx0[:], 0.0))
    op("v", ["m4", "pf"], ["phi"], lambda e: e.tensor_scalar(T.phi[:], T.m4[:], pf, MAGIC, OP.add, OP.subtract))
    op("v", [], ["zer"], lambda e: e.memset(T.zer[:], 0.0))
    op("v", ["phi", "pf"], ["plo"], lambda e: e.tensor_scalar(T.plo[:], T.phi[:], pf, -1.0, OP.subtract, OP.mult))
    op("g", ["ldz"], ["ld0"], lambda e: e.affine_select(T.ld0[:], T.ldz[:], [[-1, 128]], OP.is_gt, 1.0, 0, 1))
    op("g", ["onesa", "onesb"], ["zd"], lambda e: e.affine_select(T.zd[:, 0:516], T.ones[:, 0:516], [[-1, 516]], OP.is_equal, 0.0, 3, 4))
    op("g", [], ["kr"], lambda e: e.iota(T.kr[:], [[0, 4], [1, 16]], 0, 0, allow_small_or_imprecise_dtypes=True))
    op("g", [], ["hp"], lambda e: e.iota(T.hp[:], [[0, 8], [1, 16], [16, 4]], 0, 0, allow_small_or_imprecise_dtypes=True))
    op("g", [], ["iot"], lambda e: e.iota(T.iot[:], [[1, 256]], 0, 0, allow_small_or_imprecise_dtypes=True))
    op("g", [], ["t10"], lambda e: e.iota(T.t10[:], [[0, 256]], 64, 0, allow_small_or_imprecise_dtypes=True))
    op("g", ["onesa"], ["dgb"], lambda e: e.affine_select(T.dgb[:], T.ones[:, 0:64], [[-1, 64]], OP.is_equal, 0.0, -64, 1))
    for i, src, add in ((0, "phi", 0.0), (32, "phi", 128.0), (64, "plo", 0.0)):
        op("a", [src, "xx0z"], ["xx0"], lambda e: e.activation(T.xx0[:, i:i + 16:5], T[src][:], AF.Copy, bias=add))
    for t in range(4):
        op("v", ["onesa", "ut"], ["ur"], lambda e: e.tensor_scalar(T.ur[:, t:512:4], T.ones[:, 0:128], T.ut[:, t:t + 1], None, OP.mult))
    H = [slice(0, 128), slice(128, 256)]
    op("v", ["gr0"], ["qg0"], lambda e: e.quantize_mx(T.qg[:, H[0]], T.sg[:, H[0]], T.grt[:, 0:512]))
    op("v", ["ur"], ["qu"], lambda e: e.quantize_mx(T.qu[:], T.su[:], T.ur[:]))
    op("v", ["gr1"], ["qg1"], lambda e: e.quantize_mx(T.qg[:, H[1]], T.sg[:, H[1]], T.grt[:, 512:1024]))
    op("v", ["xx0"], ["qx0"], lambda e: e.quantize_mx(T.qx0[:], T.sx0[:], T.xx0[:]))

    def unpacker(t):
        op("v", ["zd"], ["qe"], lambda e: e.quantize_mx(T.qe[:, 128 * t:128 * t + 128], T.se[:, 128 * t:128 * t + 128], T.zd[:, 3 - t:515 - t]))

    def zeros(b):
        z, s = T["z%d" % b], T["sz%d" % b]
        op("v", ["zer"], ["z%dm" % b], lambda e: e.quantize_mx(z[:, 256:384], s[:, 256:384], T.zer[:]))
        op("v", ["zer"], ["z%dz" % b], lambda e: e.quantize_mx(z[:, 0:128], s[:, 0:128], T.zer[:]))

    for h, P in ((0, "PC"), (1, "PS")):
        op("t", ["qu", "qg%d" % h], [P], lambda e: e.matmul_mx(T[P][:, 0:128], T.qg[:, H[h]], T.sg[:, H[h]], T.qu[:], T.su[:], True, True))
        op("t", ["qu", "qg%d" % h], ["PE%d" % h], lambda e: e.matmul_mx(T.PE[:, 512 * h:512 * h + 128], T.qu[:], T.su[:], T.qg[:, H[h]], T.sg[:, H[h]], True, True))
        op("a", [P, "floor"], ["sc0%d" % h], lambda e: e.activation(T.sc0[:, h:h + 1], T[P][:, 0:1], AF.Abs, bias=floor))
        op("a", ["PE%d" % h, "floor"], ["sr0%d" % h], lambda e: e.activation(T.sr0[:, H[h]], T.PE[:, 512 * h:512 * h + 128], AF.Abs, bias=floor))

    def across(h):
        op("v", ["sr0%d" % (1 - h), "sc0%d" % h], ["c%da" % h], lambda e: e.tensor_scalar(
            T["c%d" % h][:, H[1 - h]], T.sr0[:, H[1 - h]], T.sc0[:, h:h + 1], None, OP.is_ge if h else OP.is_gt))

    def passed(h):
        op("v", ["ld0", "sc0%d" % h], ["d%d" % h], lambda e: e.tensor_scalar(T["d%d" % h][:], T.ld0[:], T.sc0[:, h:h + 1], None, OP.mult))

    def within(h):
        op("v", ["sr0%d" % h, "d%d" % h], ["c%db" % h], lambda e: e.tensor_tensor(T["c%d" % h][:, H[h]], T.sr0[:, H[h]], T["d%d" % h][:], OP.is_gt))

    def total(h, k, i):
        part = H[1 - h] if k == "a" else H[h]
        op("a", ["c%d%s" % (h, k)], ["rk%d%s" % (h, k), "cx%d%s" % (h, k)], lambda e: e.activation(
            T["c%d" % (h + 2)][:, part], T["c%d" % h][:, part], AF.Copy, accum_out=T.rk0[:, i:i + 1]))

    def onehot(h):
        op("v", ["hp", "rk%da" % h, "rk%db" % h], ["ht0%d" % h], lambda e: e.tensor_scalar(
            T.ht0[:, 512 * h:512 * h + 512], T.hp[:], T.rk0[:, 2 * h:2 * h + 1], T.rk0[:, 2 * h + 1:2 * h + 2], OP.subtract, OP.is_equal))

    op("v", ["pi"], ["pi15"], lambda e: e.tensor_scalar(T.pi[:, 1:2], T.pi[:, 0:1], 15, None, OP.bitwise_and))
    unpacker(0)
    passed(0)
    op("v", ["pi15"], ["pm"], lambda e: e.tensor_copy(pm, T.pi[:, 1:2]))
    op("v", ["kr"], ["rst"], lambda e: e.tensor_scalar(T.rst[:], T.kr[:], 0.5, None, OP.is_gt))
    within(0)
    passed(1)
    across(0)
    across(1)
    within(1)
    total(0, "b", 0)
    total(0, "a", 1)
    total(1, "a", 2)
    total(1, "b", 3)
    unpacker(1)
    onehot(0)
    op("v", ["kr", "pm"], ["mask"], lambda e: e.tensor_scalar(T.mask[:], T.kr[:], pm, None, OP.is_equal))
    onehot(1)
    for h in range(2):
        op("v", ["ht0%d" % h], ["qh0%d" % h], lambda e: e.quantize_mx(T.qh0[:, H[h]], T.sh0[:, H[h]], T.ht0[:, 512 * h:512 * h + 512]))
        for c in (8 * h, 16):
            op("t", ["qh0%d" % h, "qx0"], ["PL"], lambda e: e.matmul_mx(
                T.PL[:, 0:128], T.qh0[:, H[h]], T.sh0[:, H[h]], T.qx0[:, c:c + 128], T.sx0[:, c:c + 128], h == 0 and c == 0, h == 1 and c == 16))
    zeros(0)
    unpacker(2)
    unpacker(3)
    op("v", [], ["daz"], lambda e: e.memset(T.m_da[:, 64:320:80], 0.0))
    op("v", ["PL"], ["lst0"], lambda e: e.tensor_copy(T.lst0[:, 0:4], T.PL[:, 0:4]))
    op("v", [], ["neg1"], lambda e: e.memset(T.neg1[:], -1.0))
    op("v", ["hp", "pm"], ["jc"], lambda e: e.tensor_scalar(T.jc[:], T.hp[:, 0:4], pm, None, OP.add))

    def pick(b, into, at):
        src, ssrc, w, frm = (("qg", "sg", slice(0, 256), ["qg0", "qg1"]) if b == 0 else
                             ("z%d" % (b - 1), "sz%d" % (b - 1), slice(128, 320), ["z%d%s" % (b - 1, k) for k in "psom"]))
        lst = "lst%d" % b
        op("v", frm + [lst], [into + "o"], lambda e: e.tensor_copy(
            T[into][:, at].bitcast(dt.uint32), T[src][:, w].bitcast(dt.uint32).indirect(T[lst][:, 0:4])))
        op("a", frm + [lst], [into + "s"], lambda e: e.activation(T["s" + into][:, at], T[ssrc][:, w].indirect(T[lst][:, 0:4]), AF.Copy))

    ha, hb = helpers(rank)
    away = T.cores[rank ^ 2]
    ready("g", ["lst0"])
    send(T.hl[:], T.lst0[:, 0:4], hb, "hl", away)
    pick(0, "z0", OWN)
    ready("g", ["z0o"])
    send(bits(T.hc[:]), bits(T.z0[:, OWN]), ha, "hc", away)
    ready("g", ["z0s"])
    send(T.hs[:], T.sz0[:, OWN], hb, "hs", away)

    def big(b):
        op("g", ["iot"], ["t4%d" % b], lambda e: e.affine_select(T["t4%d" % b][:], T.iot[:], [[0, 256]], OP.is_gt, BIG, -1, 0))

    def own_tables(b, aw, awt):
        z, s, zt = T["z%d" % b], T["sz%d" % b], ["z%d%s" % (b, k) for k in "osm"]
        op("v", ["iot", awt, "t1%d" % b], ["t1%d" % b], lambda e: e.tensor_copy(T["t1%d" % b][:].indirect(aw), T.iot[:, 0:64]))
        op("a", ["iot", awt], ["nra"], lambda e: e.activation(T.m_nr[:, 0:64], T.iot[:].indirect(aw), AF.Copy))
        op("g", ["nra"], ["dxa"], lambda e: e.affine_select(T.m_dx[:, 0:64], T.m_nr[:, 0:64], [[-1, 64]], OP.is_equal, 0.0, 0, 1))
        if b == 0:
            big(0)
        for t in range(4):
            op("t", ["qe"] + zt, ["PE%d" % t], lambda e: e.matmul_mx(
                T.PE[:, 512 * t:512 * t + 128], T.qe[:, 128 * t:128 * t + 128], T.se[:, 128 * t:128 * t + 128], z[:, 192:320], s[:, 192:320], True, True))
            op("a", ["PE%d" % t, "daz"], ["da%d" % t], lambda e: e.activation(T.m_da[:, 80 * t:80 * t + 64], T.PE[:, 512 * t:512 * t + 64], AF.Copy))
        op("t", ["qu"] + zt, ["PR"], lambda e: e.matmul_mx(T.PR[:, 0:128], T.qu[:], T.su[:], z[:, 192:320], s[:, 192:320], True, True))

    own_tables(0, T.lst0[:, 0:4], "lst0")
    op("v", ["pf"], ["nisa"], lambda e: e.tensor_scalar(nisa, pf, 63.5, -1.0, OP.is_lt, OP.mult))
    op("v", ["pf"], ["okb"], lambda e: e.tensor_scalar(okb, pf, 63.5, 1.0, OP.is_lt, OP.add))
    op("v", ["phi"], ["ph64"], lambda e: e.tensor_scalar(T.ph64[:], T.phi[:], 64.0, None, OP.add))
    op("v", [], ["mtz"], lambda e: e.memset(T.m_mt[:, 256:512], 0.0))
    op("v", [], ["xxz"], lambda e: e.memset(T.xx[:], 0.0))
    zeros(1)
    op("v", ["plo", "xxz"], ["xxl"], lambda e: e.tensor_copy(T.xx[:, 48:64:5], T.plo[:]))

    for b in range(3):
        nx = b + 1
        z, sz = T["z%d" % b], T["sz%d" % b]
        own, mrg, prt = ["z%do" % b, "z%ds" % b], "z%dm" % b, "z%dp" % b
        t1, t4 = "t1%d" % b, "t4%d" % b
        aw, awt = (T.lst0[:, 0:4], "lst0") if b == 0 else (T["lst%d" % b][:, 4:8], "lst%d" % b)
        src = helpers(rank ^ 1)[0] if b == 0 else T.cores[rank ^ (1 << b)]
        n = len(topo.engines(src, core))
        arrives("bl%d" % b, "al%d" % b, n)
        arrives(prt, "ac%d" % b, 2 * n)

        if b == 2:
            op("v", ["bl2"], ["bi"], lambda e: e.tensor_copy(T.bi[:, 0:2], T.bl2[:]))
            op("v", ["bi"], ["bj0"], lambda e: e.tensor_scalar(T.bj[:, 0:2], T.bi[:, 0:2], 255, None, OP.bitwise_and))
            op("v", ["bi"], ["bj1"], lambda e: e.tensor_scalar(T.bj[:, 2:4], T.bi[:, 0:2], 8, None, OP.logical_shift_right))
            op("v", ["bj0", "bj1"], ["bu"], lambda e: e.tensor_copy(T.bu[:], T.bj[:, 0:4]))
        bwt = "bl%d" % b if b < 2 else "bu"
        bw = T[bwt][:]
        op("v", [t1, bwt, "mask"], ["g4"], lambda e: e.tensor_tensor(T.m_g4[:], T[t1][:].indirect(bw), T.mask[:], OP.mult))
        op("v", ["iot", bwt, "dgb"], ["dxb"], lambda e: e.tensor_tensor(T.m_dx[:, 64:128], T.iot[:].indirect(bw), T.dgb[:], OP.mult))
        op("v", ["g4", "rst"], ["g5"], lambda e: e.tensor_tensor_scan(T.m_g5[:], T.rst[:], T.m_g4[:], 0.0, OP.mult, OP.add))
        op("v", [t1, bwt, "dgb"], ["vv"], lambda e: e.tensor_tensor(T.m_vv[:], T[t1][:].indirect(bw), T.dgb[:], OP.mult))
        op("v", ["g5"], ["toff"], lambda e: e.tensor_copy(T.m_toff[:], T.m_g5[:, 15:64:16]))
        op("v", ["g5"], ["fa"], lambda e: e.tensor_scalar(T.m_fa[:], T.m_g5[:, 15:64:16], 63.5, 64.0, OP.is_lt, OP.mult))
        op("v", ["vv"], ["v"], lambda e: e.tensor_reduce(v, T.m_vv[:], X, OP.add))
        op("a", ["iot", bwt], ["nrb"], lambda e: e.activation(T.m_nr[:, 64:128], T.iot[:].indirect(bw), AF.Copy))
        op("a", ["dxa", "dxb"], ["nc", "dy"], lambda e: e.activation(T.m_dy[:], T.m_dx[:], AF.Copy, accum_out=nc))
        if b < 2:
            op("g", [], ["t1%d" % nx], lambda e: e.iota(T["t1%d" % nx][:], [[0, 256]], 64, 0, allow_small_or_imprecise_dtypes=True))
            big(nx)
        if b == 0:
            op("g", [], ["ptz"], lambda e: e.iota(T.pt[:], [[0, 512]], 0, 0, allow_small_or_imprecise_dtypes=True))
        for t in range(4):
            pa, da = T.m_pa[:, 64 * t:64 * t + 64], T.m_da[:, 80 * t:80 * t + 65].indirect(T.m_toff[:])
            if t < 2:
                op("v", ["da%d" % t, "toff"], ["pa%d" % t], lambda e: e.tensor_copy(pa, da))
            else:
                op("a", ["da%d" % t, "toff"], ["pa%d" % t], lambda e: e.activation(pa, da, AF.Copy))
        op("v", ["v"], ["hc"], lambda e: e.tensor_scalar(hc, v, 63.5, None, OP.is_gt))
        op("v", ["v"], ["mc"], lambda e: e.tensor_scalar(mc, v, 63.5, None, OP.is_lt))
        op("a", ["PR", "floor"], ["rw"], lambda e: e.activation(T.m_rw[:], T.PR[:, 0:64], AF.Abs, bias=floor))
        op("a", ["nra", "nrb", "nc"], ["eq"], lambda e: e.activation(T.m_eq[:], T.m_nr[:], AF.Abs, bias=nc, scale=-1.0))
        op("a", ["eq"], ["cnt", "eq2"], lambda e: e.activation(T.m_eq2[:], T.m_eq[:], AF.Relu, bias=1.0, scale=-1.0, accum_out=cnt))

        for t in range(4):
            op("t", ["qe", prt] + own, ["PE%d" % t], lambda e: e.matmul_mx(
                T.PE[:, 512 * t:512 * t + 128], T.qe[:, 128 * t:128 * t + 128], T.se[:, 128 * t:128 * t + 128], z[:, 128:256], sz[:, 128:256], True, True))
        op("t", ["qu", "z%dz" % b, prt], ["PL"], lambda e: e.matmul_mx(T.PL[:, 0:128], z[:, 64:192], sz[:, 64:192], T.qu[:], T.su[:], True, True))
        op("t", ["qu", prt] + own, ["PR"], lambda e: e.matmul_mx(T.PR[:, 0:128], T.qu[:], T.su[:], z[:, 128:256], sz[:, 128:256], True, True))
        for t in (0, 2, 1, 3):
            op("v", ["PE%d" % t, "pa%d" % t], ["mt%d" % t], lambda e: e.tensor_tensor(
                T.m_mt[:, t:256:4], T.PE[:, 512 * t:512 * t + 64], T.m_pa[:, 64 * t:64 * t + 64], OP.add))
        op("v", ["nra", "nrb", "nc"], ["f"], lambda e: e.tensor_scalar(T.m_f[:], T.m_nr[:], nc, BELOW, OP.is_ge, OP.max))
        op("v", ["fa", "jc"], ["fb"], lambda e: e.tensor_tensor(T.m_fb[:], T.m_fa[:], T.jc[:], OP.add))
        op("v", ["mt0", "mt1", "mt2", "mt3", "mtz"], [mrg], lambda e: e.quantize_mx(z[:, 256:384], sz[:, 256:384], T.m_mt[:]))
        op("t", ["qu", mrg] + own, ["PC"], lambda e: e.matmul_mx(T.PC[:, 0:128], z[:, 192:320], sz[:, 192:320], T.qu[:], T.su[:], True, True))
        op("t", ["qu", mrg] + own, ["PS"], lambda e: e.matmul_mx(T.PS[:, 0:128], T.qu[:], T.su[:], z[:, 192:320], sz[:, 192:320], True, True))
        op("v", ["PL", "hc"], ["cc"], lambda e: e.tensor_scalar(cc, T.PL[:, 0:1], hc, FLOOR, OP.mult, OP.add))
        if b < 2:
            op("v", ["m4", "nc", "xxz"], ["xxn"], lambda e: e.tensor_scalar(T.xx[:, 16:32:5], T.m4[:], nc, MAGIC, OP.add, OP.subtract))
        else:
            op("v", ["nra", "nrb", "nc"], ["gt"], lambda e: e.tensor_scalar(T.m_gt[:], T.m_nr[:], nc, 1000.0, OP.is_le, OP.mult))
        op("v", ["v"], ["ph"], lambda e: e.tensor_scalar(ph, v, 63.5, -128.0, OP.is_gt, OP.mult))
        op("v", [t4, "neg1", bwt], [t4], lambda e: e.tensor_copy(T[t4][:].indirect(bw), T.neg1[:]))
        op("v", ["ph64", "ph", "xxz"], ["xxh"], lambda e: e.tensor_scalar(T.xx[:, 0:16:5], T.ph64[:], ph, None, OP.add))
        if b < 2:
            op("v", ["xxn", "nc"], ["xxm"], lambda e: e.tensor_scalar(T.xx[:, 64:80:5], T.xx[:, 16:32:5], nc, -1.0, OP.subtract, OP.mult))
        op("v", ["fb"], ["fl"], lambda e: e.tensor_copy(T.m_fl[:], T.m_fb[:]))
        op("v", [t4, "rw", awt], ["sra"], lambda e: e.tensor_tensor(T.m_sra[:], T[t4][:].indirect(aw), T.m_rw[:], OP.min))
        op("a", ["cnt", "nisa", "okb"], ["ok"], lambda e: e.activation(okc, cnt, AF.Identity, bias=okb, scale=nisa))
        op("a", ["PR", "floor"], ["wp"], lambda e: e.activation(T.m_w[:, 0:64], T.PR[:, 0:64], AF.Abs, bias=floor))

        op("a", ["PC", "mc", "cc"], ["sc"], lambda e: e.activation(sc, T.PC[:, 0:1], AF.Abs, bias=cc, scale=mc))
        op("a", ["PS", "floor"], ["wm"], lambda e: e.activation(T.m_w[:, 64:128], T.PS[:, 64:128], AF.Abs, bias=floor))
        if b == 1:
            for i in (0, 48):
                op("a", ["xxn", "xxm"], ["xxp"], lambda e: e.activation(T.xx[:, i + 32:i + 38:5], T.xx[:, i + 16:i + 22:5], AF.Copy))
                op("a", ["xxn", "xxm"], ["xxp"], lambda e: e.activation(T.xx[:, i + 34:i + 40:5], T.xx[:, i + 16:i + 22:5], AF.Copy, scale=256.0))
        for k, i in (("m0", 0), ("m1", 64)):
            op("v", ["f", "sc", "ok"], [k], lambda e: e.tensor_scalar(T.m_m[:, i:i + 64], T.m_f[:, i:i + 64], sc, okc, OP.mult, OP.mult))
        op("v", ["sra", "m0"], ["cca"], lambda e: e.tensor_tensor(T.m_cc[:, 0:64], T.m_sra[:], T.m_m[:, 0:64], OP.is_gt))
        op("v", ["wp", "wm", "fl", "m1"], ["ccb"], lambda e: e.tensor_tensor(T.m_cc[:, 64:128], T.m_w[:].indirect(T.m_fl[:]), T.m_m[:, 64:128], OP.is_gt))

        def places():
            op("v", ["xxl", "xxh", "xxn", "xxm"] + (["xxp"] if b == 1 else []), ["qx"], lambda e: e.quantize_mx(T.qx[:], T.sx[:], T.xx[:]))

        if b < 2:
            op("v", ["cca"], ["rka"], lambda e: e.tensor_reduce(rk, T.m_cc[:, 0:64], X, OP.add))
            op("v", ["ccb"], ["rkb"], lambda e: e.tensor_reduce(rkb, T.m_cc[:, 64:128], X, OP.add))
            places()
            op("v", ["hp", "rka", "rkb"], ["ht"], lambda e: e.tensor_scalar(T.m_ht[:], T.hp[:], rk, rkb, OP.subtract, OP.is_equal))
        else:
            op("v", ["cca", "ccb"], ["rka"], lambda e: e.tensor_reduce(rk, T.m_cc[:], X, OP.add))
            op("t", ["qw", mrg, prt] + own, ["PE0"], lambda e: e.matmul_mx(T.PE[:, 0:192], T.qw[:], T.sw[:], z[:, 128:320], sz[:, 128:320], True, True))
            op("a", ["PE0"], ["yt"], lambda e: e.activation(T.ytab[:], T.PE[:, 0:192], AF.Copy))
            op("a", ["nra", "nrb"], ["nbz0"], lambda e: e.activation(T.nbz[:, 0:64], T.m_nr[:, 64:128], AF.Copy))
            op("a", ["nra", "nrb"], ["nbz1"], lambda e: e.activation(T.nbz[:, 64:192], T.m_nr[:], AF.Copy))
            op("v", ["gt", "rka", "ptz"], ["pt"], lambda e: e.tensor_scalar(T.pt[:, 0:512:4], T.m_gt[:], rk, 63.5, OP.add, OP.is_lt))
            op("v", ["rka"], ["sel"], lambda e: e.tensor_scalar(sel, rk, 63.5, None, OP.is_lt))
            op("v", ["pt"], ["qp"], lambda e: e.quantize_mx(T.qp[:], T.sp[:], T.pt[:]))
            places()
            op("t", ["qp", "qn"], ["PC"], lambda e: e.matmul_mx(T.PC[:, 0:128], T.qp[:], T.sp[:], T.qn[:], T.sn[:], True, True))
            op("v", ["hp", "PC", "sel"], ["ht"], lambda e: e.tensor_scalar(T.m_ht[:], T.hp[:], T.PC[:, 0:1], sel, OP.is_equal, OP.mult))
        op("v", ["ht"], ["qh"], lambda e: e.quantize_mx(T.qh[:], T.sh[:], T.m_ht[:]))
        for c in (0, 12):
            op("t", ["qh", "qx"], ["PL"], lambda e: e.matmul_mx(T.PL[:, 0:128], T.qh[:], T.sh[:], T.qx[:, c:c + 128], T.sx[:, c:c + 128], c == 0, c == 12))
        if b == 0:
            zeros(2)
        if b == 1:
            op("v", ["onesa", "onesb"], ["qn"], lambda e: e.quantize_mx(T.qn[:], T.sn[:], T.ones[:, 0:512]))
            op("v", ["wt"], ["qw"], lambda e: e.quantize_mx(T.qw[:], T.sw[:], T.wt[:]))
        lst = "lst%d" % nx
        k = (8, 10, 4)[b]
        op("v", ["PL"], [lst], lambda e: e.tensor_copy(T[lst][:, 0:k], T.PL[:, 0:k]))
        if b < 2:
            to = T.cores[rank ^ (1 << nx)]
            ready("g", [lst])
            send(T["bl%d" % nx][:], T[lst][:, 4:8] if b == 0 else T[lst][:, 8:10], to, "al%d" % nx)
            o = "z%d" % nx
            pick(nx, o, OWN)
            ready("g", [o + "o"])
            send(bits(T[o][:, PARTNER]), bits(T[o][:, OWN]), to, "ac%d" % nx)
            ready("g", [o + "s"])
            send(T["s" + o][:, PARTNER], T["s" + o][:, OWN], to, "ac%d" % nx)
            own_tables(nx, T[lst][:, 4:8], lst)

    pick(3, "y3", slice(0, 64))
    dma("s", ["y3o"], [], "st0", T.oc[:], bits(T.y3[:]))
    op("v", ["yt", "lst3"], ["ys"], lambda e: e.tensor_copy(T.ys[:], T.ytab[:].indirect(T.lst3[:, 0:4])))
    op("a", ["nbz0", "nbz1", "lst3"], ["nbs"], lambda e: e.activation(T.nbs[:], T.nbz[:].indirect(T.lst3[:, 0:4]), AF.Copy))
    dma("a", ["y3s"], [], "st1", T.osc[0:4, :], T.sy3[0:4, :])
    dma("s", ["ys"], [], "st6", T.y[:], T.ys[:])
    dma("a", ["y3s"], [], "st2", T.osc[4:8, :], T.sy3[32:36, :])
    dma("a", ["y3s"], [], "st3", T.osc[8:12, :], T.sy3[64:68, :])
    dma("s", ["nbs"], [], "st5", T.nb[:], T.nbs[0:1, :])
    dma("a", ["y3s"], [], "st4", T.osc[12:16, :], T.sy3[96:100, :])
    finish()
    g.wait_ge(T.sem.sent, sent[0])
